import numpy as np, ml_dtypes
CORES = [35,38,43,46]
N = 4
BF = ml_dtypes.bfloat16
V, G, RO, RW, TU, TD = 3072, 256, 6, 2, 4, 3
W = V + (N - 1) * G
def parts(rng):
    S = rng.integers(0, W, (N, 8, 16, V)); T = rng.integers(0, W, (N, 8, 16, V))
    cs = rng.integers(0, 16, (N, 8, V)); ct = rng.integers(0, 16, (N, 8, V))
    return S, T, cs, ct, rng.integers(-256, 257, (N, 8, 16, V)) * 0.00390625
def pack(S, T, cs, ct, s):
    return {"s0": np.ascontiguousarray(s.reshape(N, 128, V)).astype(BF), "pt": (S + 4096 * T).reshape(N, 128, V).astype(np.int32), "cur": (cs + 16 * ct).astype(np.int32)}
def plant(S, T, cs, ct, s):
    def put(v, a, b):
        np.put_along_axis(S[..., v], cs[..., v][..., None], a, 2); np.put_along_axis(T[..., v], ct[..., v][..., None], b, 2)
    s[..., 1] = 0.25; put(1, W - 1, 0); s[..., 3] = 1.0; put(3, 3, 3)
    for k in range(17):
        m = 16 + k; s[:, ::2, :k, m] = -1.0; s[:, 1::2, :k, m] = -2.0 ** -20; s[:, :, k:, m] = 0.5; put(m, 1, m)
        for v in (40 + 2 * k, V - 33 + 2 * k): s[..., v] = -1.0; put(v, 1, m)
        for v in (41 + 2 * k, V - 34 + 2 * k): s[..., v] = 1.0; put(v, 3, m)
    for j in range(8):
        for e in (80 + 3 * j, V - 64 + 3 * j):
            s[..., e] = 0.130859375; s[..., e + 1] = 0.9140625; s[..., e + 2] = 0.1875
            put(e, 1, e + 2); put(e + 1, e, e + 1); put(e + 2, e + 1, e + 2)
    for h in (106, V - 72):
        o, g, b, e, a, v, x = range(h, h + 7)
        for m, t in ((o, 0.0), (g, 0.96484375), (b, 0.388671875), (e, 0.58984375), (a, 0.84765625), (v, 0.000732421875), (x, -1.0)): s[..., m] = t
        put(o, o, o); put(g, o, g); put(b, g, b); put(e, o, e); put(a, e, a); put(v, a, 32); put(x, x, v)
        np.put_along_axis(S[..., v], ((cs[..., v] + 1) & 15)[..., None], b, 2)
def setup_inputs(rng):
    return pack(*parts(rng))
def setup_inputs_spread(rng):
    S, T, cs, ct, s = parts(rng)
    s = s * np.exp2(rng.integers(-2, 1, (N, 8, 1, V))) * (rng.random((N, 8, 1, V)) > 0.0625)
    S = np.minimum((W * rng.random(S.shape) ** 2).astype(np.int64), W - 1); T = W - 1 - np.minimum((W * rng.random(T.shape) ** 3).astype(np.int64), W - 1)
    cs = np.minimum((16 * rng.random(cs.shape) ** 3).astype(np.int64), 15); ct = 15 - np.minimum((16 * rng.random(ct.shape) ** 3).astype(np.int64), 15)
    return pack(S, T, cs, ct, s)
def setup_inputs_ends(rng):
    S, T, cs, ct, s = parts(rng)
    u = rng.random(S.shape); lo, hi = 0, W - 1
    S = np.where(u < 0.36, lo, np.where(u < 0.72, hi, np.where(u < 0.79, lo, np.where(u < 0.86, hi, S))))
    T = np.where(u < 0.36, lo, np.where(u < 0.72, hi, np.where(u < 0.79, hi, np.where(u < 0.86, lo, T))))
    u = rng.random(cs.shape)
    cs = np.where(u < 0.36, 0, np.where(u < 0.72, 15, np.where(u < 0.79, 0, np.where(u < 0.86, 15, cs))))
    ct = np.where(u < 0.36, 0, np.where(u < 0.72, 15, np.where(u < 0.79, 15, np.where(u < 0.86, 0, ct))))
    sg = np.where(rng.random((N, 8, 1, V)) < 0.5, rng.integers(0, 2, (N, 8, 1, V)), rng.integers(0, 2, s.shape)) * 2.0 - 1.0
    m = rng.random((N, 8, 1, V)) < 0.7; m[..., 0] = False; m[..., G - 1] = False
    s = np.where(m, sg, s); plant(S, T, cs, ct, s)
    return pack(S, T, cs, ct, s)
def setup_inputs_corners(rng):
    S, T, cs, ct, s = parts(rng); v = np.arange(V); z = 0 * v
    tbl = np.stack([v, (v - 1) % V, (v + 1) % V, V - 1 - v, z, z + V - 1, z + V, z + W - 1, z + G - 1, V + v % G, W - 1 - v % G, v % G])
    S = np.where(rng.random(S.shape) < 0.25, S, tbl[rng.integers(0, len(tbl), (N, 8, 16))])
    T = np.where(rng.random(T.shape) < 0.25, T, tbl[rng.integers(0, len(tbl), (N, 8, 16))])
    e = np.array([0, 1, 14, 15]); cs = rng.choice(e, cs.shape); ct = rng.choice(e, ct.shape)
    s = np.where(rng.random(s.shape) < 0.7, rng.choice(np.array([0.0, 0.25, -0.25, 0.5, -0.5, 1.0, -1.0]), s.shape), s)
    plant(S, T, cs, ct, s)
    return pack(S, T, cs, ct, s)
def setup_inputs_crowd(rng):
    S, T, cs, ct, s = parts(rng); pl = np.array([0, G - 1, G, V - 1, V, W - 1]); g = np.arange(8).reshape(1, 8, 1, 1); v = np.arange(V); home = (g == 4) | (g == 7)
    for X in (S, T):
        same = np.where(home, rng.choice(pl[:4], (N, 8, 16, 1)), rng.choice(pl, (N, 8, 16, 1)))
        few = np.where(home, rng.choice(pl[:4], X.shape), rng.choice(pl, X.shape)); but = rng.integers(0, V, (N, 8, 16, 1))
        X[...] = np.where(g % 4 == 3, few, np.where((g % 2 == 1) & (v == but), X, same))
    s[:, 4] = s[:, 4, :1] + 0.0; s[:, 7, :15] = s[:, 7, :1] + 0.0
    return pack(S, T, cs, ct, s)
def setup_inputs_calm(rng):
    S, T, cs, ct, s = parts(rng); r = np.arange(N).reshape(N, 1, 1); g = np.arange(8).reshape(1, 8, 1)
    cs = 0 * cs + (g + r) % 4; ct = 0 * ct + (g // 2 + r) % 4
    share = np.array([0.97, 0.95, 0.9, 0.8]).reshape(1, 4, 1, 1); share = np.concatenate([share, share], axis=1)
    return pack(S, T, cs, ct, np.where(rng.random(s.shape) < share, 0.5, s))
def check_ranges(d):
    bad = []; p = np.asarray(d["pt"]).astype(np.int64); c = np.asarray(d["cur"]).astype(np.int64); a = np.abs(np.asarray(d["s0"]).astype(np.float64))
    if np.min(p) < 0 or np.max(p) > 4097 * (W - 1) or np.max(p & 4095) > W - 1 or np.max(p >> 12) > W - 1: bad.append("range of pt")
    if np.min(c) < 0 or np.max(c) > 255: bad.append("range of cur")
    if not np.all((a == 0) | ((a >= 2.0 ** -20) & (a <= 1))): bad.append("size of s0")
    return bad
def pick(t, ix):
    out = []
    for r in range(N):
        w = [t[r]] + [t[(r - d) % N][(np.arange(8) + d * (d + 1) // 2) % 8][..., :G] for d in range(1, N)]
        out.append(np.take_along_axis(np.concatenate(w, axis=2), ix[r][:, None, :], 2))
    return np.stack(out)
def reference(s0, pt, cur):
    s = s0.astype(np.float32).reshape(N, 8, 16, V); y = s.astype(np.float64); c = np.zeros(s.shape, np.int64)
    p = pt.astype(np.int64).reshape(N, 8, 16, V); S = p & 4095; T = p >> 12
    cs = cur.astype(np.int64) & 15; ct = cur.astype(np.int64) >> 4; row = np.arange(16).reshape(1, 1, 16, 1)
    for step in range(RO):
        a = np.take_along_axis(S, cs[:, :, None], 2)[:, :, 0]; b = np.take_along_axis(T, ct[:, :, None], 2)[:, :, 0]
        sa, ya, cb = pick(s, a), pick(y, a), pick(c, b)
        new = np.float32(1) - np.float32(2) * np.abs(sa * s)
        z = np.add.reduce(np.where(s >= 0, cb, -cb), axis=2)
        hold = z <= -TD
        y = np.where(hold[:, :, None], y, np.tanh((1.0 + ya) * new))
        if step < RO - 1:
            via = np.take_along_axis(a, np.minimum(a, V - 1), 2)
            m = (a < V) & (z >= RW) & (z < TU)
            S = np.where(m[:, :, None] & (row == cs[:, :, None]), via[:, :, None], S)
        c = ((s < 0) & (new >= 0)).astype(np.int64) - ((s >= 0) & (new < 0)).astype(np.int64)
        cs = (cs + (z >= TU)) & 15; ct = (ct + hold) & 15; s = new
    return {"y": y.reshape(N, 128, V).astype(np.float32), "q": (cs + 16 * ct).astype(np.float32)}

def check_inputs(d):
    bad = list(check_ranges(d))
    if not bad:
        for name, y in reference(**d).items():
            for q in range(N):
                v = np.abs(np.asarray(y[q], np.float64)); s = np.sqrt(np.mean(v * v))
                if v.max() > 4 * s or s < 2.0 ** -2: bad.append('%s of rank %d is uneven or too small' % (name, q))
    return bad

@@ -1,0 +1,707 @@
+from concourse.bass import DstId, RemoteDMATransfer
+from concourse.mybir import AluOpType, ActivationFunctionType
+
+ALU = AluOpType
+AF = ActivationFunctionType
+N, V, NB, W, RO = 4, 3072, 256, 3840, 6
+KW, KD = V // 16, W // 16
+SHIFT = [d * (d + 1) // 2 for d in range(N)]
+ROWS = 128 + 16 * SHIFT[N - 1]
+USE3D = False
+MAGIC = 201326592.0
+LA, LB = 6, 5
+PESP = [2, 3, 4, 5, 6]
+DIRECT = 3072
+ZOFF = []
+
+SCRATCH = {
+    "Y": ("sbuf", [128, 5 * W + V], "float32"),
+    "SW": ("sbuf", [128, W], "float32"), "SO": ("sbuf", [128, V], "float32"), "SL": ("sbuf", [128, W - V], "float32"),
+    "SD": ("sbuf", [128, W], "bfloat16"),
+    "P0": ("sbuf", [128, V], "float32"), "P1": ("sbuf", [128, V], "float32"),
+    "U": ("sbuf", [128, 2048], "float32"),
+    "K0": ("sbuf", [128, W], "bfloat16"), "K1": ("sbuf", [128, W], "bfloat16"), "K2": ("sbuf", [128, W], "bfloat16"),
+    "TT": ("sbuf", [128, 2048], "bfloat16"), "WG": ("sbuf", [128, V], "bfloat16"),
+    "PT": ("sbuf", [128, V], "int32"),
+    "A1": ("sbuf", [128, KW, LA] if USE3D else [128, KW * LA], "float32"),
+    "A0": ("sbuf", [128, KW, LA] if USE3D else [128, KW * LA], "bfloat16"),
+    "B1": ("sbuf", [128, KW, LB] if USE3D else [128, KW * LB], "float32"),
+    "B0": ("sbuf", [128, KW, LB] if USE3D else [128, KW * LB], "bfloat16"),
+    "LST": ("sbuf", [128, 9 * KW + 16], "uint16"),
+    "IT": ("sbuf", [128, 6 * KW], "int32"),
+    "CI": ("sbuf", [128, 2 * KW], "int32"),
+    "FT": ("sbuf", [128, KW], "float32"),
+    "HI": ("sbuf", [128, KD], "bfloat16"), "LO": ("sbuf", [128, KD], "bfloat16"), "VER": ("sbuf", [128, KD], "bfloat16"),
+    "NH": ("sbuf", [128, KW], "bfloat16"),
+    "HS": ("sbuf", [128, 6 * KW], "bfloat16"), "HT": ("sbuf", [128, 6 * KW], "bfloat16"),
+    "CT": ("sbuf", [128, 8, 32], "int32"), "CB": ("sbuf", [128, 256], "bfloat16"), "QT": ("sbuf", [128, 8, 32], "float32"),
+    "YBUS": ("sbuf", [128, NB], "float32"),
+    "RI": ("sbuf", [128, 64], "int32"), "MW": ("sbuf", [128, 16], "float32"), "COL": ("sbuf", [128, 8], "float32"),
+    "GS": ("sbuf", [128, 24], "float32"),
+    "ZB": ("sbuf", [128, 144], "bfloat16"), "ZV": ("sbuf", [128, 144], "bfloat16"), "ZY": ("sbuf", [128, 144], "bfloat16"),
+    "IF": ("sbuf", [128, 128], "float32"), "IB": ("sbuf", [128, 640], "bfloat16"), "ONE": ("sbuf", [128, 704], "bfloat16"),
+    "VC": ("sbuf", [128, KD], "float32"),
+    "PS": ("psum", [128, 2048], "float32"),
+    "PZ": ("psum", [128, 512], "float32"), "PW": ("psum", [128, 512], "float32"),
+    "PN": ("psum", [128, 512], "float32"), "PX": ("psum", [128, 512], "float32"),
+    "DF": ("dram", [10 * ROWS, NB], "float32"), "DH": ("dram", [6 * ROWS, NB], "bfloat16"),
+}
+NDMA = 80
+SEMAPHORES = ["cV", "cA", "cP", "cG", "sent"] + ["d%d" % i for i in range(NDMA)] + ["r%d" % i for i in range(16)]
+
+CY, GA, GT, FIX, PEC, LAT = 1.0e-3, 1.56, 1.8, 0.07, 0.55e-3, 0.12
+TUNE = {"win": 0.05, "flex": {}, "bias": {
+    'bc0': -8, 'Se3': -2, 'Td2': 8, 'af1': -4, 'lo4': -8, 'z2': 16, 'abs0': -2, 'dll3': -4, 'kZB': 8, 'abs1': 2, 'sg1': -2, 'xy4': 16, 'nh6': 2,
+    'cw1': 2, 'sa4': 16, 'gw2': 2, 'b1p': 8, 'Se1': 16, 'qi': -2, 'th5': -2, 'ca2': 4, 'Te4': 8, 'pr2': -8, 'Se4': 16, 'k15': -4, 'Txd': -2,
+    'dl5': -4, 'k0p': -16, 'kZV': 16, 'cw0': -6, 'Sc1': 4, 'k6': -8, 'b0i': -4, 'k28': 2, 'gy6': -8, 'ns3': 16, 'gy4': -16, 'bl3': -8, 'sp5': 16,
+    'ybl3': -4, 'adv5': -4, 'sty2': -8, 'k10': 2, 'sp6': -8, 'sv3': -16, 'Tx24': -4}}
+
+
+def engine_split(src, peers, topo):
+    use = {p: topo.engines(src, p) for p in peers}
+    least = min(len(e) for e in use.values())
+    tight = [p for p in peers if len(use[p]) == least]
+    loose = [p for p in peers if len(use[p]) != least]
+    out = {}
+    taken = []
+    for grp in (tight, loose):
+        if not grp:
+            continue
+        free = [e for e in use[grp[0]] if e not in taken]
+        n = 1
+        while 2 * n * len(grp) <= len(free):
+            n *= 2
+        for j, p in enumerate(grp):
+            out[p] = free[j * n:(j + 1) * n]
+            taken = taken + out[p]
+    return out
+
+
+def make_ops(g, core, T, topo):
+    rank = T.rank_of(core)
+    cores = list(T.cores)
+    ops = []
+    acc = {}
+    banks = {}
+    cnt = {"d": 0, "r": 0}
+
+    def add(name, alts, r=(), w=(), bank=(), extra=(), kind="c", lat=0.0, sem=None, inc=1):
+        i = len(ops)
+        hard = set(extra)
+        for (k, a, b) in r:
+            for e in acc.get(k, []):
+                if e[3] and e[0] < b and a < e[1]:
+                    hard.add(e[2])
+        for (k, a, b) in w:
+            if kind != "arr":
+                for e in acc.get(k, []):
+                    if e[0] < b and a < e[1]:
+                        hard.add(e[2])
+            acc[k] = [e for e in acc.get(k, []) if not (a <= e[0] and e[1] <= b)] + [[a, b, i, True]]
+        for (k, a, b) in r:
+            acc.setdefault(k, []).append([a, b, i, False])
+        soft = set()
+        for b in bank:
+            soft.update(banks.get(b, []))
+            banks.setdefault(b, []).append(i)
+        hard.discard(i)
+        ops.append({"name": name, "alts": alts, "hard": hard, "soft": soft - hard, "kind": kind, "lat": lat, "sem": sem, "inc": inc})
+        return i
+
+    def vop(name, n, f, r, w, bank=(), mul=1.0, extra=()):
+        return add(name, {"V": (FIX + max(64, n * mul) * CY, f)}, r, w, bank, extra)
+
+    def aop(name, n, f, r, w, bank=(), mul=1.0):
+        return add(name, {"A": (FIX + 0.02 + max(64, n * mul) * CY, f)}, r, w, bank)
+
+    def flex(name, n, fv, fa, r, w, bank=(), mul=1.0, who="VA"):
+        who = TUNE["flex"].get(name, who)
+        alts = {}
+        if "A" in who:
+            alts["A"] = (FIX + 0.02 + max(64, n * mul) * CY, fa)
+        if "V" in who:
+            alts["V"] = (FIX + max(64, n * mul) * CY, fv)
+        return add(name, alts, r, w, bank)
+
+    def pop(name, mms, r, w, bank, f32=False):
+        def f(q):
+            last = None
+            for j, (o, l, x) in enumerate(mms):
+                last = q.matmul(o, l, x, j == 0, j == len(mms) - 1)
+            return [last]
+        cost = sum(max(64, x.shape[-1]) for (o, l, x) in mms) * PEC * (4 if f32 is True else f32 or 1) + 0.1
+        return add(name, {"P": (cost, f)}, r, w, bank)
+
+    def gop(name, n, f, r, w):
+        return add(name, {"G": (0.15 + 2 * n * CY, f)}, r, w)
+
+    def dma(name, eng, pairs, r, w, lat, extra=(), **kw):
+        s = "d%d" % cnt["d"]
+        cnt["d"] += 1
+        f = lambda q: [q.dma_start(o, x, **kw) for (o, x) in pairs]
+        iss = (1.0 if eng == "G" else 0.15) * len(pairs)
+        return add(name, {eng: (iss, f)}, r, w, (), extra, "dma", lat, s, 16 * len(pairs))
+
+    peers = [cores[(rank + d) % N] for d in range(1, N)]
+    mine = engine_split(core, peers, topo)
+    arrive = sum(len(engine_split(c, [x for x in cores if x != c], topo)[core]) for c in cores if c != core)
+    sent = [0]
+
+    def send(name, dr, blk, dst, c0, key, extra=()):
+        s = "r%d" % cnt["r"]
+        cnt["r"] += 1
+
+        def f(q):
+            trs = []
+            for d in range(1, N):
+                p = cores[(rank + d) % N]
+                rid, pid, se = topo.addr(p)
+                r0 = blk * ROWS + 16 * SHIFT[d]
+                trs.append(RemoteDMATransfer(dst_ids=[DstId(rid=rid, pnc=pid)], dma_engine_mask=sum(1 << e for e in mine[p]),
+                                             remote_sem=T.sem[s], src=T[dr][r0:r0 + 128, :],
+                                             dst=T[dst][:, c0 + (d - 1) * NB:c0 + d * NB]))
+            q.remote_dma_fused(trs, local_sem=T.sem.sent)
+            return []
+        sent[0] += sum(len(e) for e in mine.values())
+        i = add(name, {"G": (1.0, f)}, [(dr, blk, blk + 1)], (), (), extra, "rem")
+        return add(name + "a", {}, (), [(key, c0, c0 + (N - 1) * NB)], (), [i], "arr", 3.5, s, arrive)
+
+    def stage(name, dr, blk, src, r, eng="S", extra=()):
+        r0 = blk * ROWS
+        return dma(name, eng, [(T[dr][r0:r0 + 128, :], src[:, 0:NB]), (T[dr][r0 + 128:r0 + ROWS, :], src[0:ROWS - 128, 0:NB])],
+                   r, [(dr, blk, blk + 1)], 2.2, extra)
+
+    def ts(o, x, s1, s2, o0, o1=None):
+        if o1 is None:
+            return lambda q: [q.tensor_scalar(o, x, s1, None, o0)]
+        return lambda q: [q.tensor_scalar(o, x, s1, s2, o0, o1)]
+
+    def tt(o, x, y, o0):
+        return lambda q: [q.tensor_tensor(o, x, y, o0)]
+
+    def cp(o, x):
+        return lambda q: [q.tensor_copy(o, x)]
+
+    def act(o, x, fn, bias=0.0, scale=1.0):
+        return lambda q: [q.activation(o, x, fn, bias=bias, scale=scale)]
+
+    def ms(o, c):
+        return lambda q: [q.memset(o, c)]
+
+    def slot(nm, j, L):
+        return T[nm][:, :, j] if USE3D else T[nm][:, j::L]
+
+    def lst(j, a=0, b=KW):
+        return T.LST[:, j * KW + a:j * KW + b]
+
+    def lr(j, a=0, b=KW):
+        return ("LST", j * KW + a, j * KW + b)
+
+    def it(j):
+        return T.IT[:, j * KW:(j + 1) * KW]
+
+    def ir(j):
+        return ("IT", j * KW, (j + 1) * KW)
+
+    def ft(j):
+        return T.FT[:, :] if j == 3 else T.Y[:, 5 * W + (11 + j) * KW:5 * W + (12 + j) * KW]
+
+    def fr(j):
+        return ("FT", 0, KW) if j == 3 else ("Y", 5 * W + (11 + j) * KW, 5 * W + (12 + j) * KW)
+
+    def wrap(name, z, zk, src, sk, c0, c1, out, ok, o0, bank, f32, more=(), morer=()):
+        k0, k1 = (c0 % W) // 16, ((c1 - 1) % W) // 16 + 1
+        o = T[out][:, o0 + k0:o0 + k1]
+        mms = [(o, T[z][:, 15 - i:143 - i], T[src][:, c0 + i:c1:16]) for i in range(16)]
+        mms += [(o, l, T[x][:, k0:k1]) for (l, x) in more]
+        return pop(name, mms, [(zk, 0, 1), (sk, c0, c1)] + list(morer), [(ok, o0 + k0, o0 + k1)], [bank], f32)
+
+    L_CS, L_CT, L_A0, L_B0, L_D, L_F, L_YB = 0, 1, 2, 3, 1, 0, 9
+    L_A = {1: 2, 2: 2, 3: 5, 4: 6, 5: 5, 6: 6}
+    L_B = {2: 3, 3: 4, 4: 3, 5: 4, 6: 3}
+    L_Y = {1: 2, 2: 2, 3: 7, 4: 8, 5: 7, 6: 8}
+    PB = ["P0", "P1"]
+    KB = ["K0", "K1", "K2"]
+    C3 = [(0, 1024), (1024, 2048), (2048, 3072)]
+    C2 = [(0, 1536), (1536, 3072)]
+    CG = [(0, 256), (256, 1664), (1664, 3072)]
+    IDN, I240, I16, WT, IH = (T.IB[:, 128 * j:128 * j + 128] for j in range(5))
+
+    for h, eng in ((0, "S"), (1, "A")):
+        dma("cur%d" % h, eng, [(T.CT[0:96, gg, :], T.cur[gg:gg + 1, :]) for gg in range(4 * h, 4 * h + 4)], (), [("CT", h, h + 1)], 2.3)
+    for c, (a, b) in enumerate(C3):
+        dma("pt%d" % c, "S", [(T.PT[:, a:b], T.pt[:, a:b])], (), [("PT", a, b)], 2.9 + 0.9 * c)
+    stage("st0", "DH", 0, T.s0, (), "A")
+    dma("s0", "A", [(T.SD[:, 0:V], T.s0[:, :])], (), [("SD", 0, V)], 5.0)
+    send("x0", "DH", 0, "SD", V, "SD")
+
+    gop("i0", 16, lambda q: [q.iota(T.RI[:, 0:16], [[-1, 16]], 128, 1)], (), [("RI", 0, 16)])
+    gop("i1", 8, lambda q: [q.iota(T.RI[:, 32:40], [[-16, 8]], 0, 1)], (), [("RI", 32, 40)])
+    II = T.IT[:, 5 * KW:5 * KW + 128]
+    gop("i2", 128, lambda q: [q.iota(II, [[1, 128]], 128, -1)], (), [ir(5)])
+    gop("i3", KD, lambda q: [q.iota(T.VC[:, :], [[16, KD]], 0, 0, allow_small_or_imprecise_dtypes=True)], (), [("VC", 0, KD)])
+    vop("k0", 128, ts(IDN, II, 128.0, None, ALU.is_equal), [ir(5)], [("IB", 0, 1)])
+    aop("k0h", 128, act(IH, IDN, AF.Identity, 0.0, 0.5), [("IB", 0, 1)], [("IB", 4, 5)])
+    aop("k0f", 128, act(T.IF[:, :], IDN, AF.Identity), [("IB", 0, 1)], [("IF", 0, 1)])
+    aop("k19", 128, act(I240, IDN, AF.Identity, 0.0, float(KD)), [("IB", 0, 1)], [("IB", 1, 2)])
+    aop("k20", 128, act(I16, IDN, AF.Identity, 0.0, 0.0625), [("IB", 0, 1)], [("IB", 2, 3)])
+    if PESP:
+        vop("k0o", 512, ms(T.ONE[0:1, 0:512], 1.0), (), [("ONE", 0, 1)], mul=0.5)
+        vop("k0p", 128, ms(T.ONE[0:1, 512:640], -0.5), (), [("ONE", 1, 2)], mul=0.5)
+    if ZOFF:
+        vop("k0q", 64, ms(T.ONE[0:1, 640:704], 64.0), (), [("ONE", 2, 3)], mul=0.5)
+    vop("k1", 16, ts(T.RI[:, 16:32], T.RI[:, 0:16], 15, None, ALU.bitwise_and), [("RI", 0, 16)], [("RI", 16, 32)])
+    RR, rr = T.RI[:, 16:32], ("RI", 16, 32)
+    vop("k2", 16, ts(T.MW[:, 0:16], RR, 0.0, None, ALU.is_equal), [rr], [("MW", 0, 16)])
+    vop("k3", 72, ms(T.ZB[:, :], 0.0), (), [("ZB", 0, 1)])
+    vop("k4", 8, ts(T.RI[:, 40:48], T.RI[:, 32:40], 4, None, ALU.arith_shift_right), [("RI", 32, 40)], [("RI", 40, 48)])
+    vop("k5", 8, ts(T.GS[:, 0:8], T.RI[:, 40:48], 0.0, None, ALU.is_equal), [("RI", 40, 48)], [("GS", 0, 8)])
+    R2, r2 = T.IT[:, 4 * KW:4 * KW + 128], ir(4)
+    w0, w1, w2 = (T.P0[:, 128 * j:128 * j + 128] for j in range(3))
+    vop("k6a", 128, ts(R2, II, 15, None, ALU.bitwise_and), [ir(5)], [r2])
+    vop("k6", 128, ts(w0, R2, 1.0, None, ALU.is_ge), [r2], [("P0", 0, 128)])
+    vop("k7", 128, ts(w1, R2, 3.0, 4095.0, ALU.is_ge, ALU.mult), [r2], [("P0", 128, 256)])
+    vop("k8", 128, ts(w2, R2, 5.0, -4096.0, ALU.is_ge, ALU.mult), [r2], [("P0", 256, 384)])
+    vop("k9", 128, tt(w1, w1, w2, ALU.add), [("P0", 128, 384)], [("P0", 128, 256)], mul=2)
+    vop("k10", 128, tt(w0, w0, w1, ALU.add), [("P0", 0, 256)], [("P0", 0, 128)], mul=2)
+    gop("i4", 128, lambda q: [q.affine_select(w1, w0, [[-16, 8], [0, 16]], ALU.is_ge, 0.0, 0, 1)], [("P0", 0, 128)], [("P0", 128, 256)])
+    gop("i5", 128, lambda q: [q.affine_select(WT, w1, [[16, 8], [0, 16]], ALU.is_ge, 0.0, 15, -1)], [("P0", 128, 256)], [("IB", 3, 4)])
+    E = T.RI[:, 16:17]
+    vop("k11", 1, ts(T.RI[:, 48:49], E, 1, None, ALU.bitwise_and), [rr], [("RI", 48, 49)])
+    vop("k12", 1, ts(T.RI[:, 49:50], E, 11, None, ALU.bitwise_and), [rr], [("RI", 49, 50)])
+    vop("k13", 1, cp(T.COL[:, 0:1], T.RI[:, 48:49]), [("RI", 48, 49)], [("COL", 0, 1)])
+    vop("k14", 1, ts(T.COL[:, 1:2], T.RI[:, 48:49], -2.0, 1.0, ALU.mult, ALU.add), [("RI", 48, 49)], [("COL", 1, 2)])
+    vop("k15", 1, ts(T.COL[:, 2:3], T.RI[:, 49:50], 0.0, None, ALU.is_equal), [("RI", 49, 50)], [("COL", 2, 3)])
+    vop("k16", 1, ts(T.COL[:, 3:4], E, 8.0, None, ALU.is_equal), [rr], [("COL", 3, 4)])
+    vop("k17", 1, cp(T.COL[:, 4:5], E), [rr], [("COL", 4, 5)])
+    vop("k18", 1, ts(T.COL[:, 5:6], E, 7.5, None, ALU.subtract), [rr], [("COL", 5, 6)])
+    for j in range(2):
+        aop("kG%d" % j, 8, act(T.GS[:, 8 + 8 * j:16 + 8 * j], T.GS[:, 0:8], AF.Identity, 0.0, T.COL[:, j:j + 1]), [("GS", 0, 8), ("COL", j, j + 1)], [("GS", 8 + 8 * j, 16 + 8 * j)])
+    vop("kZB", 8, cp(T.ZB[:, 15:143:16], T.GS[:, 0:8]), [("GS", 0, 8)], [("ZB", 0, 1)])
+    for nm, j in (("ZV", 2), ("ZY", 3)):
+        aop("k" + nm, 144, act(T[nm][:, :], T.ZB[:, :], AF.Identity, 0.0, T.COL[:, j:j + 1]), [("ZB", 0, 1), ("COL", j, j + 1)], [(nm, 0, 1)])
+    aop("k21", 48, act(T.HI[:, KW:KD], T.VC[:, KW:KD], AF.Identity), [("VC", KW, KD)], [("HI", KW, KD)])
+    aop("k22", 48, act(T.LO[:, KW:KD], T.VC[:, KW:KD], AF.Identity, T.COL[:, 5:6], 0.0), [("VC", KW, KD), ("COL", 5, 6)], [("LO", KW, KD)])
+    aop("k23", KW, act(T.VC[:, 0:KW], T.VC[:, 0:KW], AF.Identity, T.COL[:, 4:5]), [("VC", 0, KW), ("COL", 4, 5)], [("VC", 0, KW)])
+    vop("k27", KW, ms(T.HS[:, 0:KW], 5.0), (), [("HS", 0, 1)], mul=0.5)
+    vop("k28", KW, ms(T.HT[:, 0:KW], 5.0), (), [("HT", 0, 1)], mul=0.5)
+    vop("k24", KW * LA, ms(T.A0[:], 0.0), (), [("A0", 0, LA)], mul=0.5)
+    vop("k25", KW * LB, ms(T.B0[:], 0.0), (), [("B0", 0, LB)], mul=0.5)
+    vop("k26", KW, ms(T.VER[:, 0:KW], 0.0), (), [("VER", 0, KW)], mul=0.5)
+
+    for b in range(2):
+        vop("cb%d" % b, 128, cp(T.CB[0:96, 128 * b:128 * b + 128], T.CT[0:96, :, 16 * b:16 * b + 16]), [("CT", 0, 2)], [("CB", b, b + 1)])
+        pop("cm%d" % b, [(T.PN[:, 96 * b:96 * b + 96], T.CB[0:96, 128 * b:128 * b + 128], T.IB[0:96, 0:96])],
+            [("CB", b, b + 1), ("IB", 0, 1)], [("PN", 96 * b, 96 * b + 96)], ["PN"])
+    for b in range(2):
+        vop("cw%d" % b, 96, cp(T.IT[:, b:KW:2], T.PN[:, 96 * b:96 * b + 96]), [("PN", 96 * b, 96 * b + 96)], [("ITc", b, b + 1)], ["PN"])
+    CS, CT2 = T.CI[:, 0:KW], T.CI[:, KW:2 * KW]
+    vop("cs", KW, ts(CS, it(0), 15, None, ALU.bitwise_and), [("ITc", 0, 2), ir(0)], [("CI", 0, 1)])
+    vop("csl", KW, cp(lst(L_CS), CS), [("CI", 0, 1)], [lr(L_CS)])
+    vop("ct", KW, ts(CT2, it(0), 4, None, ALU.logical_shift_right), [("ITc", 0, 2), ir(0)], [("CI", 1, 2)])
+    vop("ctl", KW, cp(lst(L_CT), CT2), [("CI", 1, 2)], [lr(L_CT)])
+
+    ychunk = [0]
+
+    def weigh(nm, l, lk, hot, a, b, src, sr, y0):
+        u = ychunk[0] % 2
+        ychunk[0] += 1
+        n = b - a
+        for h in range(0, n, 512):
+            pop(nm + "m", [(T.PS[:, 1024 * u + h:1024 * u + h + 512], l, T[hot][:, a + h:a + h + 512])], [lk, (hot, a + h, a + h + 512)],
+                [("PS", 1024 * u + h, 1024 * u + h + 512)], ["PS%d" % (2 * u + h // 512)])
+        vop(nm + "p", n, tt(T.Y[:, y0 + a:y0 + b], T.PS[:, 1024 * u:1024 * u + n], src, ALU.mult), [("PS", 1024 * u, 1024 * u + n), sr],
+            [("Y", y0 + a, y0 + b)], ["PS%d" % (2 * u + h // 512) for h in range(0, n, 512)])
+
+    def elect(nm, li, hot, y0, ps, chunks, tmp):
+        for c, (a, b) in enumerate(chunks):
+            src = T.MW[:, 0:16].indirect(lst(li, a // 16, b // 16))
+            if nm == "a" and b <= DIRECT:
+                vop("a%dp" % c, b - a, tt(T.Y[:, y0 + a:y0 + b], src, T.PT[:, a:b], ALU.mult), [("MW", 0, 16), lr(li), ("PT", a, b)],
+                    [("Y", y0 + a, y0 + b)], mul=GT)
+                flex("al%d" % c, b - a, cp(T[hot][:, a:b], src), act(T[hot][:, a:b], src, AF.Identity), [("MW", 0, 16), lr(li)], [(hot, a, b)], mul=GA, who="A")
+                continue
+            flex("%sh%d" % (nm, c), b - a, cp(T[hot][:, a:b], src), act(T[hot][:, a:b], src, AF.Identity), [("MW", 0, 16), lr(li)], [(hot, a, b)], mul=GA, who="A")
+            weigh("%s%d" % (nm, c), IDN, ("IB", 0, 1), hot, a, b, T.PT[:, a:b], ("PT", a, b), y0)
+        fold(nm, y0, 0, 1, ps, 256, tmp)
+
+    def fold(nm, y0, g0, nc, ps, p0, tmp):
+        w = 128 * nc
+        for b in range(2):
+            c0 = y0 + 1536 * b
+            for h in range(0, 16, 4):
+                mm = [(T[ps][0:96, p0 + w * b + i:p0 + w * b + w:16], T.Y[:, c0 + i:c0 + 1536:16], T.GS[:, g0:g0 + 8 * nc]) for i in range(h, h + 4)]
+                add("%sf%d" % (nm, b), {"P": (4 * 256 * PEC + 0.1, lambda q, mm=mm: [q.matmul(o, l, x, True, True) for (o, l, x) in mm])},
+                    [("GS", 0, 24), ("Y", c0, c0 + 1536)], [(ps + "f", 16 * b + h, 16 * b + h + 4), (ps, p0 + w * b, p0 + w * b + w)] if h == 0 else [(ps + "f", 16 * b + h, 16 * b + h + 4)], [ps])
+            o, x = T.Y[0:96, tmp + w * b:tmp + w * b + w], T[ps][0:96, p0 + w * b:p0 + w * b + w]
+            flex("%sc%d" % (nm, b), w, cp(o, x), act(o, x, AF.Identity), [(ps + "f", 16 * b, 16 * b + 16), (ps, p0 + w * b, p0 + w * b + w)],
+                 [("Y", tmp + w * b, tmp + w * b + w)], [ps], who="A")
+        for b in range(2):
+            for cl in range(nc):
+                t0, o0 = tmp + w * b + 128 * cl, KW * cl + 96 * b
+                pop("%st%d" % (nm, b), [(T[ps][:, o0:o0 + 96], T.Y[0:96, t0:t0 + 128], T.IF[0:96, 0:96])], [("Y", t0, t0 + 128), ("IF", 0, 1)],
+                    [(ps, o0, o0 + 96)], [ps], True)
+    elect("a", L_CS, "K0", 3 * W, "PZ", [(0, 1024), (1024, 1536), (1536, 2048), (2048, 2560), (2560, 3072)], 5 * W)
+    vop("a0i", KW, cp(it(1), T.PZ[:, 0:KW]), [("PZ", 0, KW)], [ir(1)], ["PZ"])
+    vop("a0m", KW, ts(it(2), it(1), 4095, None, ALU.bitwise_and), [ir(1)], [ir(2)])
+    vop("a0l", KW, cp(lst(L_A0), it(2)), [ir(2)], [lr(L_A0)])
+    vop("a0s", KW, ts(slot("A1", 5, LA), it(2), 7.5, None, ALU.subtract), [ir(2)], [("A1", 5, 6)])
+
+    for a, b in C2:
+        aop("abs0", b - a, act(T.SO[:, a:b], T.SD[:, a:b], AF.Abs), [("SD", a, b)], [("SO", a, b)])
+        dma("sw0", "S", [(T.SW[:, a:b], T.SO[:, a:b])], [("SO", a, b)], [("SW", a, b)], 3.4)
+    aop("abs1", W - V, act(T.SW[:, V:W], T.SD[:, V:W], AF.Abs), [("SD", V, W)], [("SW", V, W)])
+    aop("sg0", V, act(T.K1[:, 0:V], T.SD[:, 0:V], AF.Sign, -2.0 ** -30, -1.0), [("SD", 0, V)], [("K1", 0, V)])
+
+    def trigger0():
+        elect("b", L_CT, "WG", 4 * W, "PW", C3, 5 * W + 512)
+        vop("b0i", KW, cp(it(3), T.PW[:, 0:KW]), [("PW", 0, KW)], [ir(3)], ["PW"])
+        vop("b0m", KW, ts(it(0), it(3), 12, None, ALU.logical_shift_right), [ir(3)], [ir(0)])
+        vop("b0l", KW, cp(lst(L_B0), it(0)), [ir(0)], [lr(L_B0)])
+        vop("b0s", KW, cp(slot("B1", 4, LB), it(0)), [ir(0)], [("B1", 4, 5)])
+
+    def tables(which):
+        for nm, hot, y0, cur, ck in ((("S", "K0", 3 * W, CS, 0), ("T", "WG", 4 * W, CT2, 1))[which],):
+            for c, (a, b) in enumerate(C3):
+                src, sr = T.PT[:, a:b], ("PT", a, b)
+                if nm == "S":
+                    vop("Ss%d" % c, 1024, ts(src, src, 4095, None, ALU.bitwise_and), [sr], [sr])
+                else:
+                    vop("Ts%d" % c, 1024, ts(src, src, 12, None, ALU.logical_shift_right), [sr], [sr])
+                weigh("%s%d" % (nm, c), WT, ("IB", 3, 4), hot, a, b, src, sr, y0)
+                if nm == "S":
+                    dma("pr%d" % c, "S", [(src, T.pt[:, a:b])], (), [sr], 2.9)
+            fold(nm, y0, 8, 2, "PX", 0, 5 * W + 512 * ck)
+            P1, P2 = T.PX[:, 0:KW], T.PX[:, KW:2 * KW]
+            p1, p2 = ("PX", 0, KW), ("PX", KW, 2 * KW)
+            vop(nm + "par", KW, ts(it(0), cur, 1, None, ALU.bitwise_and), [("CI", ck, ck + 1)], [ir(0)])
+            vop(nm + "md", KW, tt(ft(0), P2, it(0), ALU.mult), [p2, ir(0)], [fr(0)], ["PX"])
+            vop(nm + "x13", KW, tt(it(1), P1, ft(0), ALU.add), [p1, fr(0)], [ir(1)], ["PX"])
+            vop(nm + "xd", KW, tt(ft(1), P2, ft(0), ALU.subtract), [p2, fr(0)], [fr(1)], ["PX"])
+            vop(nm + "x24", KW, tt(it(2), P1, ft(1), ALU.add), [p1, fr(1)], [ir(2)], ["PX"])
+            vop(nm + "e1", KW, ts(it(3), it(1), 4095, None, ALU.bitwise_and), [ir(1)], [ir(3)])
+            vop(nm + "e2", KW, ts(it(4), it(2), 4095, None, ALU.bitwise_and), [ir(2)], [ir(4)])
+            vop(nm + "e3", KW, ts(it(5), it(1), 12, None, ALU.logical_shift_right), [ir(1)], [ir(5)])
+            vop(nm + "e4", KW, ts(it(0), it(2), 12, None, ALU.logical_shift_right), [ir(2)], [ir(0)])
+            D1, L = ("A1", LA) if nm == "S" else ("B1", LB)
+            if nm == "S":
+                vop("Sd1", KW, ts(ft(2), it(3), 7.5, None, ALU.subtract), [ir(3)], [fr(2)])
+            else:
+                vop("Td1", KW, tt(slot(D1, 3, L), it(3), slot(D1, 4, L), ALU.subtract), [ir(3), (D1, 4, 5)], [(D1, 3, 4)], mul=2)
+            vop(nm + "d2", KW, tt(slot(D1, 2, L), it(4), it(3), ALU.subtract), [ir(3), ir(4)], [(D1, 2, 3)], mul=2)
+            vop(nm + "d3", KW, tt(slot(D1, 1, L), it(5), it(4), ALU.subtract), [ir(5), ir(4)], [(D1, 1, 2)], mul=2)
+            vop(nm + "d4", KW, tt(slot(D1, 0, L), it(0), it(5), ALU.subtract), [ir(0), ir(5)], [(D1, 0, 1)], mul=2)
+
+    carr = {}
+    g1s = {}
+    alpha = [slot("A1", 5, LA), ("A1", 5, 6)]
+    YO = 5 * W
+
+    def lookup(t):
+        al, ar = alpha
+        vop("hi%d" % t, KW, ts(T.HI[:, 0:KW], al, MAGIC, MAGIC, ALU.add, ALU.subtract), [ar], [("HI", 0, KW)])
+        vop("lo%d" % t, KW, tt(T.LO[:, 0:KW], al, T.HI[:, 0:KW], ALU.subtract), [ar, ("HI", 0, KW)], [("LO", 0, KW)], mul=2)
+        al, ar = slot("A1", 5, LA), ("A1", 5, 6)
+        pop("dl%d" % t, [(T.PN[:, 0:KW], I240, T.LO[:, 0:KW]), (T.PN[:, 0:KW], I16, T.HI[:, 0:KW])],
+            [("IB", 1, 3), ("LO", 0, KW), ("HI", 0, KW)], [("PN", 0, KW)], ["PN"])
+        vop("dll%d" % t, KW, ts(lst(L_D), T.PN[:, 0:KW], 7.5 * KD, None, ALU.add), [("PN", 0, KW)], [lr(L_D)], ["PN"])
+        pairs, rd = [], []
+        if t < RO:
+            pairs += [(T.SD[0::16, :], T.HI[:, :]), (T.SD[4::16, :], T.LO[:, :])]
+            rd += [("HI", 0, KD), ("LO", 0, KD)]
+        if t > 2:
+            aop("vc%d" % t, 48, act(T.VER[:, KW:KD], T.HI[:, KW:KD], AF.Identity, float(W * (t - 2)), 0.0), [("HI", KW, KD)], [("VER", KW, KD)])
+            pairs += [(T.SD[8::16, :], T.VER[:, :])]
+            rd += [("VER", 0, KD)]
+        dma("D%d" % t, "S", pairs, rd, [("SD", 0, W)], 2.8)
+        for c, (a, b) in enumerate(C2):
+            src = T.SD[:, :].indirect(lst(L_D, a // 16, b // 16))
+            flex("gw%d" % t, b - a, cp(T.WG[:, a:b], src), act(T.WG[:, a:b], src, AF.Identity),
+                 [("SD", 0, W), lr(L_D)], [("WG", a, b)], mul=GA, who="A")
+            if t < RO:
+                wrap("via%d_%d" % (t, c), "ZV", "ZV", "WG", "WG", a, b, "PW", "PW", 0, "PW", False)
+            if t > 2:
+                wrap("yo%d_%d" % (t, c), "ZY", "ZY", "WG", "WG", a, b, "PW", "PW", KW, "PW", False,
+                     [(IDN, "HI"), (IDN, "LO")], [("IB", 0, 1), ("HI", 0, KW), ("LO", 0, KW)])
+        if t > 2:
+            vop("yl%d" % t, KW, ts(lst(L_Y[t]), T.PW[:, KW:2 * KW], 7.5, None, ALU.add), [("PW", KW, 2 * KW)], [lr(L_Y[t])], ["PW"])
+        if t < RO:
+            vop("sv%d" % t, KW, tt(slot("A1", 3, LA), ft(2), T.PW[:, 0:KW], ALU.subtract), [fr(2), ("PW", 0, KW)], [("A1", 3, 4)], ["PW"])
+            vop("dv%d" % t, KW, tt(slot("A1", 4, LA), T.PW[:, 0:KW], al, ALU.subtract), [ar, ("PW", 0, KW)], [("A1", 4, 5)], ["PW"])
+
+    def product(t):
+        sw, nw, P = "SW", "SO", PB[t % 2]
+        k0, k1 = KB[t % 3], KB[(t + 1) % 3]
+        sgn = 1.0 if t % 2 else -1.0
+        g1 = []
+        for c, (a, b) in enumerate(CG if t < RO else C3):
+            g1.append(vop("g1%d_%d" % (t, c), b - a, tt(T[P][:, a:b], T[sw][:, :].indirect(lst(L_A[t], a // 16, b // 16)), T[nw][:, a:b], ALU.mult),
+                          [(sw, 0, W), (nw, a, b), lr(L_A[t])], [(P, a, b)], mul=GT))
+            if t == RO:
+                continue
+            aop("ab%d_%d" % (t, c), b - a, act(T[nw][:, a:b], T[P][:, a:b], AF.Abs, 1.0, -2.0), [(P, a, b)], [(nw, a, b)])
+            aop("sg%d_%d" % (t, c), b - a, act(T[k1][:, a:b], T[P][:, a:b], AF.Sign, sgn * (0.875 + 2.0 ** -24), -1.75 * sgn), [(P, a, b)], [(k1, a, b)])
+            if c == 0:
+                stage("sts%d" % t, "DF", t - 1, T[nw], [(nw, 0, NB)])
+                send("xs%d" % t, "DF", t - 1, "SL", 0, "SL", [carr[t]] if t in carr else [])
+        if t < RO:
+            m = CG[2][0]
+            dma("sw%d_0" % t, "S", [(T.SW[:, 0:m], T.SO[:, 0:m])], [("SO", 0, m)], [("SW", 0, m)], 3.6)
+            dma("sw%d_1" % t, "S", [(T.SW[:, m:V], T.SO[:, m:V])], [("SO", m, V)], [("SW", m, V)], 3.6)
+            g1 = [dma("sw%d_2" % t, "S", [(T.SW[:, V:W], T.SL[:, :])], [("SL", 0, W - V)], [("SW", V, W)], 2.8)]
+        g1s[t] = g1
+
+    def crossings(t):
+        k0, k1 = KB[t % 3], KB[(t + 1) % 3]
+        dma("cb%d" % t, "G", [(T[k0][:, 0:NB], T[k1][:, 0:NB])], [(k0, 0, NB), (k1, 0, NB)], [(k0, 0, NB)], 2.6, accum_op=ALU.add)
+        stage("stc%d" % t, "DH", t, T[k0], [(k0, 0, NB)])
+        dma("ca%d" % t, "G", [(T[k0][:, NB:V], T[k1][:, NB:V])], [(k0, NB, V), (k1, NB, V)], [(k0, NB, V)], 4.5,
+            accum_op=ALU.add, max_dma_last_dim=V - NB)
+        carr[t + 1] = send("xc%d" % t, "DH", t, k0, V, k0, g1s[t] + ([carr[t]] if t in carr else []))
+
+    def sums(t):
+        cw, k0 = KB[(t - 1) % 3], KB[t % 3]
+        for c, (a, b) in enumerate(C3):
+            u = (a + 1024 * t) % 2048
+            src, o, tr = T[cw][:, :].indirect(lst(L_B[t], a // 16, b // 16)), T.TT[:, u:u + 1024], ("TT", u, u + 1024)
+            more = ()
+            if (t, c) in ZOFF:
+                aop("gd%d_%d" % (t, c), 1024, act(o, src, AF.Identity), [(cw, 0, W), lr(L_B[t])], [tr], mul=GA)
+                w = ychunk[0] % 2
+                ychunk[0] += 1
+                for h in (0, 512):
+                    ps = T.PS[:, 1024 * w + h:1024 * w + h + 512]
+                    pop("ge%d" % t, [(ps, IH, T.TT[:, u + h:u + h + 512]), (ps, IDN, T[k0][:, a + h:a + h + 512])],
+                        [tr, (k0, a, b), ("IB", 0, 5)], [("PS", 1024 * w + h, 1024 * w + h + 512)], ["PS%d" % (2 * w + h // 512)])
+                aop("gf%d_%d" % (t, c), 1024, act(o, T.PS[:, 1024 * w:1024 * w + 1024], AF.Abs, 0.0, 2.0), [("PS", 1024 * w, 1024 * w + 1024)], [tr],
+                    ["PS%d" % (2 * w), "PS%d" % (2 * w + 1)])
+                k0c, o0 = a // 16, T.PZ[:, a // 16:b // 16]
+                pop("z%d_%d" % (t, c), [(o0, T.ZB[:, 15 - i:143 - i], T.TT[:, u + i:u + 1024:16]) for i in range(16)] + [(o0, T.ONE[0:1, 512:640], T.ONE[0:1, 640:704])],
+                    [("ZB", 0, 1), tr, ("ONE", 1, 3)], [("PZ", k0c, k0c + 64)], ["PZ"])
+                continue
+            vop("gc%d_%d" % (t, c), b - a, tt(o, src, T[k0][:, a:b], ALU.mult), [(cw, 0, W), lr(L_B[t]), (k0, a, b)], [tr], mul=GT)
+            wrap("z%d_%d" % (t, c), "ZB", "ZB", "TT", "TT", u, u + 1024, "PZ", "PZ", (a - u) // 16, "PZ", False)
+
+    def turn(t):
+        Z, z = T.PZ[:, 0:KW], ("PZ", 0, KW)
+        j = t - 1
+        hs, ht = T.HS[:, j * KW:(j + 1) * KW], T.HT[:, j * KW:(j + 1) * KW]
+        if t < RO:
+            vop("g4%d" % t, KW, ts(slot("A0", 5, LA), Z, 3.0, None, ALU.is_ge), [z], [("A0", 5, 6)], ["PZ"])
+            vop("adv%d" % t, KW, ts(slot("A0", 4, LA), Z, 7.0, None, ALU.is_ge), [z], [("A0", 4, 5)], ["PZ"])
+        aop("ht%d" % t, KW, act(ht, Z, AF.Sign, -5.0, -1.0), [z], [("HT", j, j + 1)], ["PZ"])
+        aop("hs%d" % t, KW, act(hs, Z, AF.Sign, -7.0, 1.0), [z], [("HS", j, j + 1)], ["PZ"])
+        if t == 2:
+            aop("mt%d" % t, KW, act(slot("B0", 4, LB), ht, AF.Relu), [("HT", j, j + 1)], [("B0", 4, 5)])
+        aop("nh%d" % t, KW, act(T.NH[:, :], ht, AF.Relu, 0.0, -float(W * (t - 1))), [("HT", j, j + 1)], [("NH", 0, 1)])
+        vop("ver%d" % t, KW, tt(T.VER[:, 0:KW], T.VER[:, 0:KW], T.NH[:, :], ALU.max), [("VER", 0, KW), ("NH", 0, 1)], [("VER", 0, KW)], mul=1.5)
+        if t < RO:
+            la = t + 1 if USE3D else LA
+            d0, d1 = (T.A0[:, :, LA - la:LA], T.A1[:, :, LA - la:LA]) if USE3D else (T.A0[:, :], T.A1[:, :])
+            vop("sa%d" % t, KW * la, lambda q: [q.tensor_tensor_scan(T.Y[:, YO:YO + KW * la], d0, d1, 0.0, ALU.mult, ALU.add)],
+                [("A0", LA - la, LA), ("A1", LA - la, LA)], [("Y", YO, YO + KW * la)])
+            na, nr = T.Y[:, YO + la - 1:YO + KW * la:la], ("Y", YO, YO + KW * la)
+            vop("al%d" % t, KW, ts(lst(L_A[t + 1]), na, 7.5, None, ALU.add), [nr], [lr(L_A[t + 1])])
+            aop("as%d" % t, KW, act(slot("A1", 5, LA), na, AF.Identity), [nr], [("A1", 5, 6)])
+            alpha[0], alpha[1] = na, nr
+            if t > 2:
+                pop("nt%d" % t, [(T.PN[:, KW:2 * KW], IDN, T.HT[:, u * KW:(u + 1) * KW]) for u in range(1, t)],
+                    [("IB", 0, 1), ("HT", 1, t)], [("PN", KW, 2 * KW)], ["PN"])
+                for m in range(1, t):
+                    vop("mt%d_%d" % (t, m), KW, ts(slot("B0", LB - m, LB), T.PN[:, KW:2 * KW], float(2 * m - t), None, ALU.is_ge),
+                        [("PN", KW, 2 * KW)], [("B0", LB - m, LB - m + 1)], ["PN"])
+            lb = t if USE3D else LB
+            yb = YO + KW * LA
+            e0, e1 = (T.B0[:, :, LB - lb:LB], T.B1[:, :, LB - lb:LB]) if USE3D else (T.B0[:, :], T.B1[:, :])
+            vop("sb%d" % t, KW * lb, lambda q: [q.tensor_tensor_scan(T.Y[:, yb:yb + KW * lb], e0, e1, 0.0, ALU.mult, ALU.add)],
+                [("B0", LB - lb, LB), ("B1", LB - lb, LB)], [("Y", yb, yb + KW * lb)])
+            vop("bl%d" % t, KW, cp(lst(L_B[t + 1]), T.Y[:, yb + lb - 1:yb + KW * lb:lb]), [("Y", yb, yb + KW * lb)], [lr(L_B[t + 1])])
+
+    def counts(t):
+        if t == 2:
+            aop("ms2", KW, act(slot("A0", 3, LA), T.HS[:, KW:2 * KW], AF.Relu), [("HS", 1, 2)], [("A0", 3, 4)])
+            return
+        pop("ns%d" % t, [(T.PN[:, KW:2 * KW], IDN, T.HS[:, u * KW:(u + 1) * KW]) for u in range(1, t)],
+            [("IB", 0, 1), ("HS", 1, t)], [("PN", KW, 2 * KW)], ["PN"])
+        for m in range(1, t):
+            vop("ms%d_%d" % (t, m), KW, ts(slot("A0", 4 - m, LA), T.PN[:, KW:2 * KW], float(2 * m - t), None, ALU.is_ge),
+                [("PN", KW, 2 * KW)], [("A0", 4 - m, 5 - m)], ["PN"])
+
+    def ystep(t):
+        P = PB[t % 2]
+        wn, we = ("SD", W) if t == 1 else ("Y", W * (t - 1))
+        y0 = W * (t - 1)
+        for c, (a, b) in enumerate(C3):
+            u = ychunk[0] % 2
+            ychunk[0] += 1
+            Uc, ur = T.U[:, 1024 * u:1024 * u + 1024], ("U", u, u + 1)
+            Sc, sr, bk = T.PS[:, 1024 * u:1024 * u + 1024], ("PS", 1024 * u, 1024 * u + 1024), ["PS%d" % (2 * u), "PS%d" % (2 * u + 1)]
+            src = T[wn][:, 0:we].indirect(lst(L_Y[t], a // 16, b // 16))
+            flex("gy%d" % t, 1024, ts(Uc, src, 1.0, None, ALU.add), act(Uc, src, AF.Identity, 1.0), [(wn, 0, we), lr(L_Y[t])], [ur], mul=GA, who="A")
+            if t in PESP:
+                for h in (0, 512):
+                    o = T.PS[:, 1024 * u + h:1024 * u + h + 512]
+                    pop("sp%d" % t, [(o, T.ONE[0:1, 512:640], T.ONE[0:1, 0:512]), (o, T.IF[:, :], T[P][:, a + h:a + h + 512])],
+                        [(P, a + h, a + h + 512), ("ONE", 0, 2), ("IF", 0, 1)], [("PS", 1024 * u + h, 1024 * u + h + 512)], [bk[h // 512]], 2.5)
+            else:
+                aop("sp%d" % t, 1024, act(Sc, T[P][:, a:b], AF.Identity, 1.0, -2.0), [(P, a, b)], [sr], bk)
+            vop("x%d_%d" % (t, c), 1024, tt(Uc, Uc, Sc, ALU.mult), [ur, sr], [ur], bk)
+            aop("th%d_%d" % (t, c), 1024, act(T.Y[:, y0 + a:y0 + b], Uc, AF.Tanh, 0.0, -2.0 if t in PESP else 1.0), [ur], [("Y", y0 + a, y0 + b)])
+            if c == 0 and t < RO:
+                if t == 1:
+                    stage("sty1", "DF", 5, T.Y, [("Y", 0, NB)])
+                else:
+                    vop("yb%d" % t, 16, tt(T.FT[:, 0:16], T.VER[:, 0:16], T.VC[:, 0:16], ALU.add), [("VER", 0, KW), ("VC", 0, KW)], [("FT", 0, 16)])
+                    vop("ybl%d" % t, 16, cp(lst(L_YB, 0, 16), T.FT[:, 0:16]), [("FT", 0, 16)], [lr(L_YB, 0, 16)])
+                    s2 = T.Y[:, 0:y0 + NB].indirect(lst(L_YB, 0, 16))
+                    flex("yg%d" % t, NB, cp(T.YBUS[:, :], s2), act(T.YBUS[:, :], s2, AF.Identity), [("Y", 0, y0 + NB), lr(L_YB, 0, 16)],
+                         [("YBUS", 0, 1)], mul=GA, who="A")
+                    stage("sty%d" % t, "DF", 4 + t, T.YBUS, [("YBUS", 0, 1)])
+                send("xy%d" % t, "DF", 4 + t, "Y", y0 + V, "Y")
+            if t == RO:
+                s3 = T.Y[:, 0:y0 + b].indirect(lst(L_F, a // 16, b // 16))
+                O = PB[(t + 1) % 2]
+                flex("fg%d" % c, 1024, cp(T[O][:, a:b], s3), act(T[O][:, a:b], s3, AF.Identity), [("Y", 0, y0 + b), lr(L_F)], [(O, a, b)], mul=GA)
+                dma("yo%d" % c, "S", [(T.y[:, a:b], T[O][:, a:b])], [(O, a, b)], (), 2.9)
+
+    def finish():
+        vop("fl0", KW, tt(ft(3), T.VER[:, 0:KW], T.VC[:, 0:KW], ALU.add), [("VER", 0, KW), ("VC", 0, KW)], [fr(3)], mul=2)
+        vop("fl1", KW, cp(lst(L_F), ft(3)), [fr(3)], [lr(L_F)])
+        for h, nm in enumerate(("HS", "HT")):
+            pop("q%d" % h, [(T.PX[:, h * KW:(h + 1) * KW], IH, T[nm][:, u * KW:(u + 1) * KW]) for u in range(6)],
+                [("IB", 4, 5), (nm, 0, 6)], [("PX", h * KW, (h + 1) * KW)], ["PX"])
+        vop("qi", 2 * KW, tt(T.IT[:, 0:2 * KW], T.PX[:, 0:2 * KW], T.CI[:, :], ALU.add), [("PX", 0, 2 * KW), ("CI", 0, 2)], [("IT", 0, 2 * KW)], ["PX"])
+        vop("qm", 2 * KW, ts(T.IT[:, 2 * KW:4 * KW], T.IT[:, 0:2 * KW], 15, None, ALU.bitwise_and), [("IT", 0, 2 * KW)], [("IT", 2 * KW, 4 * KW)])
+        vop("q16", KW, ts(ft(3), it(3), 16.0, None, ALU.mult), [ir(3)], [fr(3)])
+        for b in range(2):
+            vop("qa%d" % b, 96, tt(T.CB[:, 128 * b:128 * b + 96], T.IT[:, 2 * KW + b:3 * KW:2], T.FT[:, b:KW:2], ALU.add), [ir(2), fr(3)], [("CB", b, b + 1)], mul=2)
+            pop("qt%d" % b, [(T.PX[0:96, 128 * b:128 * b + 128], T.CB[:, 128 * b:128 * b + 96], IDN)],
+                [("CB", b, b + 1), ("IB", 0, 1)], [("PX", 128 * b, 128 * b + 128)], ["PX"])
+        for b in range(2):
+            vop("qc%d" % b, 128, cp(T.QT[0:96, :, 16 * b:16 * b + 16], T.PX[0:96, 128 * b:128 * b + 128]),
+                [("PX", 128 * b, 128 * b + 128)], [("QT", b, b + 1)], ["PX"])
+        dma("qo", "S", [(T.q[gg:gg + 1, :], T.QT[0:96, gg, :]) for gg in range(8)], [("QT", 0, 2)], (), 2.3)
+
+    product(1)
+    crossings(1)
+    trigger0()
+    tables(0)
+    tables(1)
+    ystep(1)
+    for t in range(2, RO + 1):
+        lookup(t)
+        product(t)
+        sums(t)
+        if t < RO:
+            crossings(t)
+        turn(t)
+        if t == RO:
+            finish()
+        ystep(t)
+        if t < RO - 1:
+            counts(t)
+    return ops, sent[0]
+
+
+def schedule(ops):
+    n = len(ops)
+    succ = [[] for _ in range(n)]
+    left = [0] * n
+    for i, o in enumerate(ops):
+        for d in o["hard"] | o["soft"]:
+            succ[d].append(i)
+            left[i] += 1
+    pri = [0.0] * n
+    for i in range(n - 1, -1, -1):
+        o = ops[i]
+        c = min([a[0] for a in o["alts"].values()] or [0.0]) + o["lat"]
+        pri[i] = c + max([pri[s] + LAT for s in succ[i]] or [0.0])
+    for i, o in enumerate(ops):
+        pri[i] += TUNE["bias"].get(o["name"].split("_")[0], 0.0)
+    free = {e: 0.0 for e in "VAPGS"}
+    fin = [0.0] * n
+    eng = [None] * n
+    ready = [i for i in range(n) if left[i] == 0]
+    order = []
+    while ready:
+        cand = []
+        for i in ready:
+            o = ops[i]
+            t0 = max([fin[d] + LAT for d in o["hard"]] or [0.0])
+            if not o["alts"]:
+                cand = [(-1.0, i, None, t0)]
+                break
+            best = None
+            for e, (c, f) in o["alts"].items():
+                t1 = max([t0, free[e]] + [fin[d] + LAT for d in o["soft"] if eng[d] != e])
+                if best is None or t1 + c < best[0] + best[3]:
+                    best = (t1, i, e, c)
+            cand.append(best)
+        first = min(cand)
+        if first[2] is None:
+            i = first[1]
+            fin[i] = first[3] + ops[i]["lat"]
+        else:
+            near = [c for c in cand if c[2] == first[2] and c[0] <= first[0] + TUNE["win"]]
+            t1, i, e, c = max(near, key=lambda x: (pri[x[1]], -x[1]))
+            eng[i] = e
+            free[e] = t1 + c
+            fin[i] = t1 + c + ops[i]["lat"]
+            ops[i]["t"] = t1
+        order.append(i)
+        ready.remove(i)
+        for s in succ[i]:
+            left[s] -= 1
+            if left[s] == 0:
+                ready.append(s)
+    return order, eng, fin
+
+
+def rank_program(g, core, T, topo):
+    if T.rank_of(core) is None:
+        return
+    ops, sent = make_ops(g, core, T, topo)
+    order, eng, fin = schedule(ops)
+    Q = {"V": g.vector, "A": g.scalar, "P": g.tensor, "G": g, "S": g.sync}
+    known = {e: {} for e in Q}
+    count = {e: 0 for e in Q}
+    tok = {}
+    clock = {}
+    total = {}
+    for i in order:
+        o = ops[i]
+        if o["kind"] == "arr":
+            tok[i] = (o["sem"], o["inc"])
+            clock[i] = {o["sem"]: o["inc"]}
+            total[o["sem"]] = o["inc"]
+            continue
+        e = eng[i]
+        kn = known[e]
+        deps = [d for d in o["hard"] if ops[d]["kind"] != "rem"] + [d for d in o["soft"] if eng[d] != e]
+        deps.sort(key=lambda d: -fin[d])
+        for d in deps:
+            s, v = tok[d]
+            if kn.get(s, 0) >= v:
+                continue
+            Q[e].wait_ge(T.sem[s], v)
+            for s2, v2 in clock[d].items():
+                if kn.get(s2, 0) < v2:
+                    kn[s2] = v2
+        ins = o["alts"][e][1](Q[e])
+        if o["kind"] == "rem":
+            continue
+        if o["kind"] == "dma":
+            for x in ins:
+                x.then_inc(T.sem[o["sem"]], 16)
+            tok[i] = (o["sem"], o["inc"])
+        else:
+            count[e] += 1
+            ins[-1].then_inc(T.sem["c" + e], 1)
+            tok[i] = ("c" + e, count[e])
+        total[tok[i][0]] = tok[i][1]
+        clock[i] = dict(kn)
+        clock[i][tok[i][0]] = tok[i][1]
+    total["sent"] = sent
+    for s, v in total.items():
+        if known["G"].get(s, 0) < v:
+            g.wait_ge(T.sem[s], v)

@@ -7,54 +7,52 @@ N, V, NB, W, RO = 4, 3072, 256, 3840, 6
 KW, KD = V // 16, W // 16
 SHIFT = [d * (d + 1) // 2 for d in range(N)]
 ROWS = 128 + 16 * SHIFT[N - 1]
-USE3D = False
 MAGIC = 201326592.0
 LA, LB = 6, 5
-PESP = [2, 3, 4, 5, 6]
-DIRECT = 3072
-ZOFF = []
+OFF = [None] + [W * j for j in range(5)] + [4 * W + V]
+STEEP = 200.0
 
+TH = V // 3
 SCRATCH = {
-    "Y": ("sbuf", [128, 5 * W + V], "float32"),
-    "SW": ("sbuf", [128, W], "float32"), "SO": ("sbuf", [128, V], "float32"), "SL": ("sbuf", [128, W - V], "float32"),
+    "Y": ("sbuf", [128, 4 * W + 2 * V], "float32"),
+    "HB": ("sbuf", [128, V], "bfloat16"),
+    "SA": ("sbuf", [128, W], "float32"), "SB": ("sbuf", [128, W], "float32"),
     "SD": ("sbuf", [128, W], "bfloat16"),
-    "P0": ("sbuf", [128, V], "float32"), "P1": ("sbuf", [128, V], "float32"),
     "U": ("sbuf", [128, 2048], "float32"),
     "K0": ("sbuf", [128, W], "bfloat16"), "K1": ("sbuf", [128, W], "bfloat16"), "K2": ("sbuf", [128, W], "bfloat16"),
     "TT": ("sbuf", [128, 2048], "bfloat16"), "WG": ("sbuf", [128, V], "bfloat16"),
-    "PT": ("sbuf", [128, V], "int32"),
-    "A1": ("sbuf", [128, KW, LA] if USE3D else [128, KW * LA], "float32"),
-    "A0": ("sbuf", [128, KW, LA] if USE3D else [128, KW * LA], "bfloat16"),
-    "B1": ("sbuf", [128, KW, LB] if USE3D else [128, KW * LB], "float32"),
-    "B0": ("sbuf", [128, KW, LB] if USE3D else [128, KW * LB], "bfloat16"),
+    "PT": ("sbuf", [128, V], "int32"), "SO": ("sbuf", [128, V], "float32"),
+    "A1": ("sbuf", [128, KW * LA], "float32"), "A0": ("sbuf", [128, 4 * KW * LA], "bfloat16"),
+    "B1": ("sbuf", [128, KW * LB], "float32"), "B0": ("sbuf", [128, KW * LB], "bfloat16"),
     "LST": ("sbuf", [128, 9 * KW + 16], "uint16"),
     "IT": ("sbuf", [128, 6 * KW], "int32"),
     "CI": ("sbuf", [128, 2 * KW], "int32"),
     "FT": ("sbuf", [128, KW], "float32"),
-    "HI": ("sbuf", [128, KD], "bfloat16"), "LO": ("sbuf", [128, KD], "bfloat16"), "VER": ("sbuf", [128, KD], "bfloat16"),
-    "NH": ("sbuf", [128, KW], "bfloat16"),
-    "HS": ("sbuf", [128, 6 * KW], "bfloat16"), "HT": ("sbuf", [128, 6 * KW], "bfloat16"),
+    "HI": ("sbuf", [128, KD], "bfloat16"), "LO": ("sbuf", [128, KD], "bfloat16"), "AGE": ("sbuf", [128, KD], "bfloat16"),
+    "HS": ("sbuf", [128, KW], "bfloat16"), "HT": ("sbuf", [128, 6 * KW], "bfloat16"),
     "CT": ("sbuf", [128, 8, 32], "int32"), "CB": ("sbuf", [128, 256], "bfloat16"), "QT": ("sbuf", [128, 8, 32], "float32"),
     "YBUS": ("sbuf", [128, NB], "float32"),
     "RI": ("sbuf", [128, 64], "int32"), "MW": ("sbuf", [128, 16], "float32"), "COL": ("sbuf", [128, 8], "float32"),
     "GS": ("sbuf", [128, 24], "float32"),
     "ZB": ("sbuf", [128, 144], "bfloat16"), "ZV": ("sbuf", [128, 144], "bfloat16"), "ZY": ("sbuf", [128, 144], "bfloat16"),
-    "IF": ("sbuf", [128, 128], "float32"), "IB": ("sbuf", [128, 640], "bfloat16"), "ONE": ("sbuf", [128, 704], "bfloat16"),
-    "VC": ("sbuf", [128, KD], "float32"),
+    "IF": ("sbuf", [128, 128], "float32"), "IB": ("sbuf", [128, 896], "bfloat16"), "ONE": ("sbuf", [128, 640], "bfloat16"),
+    "VC": ("sbuf", [128, KW], "bfloat16"),
     "PS": ("psum", [128, 2048], "float32"),
     "PZ": ("psum", [128, 512], "float32"), "PW": ("psum", [128, 512], "float32"),
     "PN": ("psum", [128, 512], "float32"), "PX": ("psum", [128, 512], "float32"),
-    "DF": ("dram", [10 * ROWS, NB], "float32"), "DH": ("dram", [6 * ROWS, NB], "bfloat16"),
+    "DF": ("dram", [10 * ROWS, NB], "float32"), "DH": ("dram", [7 * ROWS, NB], "bfloat16"),
 }
 NDMA = 80
 SEMAPHORES = ["cV", "cA", "cP", "cG", "sent"] + ["d%d" % i for i in range(NDMA)] + ["r%d" % i for i in range(16)]
 
-CY, GA, GT, FIX, PEC, LAT = 1.0e-3, 1.56, 1.8, 0.07, 0.55e-3, 0.12
-TUNE = {"win": 0.05, "flex": {}, "bias": {
-    'bc0': -8, 'Se3': -2, 'Td2': 8, 'af1': -4, 'lo4': -8, 'z2': 16, 'abs0': -2, 'dll3': -4, 'kZB': 8, 'abs1': 2, 'sg1': -2, 'xy4': 16, 'nh6': 2,
-    'cw1': 2, 'sa4': 16, 'gw2': 2, 'b1p': 8, 'Se1': 16, 'qi': -2, 'th5': -2, 'ca2': 4, 'Te4': 8, 'pr2': -8, 'Se4': 16, 'k15': -4, 'Txd': -2,
-    'dl5': -4, 'k0p': -16, 'kZV': 16, 'cw0': -6, 'Sc1': 4, 'k6': -8, 'b0i': -4, 'k28': 2, 'gy6': -8, 'ns3': 16, 'gy4': -16, 'bl3': -8, 'sp5': 16,
-    'ybl3': -4, 'adv5': -4, 'sty2': -8, 'k10': 2, 'sp6': -8, 'sv3': -16, 'Tx24': -4}}
+EST = {"cy": 0.88e-3, "ga": 1.56, "gt": 1.7, "fix": 0.05, "pe": 0.46e-3, "lat": 0.12, "dma": 0.9, "kb": 0.22}
+CASES = [{"cy": 0.83e-3, "ga": 1.56, "gt": 1.56, "fix": 0.05, "pe": 0.42e-3, "lat": 0.1, "dma": 0.85, "kb": 0.235},
+         {"cy": 0.9e-3, "ga": 1.1, "gt": 1.1, "fix": 0.05, "pe": 0.5e-3, "lat": 0.25, "dma": 1.3, "kb": 0.25},
+         {"cy": 1.2e-3, "ga": 1.9, "gt": 2.0, "fix": 0.06, "pe": 0.6e-3, "lat": 0.12, "dma": 0.9, "kb": 0.215}]
+TUNE = {"tries": 25000, "slack": 0.002, "seed": 3, "free": 2, "pace": 2, "plan": True, "rounds": 2, "flex": {}, "bias": {}, "direct": "AAAA", "xq": "S", "xg": {"T": "V", "S": "A"}, "sp1": "AAP", "lo": "P", "last": "VAAV",
+        "cl": [(0, 1024), (1024, 2048), (2048, 2560), (2560, 3072)],
+        "setup": "c1 S tr ya T yb"}
+BIG = 16384.0
 
 
 def engine_split(src, peers, topo):
@@ -77,7 +75,8 @@ def engine_split(src, peers, topo):
     return out
 
 
-def make_ops(g, core, T, topo):
+def make_ops(g, core, T, topo, est=EST):
+    CY, GA, GT, FIX, PEC, DL = (est[k] for k in ("cy", "ga", "gt", "fix", "pe", "dma"))
     rank = T.rank_of(core)
     cores = list(T.cores)
     ops = []
@@ -100,12 +99,8 @@ def make_ops(g, core, T, topo):
             acc[k] = [e for e in acc.get(k, []) if not (a <= e[0] and e[1] <= b)] + [[a, b, i, True]]
         for (k, a, b) in r:
             acc.setdefault(k, []).append([a, b, i, False])
-        soft = set()
-        for b in bank:
-            soft.update(banks.get(b, []))
-            banks.setdefault(b, []).append(i)
         hard.discard(i)
-        ops.append({"name": name, "alts": alts, "hard": hard, "soft": soft - hard, "kind": kind, "lat": lat, "sem": sem, "inc": inc})
+        ops.append({"name": name, "alts": alts, "hard": hard, "bank": list(bank), "kind": kind, "move": 0.0, "lat": lat * DL, "sem": sem, "inc": inc})
         return i
 
     def vop(name, n, f, r, w, bank=(), mul=1.0, extra=()):
@@ -115,13 +110,14 @@ def make_ops(g, core, T, topo):
         return add(name, {"A": (FIX + 0.02 + max(64, n * mul) * CY, f)}, r, w, bank)
 
     def flex(name, n, fv, fa, r, w, bank=(), mul=1.0, who="VA"):
-        who = TUNE["flex"].get(name, who)
         alts = {}
-        if "A" in who:
+        if who != "V!":
             alts["A"] = (FIX + 0.02 + max(64, n * mul) * CY, fa)
-        if "V" in who:
+        if who != "A!":
             alts["V"] = (FIX + max(64, n * mul) * CY, fv)
-        return add(name, alts, r, w, bank)
+        i = add(name, alts, r, w, bank)
+        ops[i]["first"] = who[0] if who != "VA" else None
+        return i
 
     def pop(name, mms, r, w, bank, f32=False):
         def f(q):
@@ -135,19 +131,24 @@ def make_ops(g, core, T, topo):
     def gop(name, n, f, r, w):
         return add(name, {"G": (0.15 + 2 * n * CY, f)}, r, w)
 
-    def dma(name, eng, pairs, r, w, lat, extra=(), **kw):
+    def gcopy(name, o, x, r, w):
+        return gop(name, KW, lambda q: [q.affine_select(o, x, [[0, KW]], ALU.is_ge, 0.0, 0, 0)], r, w)
+
+    def dma(name, eng, pairs, r, w, kb, extra=(), **kw):
         s = "d%d" % cnt["d"]
         cnt["d"] += 1
         f = lambda q: [q.dma_start(o, x, **kw) for (o, x) in pairs]
-        iss = (1.0 if eng == "G" else 0.15) * len(pairs)
-        return add(name, {eng: (iss, f)}, r, w, (), extra, "dma", lat, s, 16 * len(pairs))
+        iss = (1.0 if eng == "G" else 0.12) * len(pairs)
+        i = add(name, {eng: (iss, f)}, r, w, (), extra, "dma", 2.2, s, 16 * len(pairs))
+        ops[i]["move"] = kb * est["kb"]
+        return i
 
     peers = [cores[(rank + d) % N] for d in range(1, N)]
     mine = engine_split(core, peers, topo)
     arrive = sum(len(engine_split(c, [x for x in cores if x != c], topo)[core]) for c in cores if c != core)
     sent = [0]
 
-    def send(name, dr, blk, dst, c0, key, extra=()):
+    def send(name, dr, blks, dst, c0, extra=()):
         s = "r%d" % cnt["r"]
         cnt["r"] += 1
 
@@ -156,20 +157,20 @@ def make_ops(g, core, T, topo):
             for d in range(1, N):
                 p = cores[(rank + d) % N]
                 rid, pid, se = topo.addr(p)
-                r0 = blk * ROWS + 16 * SHIFT[d]
-                trs.append(RemoteDMATransfer(dst_ids=[DstId(rid=rid, pnc=pid)], dma_engine_mask=sum(1 << e for e in mine[p]),
-                                             remote_sem=T.sem[s], src=T[dr][r0:r0 + 128, :],
-                                             dst=T[dst][:, c0 + (d - 1) * NB:c0 + d * NB]))
+                srcs = [T[dr][k * ROWS + 16 * SHIFT[d]:k * ROWS + 16 * SHIFT[d] + 128, :] for k in blks]
+                trs.append(RemoteDMATransfer(dst_ids=[DstId(rid=rid, pnc=pid)], dma_engine_mask=sum(1 << e for e in mine[p]), remote_sem=T.sem[s],
+                                             srcs=srcs, dsts=[T[dst][:, c0 + (d - 1) * NB:c0 + d * NB]], alu_op=len(blks) - 1))
             q.remote_dma_fused(trs, local_sem=T.sem.sent)
             return []
         sent[0] += sum(len(e) for e in mine.values())
-        i = add(name, {"G": (1.0, f)}, [(dr, blk, blk + 1)], (), (), extra, "rem")
-        return add(name + "a", {}, (), [(key, c0, c0 + (N - 1) * NB)], (), [i], "arr", 3.5, s, arrive)
+        i = add(name, {"G": (1.0 if cnt["r"] > 1 else 3.0, f)}, [(dr, k, k + 1) for k in blks], (), (), extra, "rem")
+        ops[i]["move"] = 3.0 * est["kb"]
+        return add(name + "a", {}, (), [(dst, c0, c0 + (N - 1) * NB)], (), [i], "arr", 3.0, s, arrive)
 
-    def stage(name, dr, blk, src, r, eng="S", extra=()):
+    def stage(name, dr, blk, src, r, eng="S"):
         r0 = blk * ROWS
         return dma(name, eng, [(T[dr][r0:r0 + 128, :], src[:, 0:NB]), (T[dr][r0 + 128:r0 + ROWS, :], src[0:ROWS - 128, 0:NB])],
-                   r, [(dr, blk, blk + 1)], 2.2, extra)
+                   r, [(dr, blk, blk + 1)], 1.75 if dr == "DF" else 0.9)
 
     def ts(o, x, s1, s2, o0, o1=None):
         if o1 is None:
@@ -188,8 +189,21 @@ def make_ops(g, core, T, topo):
     def ms(o, c):
         return lambda q: [q.memset(o, c)]
 
+    def step_at(name, o, x, thr, r, w, bank, who="VA"):
+        return flex(name, KW, ts(o, x, thr, None, ALU.is_ge), act(o, x, AF.Sigmoid, -STEEP * thr, STEEP), r + [("IB", 4, 5)], w, bank, who=who)
+
     def slot(nm, j, L):
-        return T[nm][:, :, j] if USE3D else T[nm][:, j::L]
+        return T[nm][:, j::L]
+
+    def mask(t, j, nm="A0"):
+        n, s0 = (LA, (t - 2) * LA) if nm == "A0" else (LB, 0)
+        return T[nm][:, s0 * KW + j:(s0 + n) * KW:n], (nm, s0 + j, s0 + j + 1)
+
+    def scan(name, t, nm, d1, out):
+        n, s0 = (LA, (t - 2) * LA) if nm == "A0" else (LB, 0)
+        vop(name, KW * n, lambda q: [q.tensor_tensor_scan(T.Y[:, out:out + KW * n], T[nm][:, s0 * KW:(s0 + n) * KW], T[d1][:, :], 0.0, ALU.mult, ALU.add)],
+            [(nm, s0, s0 + n), (d1, 0, n)], [("Y", out, out + KW * n)])
+        return T.Y[:, out + n - 1:out + KW * n:n], ("Y", out, out + KW * n)
 
     def lst(j, a=0, b=KW):
         return T.LST[:, j * KW + a:j * KW + b]
@@ -197,59 +211,65 @@ def make_ops(g, core, T, topo):
     def lr(j, a=0, b=KW):
         return ("LST", j * KW + a, j * KW + b)
 
-    def it(j):
-        return T.IT[:, j * KW:(j + 1) * KW]
+    def it(j, a=0, b=KW):
+        return T.IT[:, j * KW + a:j * KW + b]
 
-    def ir(j):
-        return ("IT", j * KW, (j + 1) * KW)
+    def ir(j, a=0, b=KW):
+        return ("IT", j * KW + a, j * KW + b)
+
+    YO = OFF[RO]
 
     def ft(j):
-        return T.FT[:, :] if j == 3 else T.Y[:, 5 * W + (11 + j) * KW:5 * W + (12 + j) * KW]
+        return T.FT[:, :] if j == 3 else T.Y[:, YO + (11 + j) * KW:YO + (12 + j) * KW]
 
     def fr(j):
-        return ("FT", 0, KW) if j == 3 else ("Y", 5 * W + (11 + j) * KW, 5 * W + (12 + j) * KW)
+        return ("FT", 0, KW) if j == 3 else ("Y", YO + (11 + j) * KW, YO + (12 + j) * KW)
 
-    def wrap(name, z, zk, src, sk, c0, c1, out, ok, o0, bank, f32, more=(), morer=()):
-        k0, k1 = (c0 % W) // 16, ((c1 - 1) % W) // 16 + 1
-        o = T[out][:, o0 + k0:o0 + k1]
+    def wrap(name, z, src, c0, c1, out, k0, more=(), morer=()):
+        n = (c1 - c0) // 16
+        o = T[out][:, k0:k0 + n]
         mms = [(o, T[z][:, 15 - i:143 - i], T[src][:, c0 + i:c1:16]) for i in range(16)]
-        mms += [(o, l, T[x][:, k0:k1]) for (l, x) in more]
-        return pop(name, mms, [(zk, 0, 1), (sk, c0, c1)] + list(morer), [(ok, o0 + k0, o0 + k1)], [bank], f32)
+        mms += [(o, l, T[x][:, c0 // 16:c1 // 16]) for (l, x) in more]
+        return pop(name, mms, [(z, 0, 1), (src, c0, c1)] + list(morer), [(out, k0, k0 + n)], [out])
 
-    L_CS, L_CT, L_A0, L_B0, L_D, L_F, L_YB = 0, 1, 2, 3, 1, 0, 9
+    L_CS, L_A0, L_B0, L_D, L_F, L_R, L_YB, L_CT = 0, 2, 3, 1, 0, 8, 9, 7
     L_A = {1: 2, 2: 2, 3: 5, 4: 6, 5: 5, 6: 6}
     L_B = {2: 3, 3: 4, 4: 3, 5: 4, 6: 3}
-    L_Y = {1: 2, 2: 2, 3: 7, 4: 8, 5: 7, 6: 8}
-    PB = ["P0", "P1"]
+    L_Y = {1: 2, 2: 2, 3: 7, 4: 8, 5: 7}
+    SW = ["SA", "SB"]
     KB = ["K0", "K1", "K2"]
     C3 = [(0, 1024), (1024, 2048), (2048, 3072)]
     C2 = [(0, 1536), (1536, 3072)]
-    CG = [(0, 256), (256, 1664), (1664, 3072)]
-    IDN, I240, I16, WT, IH = (T.IB[:, 128 * j:128 * j + 128] for j in range(5))
+    CG = [(0, 256), (256, 1536), (1536, 3072)]
+    IDN, I240, I16, WT, IH, INEG, IBIG = (T.IB[:, 128 * j:128 * j + 128] for j in range(7))
 
     for h, eng in ((0, "S"), (1, "A")):
-        dma("cur%d" % h, eng, [(T.CT[0:96, gg, :], T.cur[gg:gg + 1, :]) for gg in range(4 * h, 4 * h + 4)], (), [("CT", h, h + 1)], 2.3)
+        dma("cur%d" % h, eng, [(T.CT[0:96, gg, :], T.cur[gg:gg + 1, :]) for gg in range(4 * h, 4 * h + 4)], (), [("CT", h, h + 1)], 0.5)
     for c, (a, b) in enumerate(C3):
-        dma("pt%d" % c, "S", [(T.PT[:, a:b], T.pt[:, a:b])], (), [("PT", a, b)], 2.9 + 0.9 * c)
+        dma("pt%d" % c, "S", [(T.PT[:, a:b], T.pt[:, a:b])], (), [("PT", a, b)], 4)
     stage("st0", "DH", 0, T.s0, (), "A")
-    dma("s0", "A", [(T.SD[:, 0:V], T.s0[:, :])], (), [("SD", 0, V)], 5.0)
-    send("x0", "DH", 0, "SD", V, "SD")
+    for a, b in C2:
+        dma("s0", "S", [(T.SD[:, a:b], T.s0[:, a:b])], (), [("SD", a, b)], 3)
+    send("x0", "DH", [0], "SD", V)
 
     gop("i0", 16, lambda q: [q.iota(T.RI[:, 0:16], [[-1, 16]], 128, 1)], (), [("RI", 0, 16)])
     gop("i1", 8, lambda q: [q.iota(T.RI[:, 32:40], [[-16, 8]], 0, 1)], (), [("RI", 32, 40)])
     II = T.IT[:, 5 * KW:5 * KW + 128]
     gop("i2", 128, lambda q: [q.iota(II, [[1, 128]], 128, -1)], (), [ir(5)])
-    gop("i3", KD, lambda q: [q.iota(T.VC[:, :], [[16, KD]], 0, 0, allow_small_or_imprecise_dtypes=True)], (), [("VC", 0, KD)])
+    gop("i3", KW, lambda q: [q.iota(T.VC[:, :], [[16, KW]], 0, 0, allow_small_or_imprecise_dtypes=True)], (), [("VC", 0, KW)])
+    gop("i6", 48, lambda q: [q.iota(T.HI[:, KW:KD], [[16, KD - KW]], V, 0, allow_small_or_imprecise_dtypes=True)], (), [("HI", KW, KD)])
+
+    def fill(name, o, c, w):
+        n = o.shape[1]
+        gop(name, n, lambda q: [q.iota(o, [[0, n]], c, 0, allow_small_or_imprecise_dtypes=True)], (), w)
+
     vop("k0", 128, ts(IDN, II, 128.0, None, ALU.is_equal), [ir(5)], [("IB", 0, 1)])
-    aop("k0h", 128, act(IH, IDN, AF.Identity, 0.0, 0.5), [("IB", 0, 1)], [("IB", 4, 5)])
-    aop("k0f", 128, act(T.IF[:, :], IDN, AF.Identity), [("IB", 0, 1)], [("IF", 0, 1)])
-    aop("k19", 128, act(I240, IDN, AF.Identity, 0.0, float(KD)), [("IB", 0, 1)], [("IB", 1, 2)])
-    aop("k20", 128, act(I16, IDN, AF.Identity, 0.0, 0.0625), [("IB", 0, 1)], [("IB", 2, 3)])
-    if PESP:
-        vop("k0o", 512, ms(T.ONE[0:1, 0:512], 1.0), (), [("ONE", 0, 1)], mul=0.5)
-        vop("k0p", 128, ms(T.ONE[0:1, 512:640], -0.5), (), [("ONE", 1, 2)], mul=0.5)
-    if ZOFF:
-        vop("k0q", 64, ms(T.ONE[0:1, 640:704], 64.0), (), [("ONE", 2, 3)], mul=0.5)
+    aop("k0h", 128, act(IH, IDN, AF.Sigmoid, -STEEP, STEEP), [("IB", 0, 1)], [("IB", 4, 5)], mul=12)
+    for nm, o, c, w in (("k0f", T.IF[:, :], 1.0, ("IF", 0, 1)), ("k19", I240, float(KD), ("IB", 1, 2)), ("k20", I16, 0.0625, ("IB", 2, 3)),
+                        ("k0n", INEG, -1.0, ("IB", 5, 6)), ("k0b", IBIG, BIG, ("IB", 6, 7))):
+        gop(nm, 128, lambda q, o=o, c=c: [q.affine_select(o, IDN, [[-1, 128]], ALU.not_equal, c, 0, 1)], [("IB", 0, 1)], [w])
+    fill("k0o", T.ONE[0:1, 0:512], 1, [("ONE", 0, 1)])
+    vop("k0p", 128, ms(T.ONE[0:1, 512:640], -0.5), (), [("ONE", 1, 2)], mul=0.5)
     vop("k1", 16, ts(T.RI[:, 16:32], T.RI[:, 0:16], 15, None, ALU.bitwise_and), [("RI", 0, 16)], [("RI", 16, 32)])
     RR, rr = T.RI[:, 16:32], ("RI", 16, 32)
     vop("k2", 16, ts(T.MW[:, 0:16], RR, 0.0, None, ALU.is_equal), [rr], [("MW", 0, 16)])
@@ -257,37 +277,35 @@ def make_ops(g, core, T, topo):
     vop("k4", 8, ts(T.RI[:, 40:48], T.RI[:, 32:40], 4, None, ALU.arith_shift_right), [("RI", 32, 40)], [("RI", 40, 48)])
     vop("k5", 8, ts(T.GS[:, 0:8], T.RI[:, 40:48], 0.0, None, ALU.is_equal), [("RI", 40, 48)], [("GS", 0, 8)])
     R2, r2 = T.IT[:, 4 * KW:4 * KW + 128], ir(4)
-    w0, w1, w2 = (T.P0[:, 128 * j:128 * j + 128] for j in range(3))
+    w0, w1, w2 = (T.U[:, 128 * j:128 * j + 128] for j in range(3))
     vop("k6a", 128, ts(R2, II, 15, None, ALU.bitwise_and), [ir(5)], [r2])
-    vop("k6", 128, ts(w0, R2, 1.0, None, ALU.is_ge), [r2], [("P0", 0, 128)])
-    vop("k7", 128, ts(w1, R2, 3.0, 4095.0, ALU.is_ge, ALU.mult), [r2], [("P0", 128, 256)])
-    vop("k8", 128, ts(w2, R2, 5.0, -4096.0, ALU.is_ge, ALU.mult), [r2], [("P0", 256, 384)])
-    vop("k9", 128, tt(w1, w1, w2, ALU.add), [("P0", 128, 384)], [("P0", 128, 256)], mul=2)
-    vop("k10", 128, tt(w0, w0, w1, ALU.add), [("P0", 0, 256)], [("P0", 0, 128)], mul=2)
-    gop("i4", 128, lambda q: [q.affine_select(w1, w0, [[-16, 8], [0, 16]], ALU.is_ge, 0.0, 0, 1)], [("P0", 0, 128)], [("P0", 128, 256)])
-    gop("i5", 128, lambda q: [q.affine_select(WT, w1, [[16, 8], [0, 16]], ALU.is_ge, 0.0, 15, -1)], [("P0", 128, 256)], [("IB", 3, 4)])
+    vop("k6", 128, ts(w0, R2, 1.0, None, ALU.is_ge), [r2], [("U", 0, 128)])
+    vop("k7", 128, ts(w1, R2, 3.0, 4095.0, ALU.is_ge, ALU.mult), [r2], [("U", 128, 256)])
+    vop("k8", 128, ts(w2, R2, 5.0, -4096.0, ALU.is_ge, ALU.mult), [r2], [("U", 256, 384)])
+    vop("k9", 128, tt(w1, w1, w2, ALU.add), [("U", 128, 384)], [("U", 128, 256)], mul=2)
+    vop("k10", 128, tt(w0, w0, w1, ALU.add), [("U", 0, 256)], [("U", 0, 128)], mul=2)
+    gop("i4", 128, lambda q: [q.affine_select(w1, w0, [[-16, 8], [0, 16]], ALU.is_ge, 0.0, 0, 1)], [("U", 0, 128)], [("U", 128, 256)])
+    gop("i5", 128, lambda q: [q.affine_select(WT, w1, [[16, 8], [0, 16]], ALU.is_ge, 0.0, 15, -1)], [("U", 128, 256)], [("IB", 3, 4)])
     E = T.RI[:, 16:17]
     vop("k11", 1, ts(T.RI[:, 48:49], E, 1, None, ALU.bitwise_and), [rr], [("RI", 48, 49)])
     vop("k12", 1, ts(T.RI[:, 49:50], E, 11, None, ALU.bitwise_and), [rr], [("RI", 49, 50)])
     vop("k13", 1, cp(T.COL[:, 0:1], T.RI[:, 48:49]), [("RI", 48, 49)], [("COL", 0, 1)])
     vop("k14", 1, ts(T.COL[:, 1:2], T.RI[:, 48:49], -2.0, 1.0, ALU.mult, ALU.add), [("RI", 48, 49)], [("COL", 1, 2)])
-    vop("k15", 1, ts(T.COL[:, 2:3], T.RI[:, 49:50], 0.0, None, ALU.is_equal), [("RI", 49, 50)], [("COL", 2, 3)])
-    vop("k16", 1, ts(T.COL[:, 3:4], E, 8.0, None, ALU.is_equal), [rr], [("COL", 3, 4)])
-    vop("k17", 1, cp(T.COL[:, 4:5], E), [rr], [("COL", 4, 5)])
-    vop("k18", 1, ts(T.COL[:, 5:6], E, 7.5, None, ALU.subtract), [rr], [("COL", 5, 6)])
     for j in range(2):
         aop("kG%d" % j, 8, act(T.GS[:, 8 + 8 * j:16 + 8 * j], T.GS[:, 0:8], AF.Identity, 0.0, T.COL[:, j:j + 1]), [("GS", 0, 8), ("COL", j, j + 1)], [("GS", 8 + 8 * j, 16 + 8 * j)])
+    vop("k15", 1, ts(T.COL[:, 2:3], T.RI[:, 49:50], 0.0, None, ALU.is_equal), [("RI", 49, 50)], [("COL", 2, 3)])
+    vop("k16", 1, ts(T.COL[:, 3:4], E, 8.0, -1.0, ALU.is_equal, ALU.mult), [rr], [("COL", 3, 4)])
+    vop("k17", 1, cp(T.COL[:, 4:5], E), [rr], [("COL", 4, 5)])
+    vop("k18", 1, ts(T.COL[:, 5:6], E, 7.5, None, ALU.subtract), [rr], [("COL", 5, 6)])
     vop("kZB", 8, cp(T.ZB[:, 15:143:16], T.GS[:, 0:8]), [("GS", 0, 8)], [("ZB", 0, 1)])
     for nm, j in (("ZV", 2), ("ZY", 3)):
         aop("k" + nm, 144, act(T[nm][:, :], T.ZB[:, :], AF.Identity, 0.0, T.COL[:, j:j + 1]), [("ZB", 0, 1), ("COL", j, j + 1)], [(nm, 0, 1)])
-    aop("k21", 48, act(T.HI[:, KW:KD], T.VC[:, KW:KD], AF.Identity), [("VC", KW, KD)], [("HI", KW, KD)])
-    aop("k22", 48, act(T.LO[:, KW:KD], T.VC[:, KW:KD], AF.Identity, T.COL[:, 5:6], 0.0), [("VC", KW, KD), ("COL", 5, 6)], [("LO", KW, KD)])
-    aop("k23", KW, act(T.VC[:, 0:KW], T.VC[:, 0:KW], AF.Identity, T.COL[:, 4:5]), [("VC", 0, KW), ("COL", 4, 5)], [("VC", 0, KW)])
-    vop("k27", KW, ms(T.HS[:, 0:KW], 5.0), (), [("HS", 0, 1)], mul=0.5)
-    vop("k28", KW, ms(T.HT[:, 0:KW], 5.0), (), [("HT", 0, 1)], mul=0.5)
-    vop("k24", KW * LA, ms(T.A0[:], 0.0), (), [("A0", 0, LA)], mul=0.5)
-    vop("k25", KW * LB, ms(T.B0[:], 0.0), (), [("B0", 0, LB)], mul=0.5)
-    vop("k26", KW, ms(T.VER[:, 0:KW], 0.0), (), [("VER", 0, KW)], mul=0.5)
+    aop("k22", 48, act(T.LO[:, KW:KD], T.HI[:, KW:KD], AF.Identity, T.COL[:, 5:6], 0.0), [("HI", KW, KD), ("COL", 5, 6)], [("LO", KW, KD)])
+    fill("k28", T.HT[:, 0:KW], 5, [("HT", 0, 1)])
+    for t in range(2, RO):
+        fill("k24", T.A0[:, (t - 2) * KW * LA:(t - 1) * KW * LA], 0, [("A0", (t - 2) * LA, (t - 1) * LA)])
+    fill("k25", T.B0[:, :], 0, [("B0", 0, LB)])
+    fill("k26", T.AGE[:, :], 0, [("AGE", 0, KD)])
 
     for b in range(2):
         vop("cb%d" % b, 128, cp(T.CB[0:96, 128 * b:128 * b + 128], T.CT[0:96, :, 16 * b:16 * b + 16]), [("CT", 0, 2)], [("CB", b, b + 1)])
@@ -302,32 +320,26 @@ def make_ops(g, core, T, topo):
     vop("ctl", KW, cp(lst(L_CT), CT2), [("CI", 1, 2)], [lr(L_CT)])
 
     ychunk = [0]
+    gchunk = [0]
+    held = {}
 
-    def weigh(nm, l, lk, hot, a, b, src, sr, y0):
+    def weigh(nm, l, lk, hot, a, b, src, y0):
         u = ychunk[0] % 2
         ychunk[0] += 1
         n = b - a
         for h in range(0, n, 512):
             pop(nm + "m", [(T.PS[:, 1024 * u + h:1024 * u + h + 512], l, T[hot][:, a + h:a + h + 512])], [lk, (hot, a + h, a + h + 512)],
                 [("PS", 1024 * u + h, 1024 * u + h + 512)], ["PS%d" % (2 * u + h // 512)])
-        vop(nm + "p", n, tt(T.Y[:, y0 + a:y0 + b], T.PS[:, 1024 * u:1024 * u + n], src, ALU.mult), [("PS", 1024 * u, 1024 * u + n), sr],
+        vop(nm + "p", n, tt(T.Y[:, y0 + a:y0 + b], T.PS[:, 1024 * u:1024 * u + n], T[src][:, a:b], ALU.mult), [("PS", 1024 * u, 1024 * u + n), (src, a, b)],
             [("Y", y0 + a, y0 + b)], ["PS%d" % (2 * u + h // 512) for h in range(0, n, 512)])
 
-    def elect(nm, li, hot, y0, ps, chunks, tmp):
-        for c, (a, b) in enumerate(chunks):
-            src = T.MW[:, 0:16].indirect(lst(li, a // 16, b // 16))
-            if nm == "a" and b <= DIRECT:
-                vop("a%dp" % c, b - a, tt(T.Y[:, y0 + a:y0 + b], src, T.PT[:, a:b], ALU.mult), [("MW", 0, 16), lr(li), ("PT", a, b)],
-                    [("Y", y0 + a, y0 + b)], mul=GT)
-                flex("al%d" % c, b - a, cp(T[hot][:, a:b], src), act(T[hot][:, a:b], src, AF.Identity), [("MW", 0, 16), lr(li)], [(hot, a, b)], mul=GA, who="A")
-                continue
-            flex("%sh%d" % (nm, c), b - a, cp(T[hot][:, a:b], src), act(T[hot][:, a:b], src, AF.Identity), [("MW", 0, 16), lr(li)], [(hot, a, b)], mul=GA, who="A")
-            weigh("%s%d" % (nm, c), IDN, ("IB", 0, 1), hot, a, b, T.PT[:, a:b], ("PT", a, b), y0)
-        fold(nm, y0, 0, 1, ps, 256, tmp)
+    def onehot(nm, li, hot, a, b):
+        src = T.MW[:, 0:16].indirect(lst(li, a // 16, b // 16))
+        flex(nm, b - a, cp(T[hot][:, a:b], src), act(T[hot][:, a:b], src, AF.Identity), [("MW", 0, 16), lr(li), ("IB", 4, 5)], [(hot, a, b)], mul=GA, who="A")
 
-    def fold(nm, y0, g0, nc, ps, p0, tmp):
+    def fold(nm, y0, g0, nc, ps, p0, tmp, halves=(0, 1)):
         w = 128 * nc
-        for b in range(2):
+        for b in halves:
             c0 = y0 + 1536 * b
             for h in range(0, 16, 4):
                 mm = [(T[ps][0:96, p0 + w * b + i:p0 + w * b + w:16], T.Y[:, c0 + i:c0 + 1536:16], T.GS[:, g0:g0 + 8 * nc]) for i in range(h, h + 4)]
@@ -336,240 +348,252 @@ def make_ops(g, core, T, topo):
             o, x = T.Y[0:96, tmp + w * b:tmp + w * b + w], T[ps][0:96, p0 + w * b:p0 + w * b + w]
             flex("%sc%d" % (nm, b), w, cp(o, x), act(o, x, AF.Identity), [(ps + "f", 16 * b, 16 * b + 16), (ps, p0 + w * b, p0 + w * b + w)],
                  [("Y", tmp + w * b, tmp + w * b + w)], [ps], who="A")
-        for b in range(2):
+        for b in halves:
             for cl in range(nc):
                 t0, o0 = tmp + w * b + 128 * cl, KW * cl + 96 * b
                 pop("%st%d" % (nm, b), [(T[ps][:, o0:o0 + 96], T.Y[0:96, t0:t0 + 128], T.IF[0:96, 0:96])], [("Y", t0, t0 + 128), ("IF", 0, 1)],
                     [(ps, o0, o0 + 96)], [ps], True)
-    elect("a", L_CS, "K0", 3 * W, "PZ", [(0, 1024), (1024, 1536), (1536, 2048), (2048, 2560), (2560, 3072)], 5 * W)
-    vop("a0i", KW, cp(it(1), T.PZ[:, 0:KW]), [("PZ", 0, KW)], [ir(1)], ["PZ"])
-    vop("a0m", KW, ts(it(2), it(1), 4095, None, ALU.bitwise_and), [ir(1)], [ir(2)])
-    vop("a0l", KW, cp(lst(L_A0), it(2)), [ir(2)], [lr(L_A0)])
-    vop("a0s", KW, ts(slot("A1", 5, LA), it(2), 7.5, None, ALU.subtract), [ir(2)], [("A1", 5, 6)])
+
+    for c, (a, b) in enumerate(C3):
+        vop("Ss%d" % c, 1024, ts(T.PT[:, a:b], T.PT[:, a:b], 4095, None, ALU.bitwise_and), [("PT", a, b)], [("PT", a, b)])
+    for c, (a, b) in enumerate([(0, 1024), (1024, 1536), (1536, 2048), (2048, 3072)]):
+        onehot("oh%d" % c, L_CS, "HB", a, b)
+        if TUNE["direct"][c] == "V":
+            vop("a%dp" % c, b - a, tt(T.Y[:, OFF[2] + a:OFF[2] + b], T.MW[:, 0:16].indirect(lst(L_CS, a // 16, b // 16)), T.PT[:, a:b], ALU.mult),
+                [("MW", 0, 16), lr(L_CS), ("PT", a, b)], [("Y", OFF[2] + a, OFF[2] + b)], mul=GT)
+        else:
+            weigh("a%d" % c, IDN, ("IB", 0, 1), "HB", a, b, "PT", OFF[2])
+        if b % 1536 == 0:
+            h = b // 1536 - 1
+            k0, k1, ps = 96 * h, 96 * h + 96, ("PZ", "PW")[h]
+            fold("a", OFF[2], 0, 1, ps, 256, YO, [h])
+            vop("a0l", 96, cp(lst(L_A0, k0, k1), T[ps][:, k0:k1]), [(ps, k0, k1)], [lr(L_A0, k0, k1)], [ps])
+            o = T.A1[:, k0 * LA + 5:k1 * LA:LA]
+            flex("a0s", 96, ts(o, T[ps][:, k0:k1], 7.5, None, ALU.subtract), act(o, T[ps][:, k0:k1], AF.Identity, -7.5), [(ps, k0, k1)], [("A1", 5, 6)], [ps], who="A")
 
     for a, b in C2:
-        aop("abs0", b - a, act(T.SO[:, a:b], T.SD[:, a:b], AF.Abs), [("SD", a, b)], [("SO", a, b)])
-        dma("sw0", "S", [(T.SW[:, a:b], T.SO[:, a:b])], [("SO", a, b)], [("SW", a, b)], 3.4)
-    aop("abs1", W - V, act(T.SW[:, V:W], T.SD[:, V:W], AF.Abs), [("SD", V, W)], [("SW", V, W)])
-    aop("sg0", V, act(T.K1[:, 0:V], T.SD[:, 0:V], AF.Sign, -2.0 ** -30, -1.0), [("SD", 0, V)], [("K1", 0, V)])
+        aop("abs0", b - a, act(T.K0[:, a:b], T.SD[:, a:b], AF.Abs), [("SD", a, b)], [("K0", a, b)])
+        dma("so0", "S", [(T.WG[:, a:b], T.K0[:, a:b])], [("K0", a, b)], [("WG", a, b)], 3)
+    aop("abs1", W - V, act(T.K0[:, V:W], T.SD[:, V:W], AF.Abs), [("SD", V, W)], [("K0", V, W)])
+    for c, (a, b) in enumerate(CG):
+        aop("sg0_%d" % c, b - a, act(T.K1[:, a:b], T.SD[:, a:b], AF.Sign, -2.0 ** -30, -1.0), [("SD", a, b)], [("K1", a, b)])
+    stage("stc0", "DH", 1, T.K1, [("K1", 0, NB)])
 
     def trigger0():
-        elect("b", L_CT, "WG", 4 * W, "PW", C3, 5 * W + 512)
-        vop("b0i", KW, cp(it(3), T.PW[:, 0:KW]), [("PW", 0, KW)], [ir(3)], ["PW"])
-        vop("b0m", KW, ts(it(0), it(3), 12, None, ALU.logical_shift_right), [ir(3)], [ir(0)])
-        vop("b0l", KW, cp(lst(L_B0), it(0)), [ir(0)], [lr(L_B0)])
-        vop("b0s", KW, cp(slot("B1", 4, LB), it(0)), [ir(0)], [("B1", 4, 5)])
+        for c, (a, b) in enumerate(C3):
+            dma("pr%d" % c, "S", [(T.PT[:, a:b], T.pt[:, a:b])], (), [("PT", a, b)], 4)
+            vop("Ts%d" % c, 1024, ts(T.PT[:, a:b], T.PT[:, a:b], 12, None, ALU.logical_shift_right), [("PT", a, b)], [("PT", a, b)])
+            onehot("bh%d" % c, L_CT, "HB", a, b)
+            weigh("b%d" % c, IDN, ("IB", 0, 1), "HB", a, b, "PT", OFF[5])
+        fold("b", OFF[5], 0, 1, "PW", 256, YO + 512)
+        vop("b0l", KW, cp(lst(L_B0), T.PW[:, 0:KW]), [("PW", 0, KW)], [lr(L_B0)], ["PW"])
+        flex("b0s", KW, cp(slot("B1", 4, LB), T.PW[:, 0:KW]), act(slot("B1", 4, LB), T.PW[:, 0:KW], AF.Identity), [("PW", 0, KW)], [("B1", 4, 5)], ["PW"], who="A")
 
-    def tables(which):
-        for nm, hot, y0, cur, ck in ((("S", "K0", 3 * W, CS, 0), ("T", "WG", 4 * W, CT2, 1))[which],):
-            for c, (a, b) in enumerate(C3):
-                src, sr = T.PT[:, a:b], ("PT", a, b)
-                if nm == "S":
-                    vop("Ss%d" % c, 1024, ts(src, src, 4095, None, ALU.bitwise_and), [sr], [sr])
-                else:
-                    vop("Ts%d" % c, 1024, ts(src, src, 12, None, ALU.logical_shift_right), [sr], [sr])
-                weigh("%s%d" % (nm, c), WT, ("IB", 3, 4), hot, a, b, src, sr, y0)
-                if nm == "S":
-                    dma("pr%d" % c, "S", [(src, T.pt[:, a:b])], (), [sr], 2.9)
-            fold(nm, y0, 8, 2, "PX", 0, 5 * W + 512 * ck)
-            P1, P2 = T.PX[:, 0:KW], T.PX[:, KW:2 * KW]
-            p1, p2 = ("PX", 0, KW), ("PX", KW, 2 * KW)
-            vop(nm + "par", KW, ts(it(0), cur, 1, None, ALU.bitwise_and), [("CI", ck, ck + 1)], [ir(0)])
-            vop(nm + "md", KW, tt(ft(0), P2, it(0), ALU.mult), [p2, ir(0)], [fr(0)], ["PX"])
-            vop(nm + "x13", KW, tt(it(1), P1, ft(0), ALU.add), [p1, fr(0)], [ir(1)], ["PX"])
-            vop(nm + "xd", KW, tt(ft(1), P2, ft(0), ALU.subtract), [p2, fr(0)], [fr(1)], ["PX"])
-            vop(nm + "x24", KW, tt(it(2), P1, ft(1), ALU.add), [p1, fr(1)], [ir(2)], ["PX"])
-            vop(nm + "e1", KW, ts(it(3), it(1), 4095, None, ALU.bitwise_and), [ir(1)], [ir(3)])
-            vop(nm + "e2", KW, ts(it(4), it(2), 4095, None, ALU.bitwise_and), [ir(2)], [ir(4)])
-            vop(nm + "e3", KW, ts(it(5), it(1), 12, None, ALU.logical_shift_right), [ir(1)], [ir(5)])
-            vop(nm + "e4", KW, ts(it(0), it(2), 12, None, ALU.logical_shift_right), [ir(2)], [ir(0)])
-            D1, L = ("A1", LA) if nm == "S" else ("B1", LB)
-            if nm == "S":
-                vop("Sd1", KW, ts(ft(2), it(3), 7.5, None, ALU.subtract), [ir(3)], [fr(2)])
-            else:
-                vop("Td1", KW, tt(slot(D1, 3, L), it(3), slot(D1, 4, L), ALU.subtract), [ir(3), (D1, 4, 5)], [(D1, 3, 4)], mul=2)
-            vop(nm + "d2", KW, tt(slot(D1, 2, L), it(4), it(3), ALU.subtract), [ir(3), ir(4)], [(D1, 2, 3)], mul=2)
-            vop(nm + "d3", KW, tt(slot(D1, 1, L), it(5), it(4), ALU.subtract), [ir(5), ir(4)], [(D1, 1, 2)], mul=2)
-            vop(nm + "d4", KW, tt(slot(D1, 0, L), it(0), it(5), ALU.subtract), [ir(0), ir(5)], [(D1, 0, 1)], mul=2)
+    def tables(nm):
+        y0, cur, ck = (OFF[3], CS, 0) if nm == "S" else (OFF[4], CT2, 1)
+        for c, (a, b) in enumerate(C3):
+            weigh("%s%d" % (nm, c), WT, ("IB", 3, 4), "HB", a, b, "PT", y0)
+        fold(nm, y0, 8, 2, "PX", 0, YO + 768 + 512 * ck)
+        P1, P2 = T.PX[:, 0:KW], T.PX[:, KW:2 * KW]
+        p1, p2 = ("PX", 0, KW), ("PX", KW, 2 * KW)
+        vop(nm + "par", KW, ts(it(0), cur, 1, None, ALU.bitwise_and), [("CI", ck, ck + 1)], [ir(0)])
+        vop(nm + "md", KW, tt(ft(0), P2, it(0), ALU.mult), [p2, ir(0)], [fr(0)], ["PX"])
+        vop(nm + "x13", KW, tt(it(1), P1, ft(0), ALU.add), [p1, fr(0)], [ir(1)], ["PX"])
+        vop(nm + "xd", KW, tt(ft(1), P2, ft(0), ALU.subtract), [p2, fr(0)], [fr(1)], ["PX"])
+        vop(nm + "x24", KW, tt(it(2), P1, ft(1), ALU.add), [p1, fr(1)], [ir(2)], ["PX"])
+        vop(nm + "lo", 2 * KW, ts(T.IT[:, 3 * KW:5 * KW], T.IT[:, KW:3 * KW], 4095, None, ALU.bitwise_and), [ir(1), ir(2)], [ir(3), ir(4)])
+        vop(nm + "hi", 2 * KW, ts(T.IT[:, KW:3 * KW], T.IT[:, KW:3 * KW], 12, None, ALU.logical_shift_right), [ir(1), ir(2)], [ir(1), ir(2)])
+        e1, e2, e3, e4 = 3, 4, 1, 2
+        D1, L = ("A1", LA) if nm == "S" else ("B1", LB)
+        if nm == "S":
+            vop("Sd1", KW, ts(ft(2), it(e1), 7.5, None, ALU.subtract), [ir(e1)], [fr(2)])
+        else:
+            vop("Td1", KW, tt(slot(D1, 3, L), it(e1), slot(D1, 4, L), ALU.subtract), [ir(e1), (D1, 4, 5)], [(D1, 3, 4)], mul=2)
+        for j, (u, v) in enumerate(((e4, e3), (e3, e2), (e2, e1))):
+            vop(nm + "d%d" % (4 - j), KW, tt(slot(D1, j, L), it(u), it(v), ALU.subtract), [ir(u), ir(v)], [(D1, j, j + 1)], mul=2)
 
     carr = {}
     g1s = {}
     alpha = [slot("A1", 5, LA), ("A1", 5, 6)]
-    YO = 5 * W
 
     def lookup(t):
         al, ar = alpha
         vop("hi%d" % t, KW, ts(T.HI[:, 0:KW], al, MAGIC, MAGIC, ALU.add, ALU.subtract), [ar], [("HI", 0, KW)])
-        vop("lo%d" % t, KW, tt(T.LO[:, 0:KW], al, T.HI[:, 0:KW], ALU.subtract), [ar, ("HI", 0, KW)], [("LO", 0, KW)], mul=2)
+        if TUNE["lo"] == "V":
+            vop("lo%d" % t, KW, tt(T.LO[:, 0:KW], al, T.HI[:, 0:KW], ALU.subtract), [ar, ("HI", 0, KW)], [("LO", 0, KW)], mul=2)
+        else:
+            pop("lp%d" % t, [(T.PN[:, 0:KW], T.IF[:, :], al), (T.PN[:, 0:KW], INEG, T.HI[:, 0:KW])], [ar, ("HI", 0, KW), ("IF", 0, 1), ("IB", 5, 6)], [("PN", 0, KW)], ["PN"], 2.5)
+            flex("lo%d" % t, KW, cp(T.LO[:, 0:KW], T.PN[:, 0:KW]), act(T.LO[:, 0:KW], T.PN[:, 0:KW], AF.Identity), [("PN", 0, KW)], [("LO", 0, KW)], ["PN"])
         al, ar = slot("A1", 5, LA), ("A1", 5, 6)
         pop("dl%d" % t, [(T.PN[:, 0:KW], I240, T.LO[:, 0:KW]), (T.PN[:, 0:KW], I16, T.HI[:, 0:KW])],
             [("IB", 1, 3), ("LO", 0, KW), ("HI", 0, KW)], [("PN", 0, KW)], ["PN"])
         vop("dll%d" % t, KW, ts(lst(L_D), T.PN[:, 0:KW], 7.5 * KD, None, ALU.add), [("PN", 0, KW)], [lr(L_D)], ["PN"])
-        pairs, rd = [], []
-        if t < RO:
-            pairs += [(T.SD[0::16, :], T.HI[:, :]), (T.SD[4::16, :], T.LO[:, :])]
-            rd += [("HI", 0, KD), ("LO", 0, KD)]
+        pairs = [(T.SD[0::16, :], T.HI[:, :]), (T.SD[4::16, :], T.LO[:, :])]
+        rd = [("HI", 0, KD), ("LO", 0, KD)]
         if t > 2:
-            aop("vc%d" % t, 48, act(T.VER[:, KW:KD], T.HI[:, KW:KD], AF.Identity, float(W * (t - 2)), 0.0), [("HI", KW, KD)], [("VER", KW, KD)])
-            pairs += [(T.SD[8::16, :], T.VER[:, :])]
-            rd += [("VER", 0, KD)]
-        dma("D%d" % t, "S", pairs, rd, [("SD", 0, W)], 2.8)
+            pairs += [(T.SD[8::16, :], T.AGE[:, :])]
+            rd += [("AGE", 0, KD)]
+        dma("D%d" % t, "S", pairs, rd, [("SD", 0, W)], 3)
         for c, (a, b) in enumerate(C2):
             src = T.SD[:, :].indirect(lst(L_D, a // 16, b // 16))
-            flex("gw%d" % t, b - a, cp(T.WG[:, a:b], src), act(T.WG[:, a:b], src, AF.Identity),
+            flex("gw%d_%d" % (t, c), b - a, cp(T.WG[:, a:b], src), act(T.WG[:, a:b], src, AF.Identity),
                  [("SD", 0, W), lr(L_D)], [("WG", a, b)], mul=GA, who="A")
-            if t < RO:
-                wrap("via%d_%d" % (t, c), "ZV", "ZV", "WG", "WG", a, b, "PW", "PW", 0, "PW", False)
+            wrap("via%d_%d" % (t, c), "ZV", "WG", a, b, "PW", a // 16)
             if t > 2:
-                wrap("yo%d_%d" % (t, c), "ZY", "ZY", "WG", "WG", a, b, "PW", "PW", KW, "PW", False,
-                     [(IDN, "HI"), (IDN, "LO")], [("IB", 0, 1), ("HI", 0, KW), ("LO", 0, KW)])
+                wrap("yo%d_%d" % (t, c), "ZY", "WG", a, b, "PW", KW + a // 16, [(IDN, "HI"), (IDN, "LO")], [("IB", 0, 1), ("HI", 0, KW), ("LO", 0, KW)])
+        vop("sv%d" % t, KW, tt(slot("A1", 3, LA), ft(2), T.PW[:, 0:KW], ALU.subtract), [fr(2), ("PW", 0, KW)], [("A1", 3, 4)], ["PW"])
+        vop("dv%d" % t, KW, tt(slot("A1", 4, LA), T.PW[:, 0:KW], al, ALU.subtract), [ar, ("PW", 0, KW)], [("A1", 4, 5)], ["PW"])
         if t > 2:
-            vop("yl%d" % t, KW, ts(lst(L_Y[t]), T.PW[:, KW:2 * KW], 7.5, None, ALU.add), [("PW", KW, 2 * KW)], [lr(L_Y[t])], ["PW"])
-        if t < RO:
-            vop("sv%d" % t, KW, tt(slot("A1", 3, LA), ft(2), T.PW[:, 0:KW], ALU.subtract), [fr(2), ("PW", 0, KW)], [("A1", 3, 4)], ["PW"])
-            vop("dv%d" % t, KW, tt(slot("A1", 4, LA), T.PW[:, 0:KW], al, ALU.subtract), [ar, ("PW", 0, KW)], [("A1", 4, 5)], ["PW"])
+            vop("yl%d" % t, KW, ts(lst(L_Y[t]), T.PW[:, KW:2 * KW], 7.5 + OFF[t - 1], None, ALU.add), [("PW", KW, 2 * KW)], [lr(L_Y[t])], ["PW"])
 
     def product(t):
-        sw, nw, P = "SW", "SO", PB[t % 2]
-        k0, k1 = KB[t % 3], KB[(t + 1) % 3]
+        sw, nw, y0 = SW[(t - 1) % 2], SW[t % 2], OFF[t]
+        sw, so = (sw, "SO") if t > 1 else ("K0", "WG")
+        k1 = KB[(t + 1) % 3]
         sgn = 1.0 if t % 2 else -1.0
         g1 = []
         for c, (a, b) in enumerate(CG if t < RO else C3):
-            g1.append(vop("g1%d_%d" % (t, c), b - a, tt(T[P][:, a:b], T[sw][:, :].indirect(lst(L_A[t], a // 16, b // 16)), T[nw][:, a:b], ALU.mult),
-                          [(sw, 0, W), (nw, a, b), lr(L_A[t])], [(P, a, b)], mul=GT))
+            P, pr = T.Y[:, y0 + a:y0 + b], ("Y", y0 + a, y0 + b)
+            g1.append(vop("g1%d_%d" % (t, c), b - a, tt(P, T[sw][:, :].indirect(lst(L_A[t], a // 16, b // 16)), T[so][:, a:b], ALU.mult),
+                          [(sw, 0, W), (so, a, b), lr(L_A[t], a // 16, b // 16)], [pr], mul=GT))
             if t == RO:
                 continue
-            aop("ab%d_%d" % (t, c), b - a, act(T[nw][:, a:b], T[P][:, a:b], AF.Abs, 1.0, -2.0), [(P, a, b)], [(nw, a, b)])
-            aop("sg%d_%d" % (t, c), b - a, act(T[k1][:, a:b], T[P][:, a:b], AF.Sign, sgn * (0.875 + 2.0 ** -24), -1.75 * sgn), [(P, a, b)], [(k1, a, b)])
+            aop("ab%d_%d" % (t, c), b - a, act(T[nw][:, a:b], P, AF.Abs, 1.0, -2.0), [pr], [(nw, a, b)])
+            if c:
+                a0 = a if c > 1 else 0
+                dma("so%d_%d" % (t, c), "S", [(T.SO[:, a0:b], T[nw][:, a0:b])], [(nw, a0, b)], [("SO", a0, b)], 6)
+            aop("sg%d_%d" % (t, c), b - a, act(T[k1][:, a:b], P, AF.Sign, sgn * (0.875 + 2.0 ** -24), -1.75 * sgn), [pr], [(k1, a, b)])
             if c == 0:
                 stage("sts%d" % t, "DF", t - 1, T[nw], [(nw, 0, NB)])
-                send("xs%d" % t, "DF", t - 1, "SL", 0, "SL", [carr[t]] if t in carr else [])
-        if t < RO:
-            m = CG[2][0]
-            dma("sw%d_0" % t, "S", [(T.SW[:, 0:m], T.SO[:, 0:m])], [("SO", 0, m)], [("SW", 0, m)], 3.6)
-            dma("sw%d_1" % t, "S", [(T.SW[:, m:V], T.SO[:, m:V])], [("SO", m, V)], [("SW", m, V)], 3.6)
-            g1 = [dma("sw%d_2" % t, "S", [(T.SW[:, V:W], T.SL[:, :])], [("SL", 0, W - V)], [("SW", V, W)], 2.8)]
+                send("xs%d" % t, "DF", [t - 1], nw, V, [carr[t - 1]] if t > 1 else [])
+                stage("stc%d" % t, "DH", t + 1, T[k1], [(k1, 0, NB)])
         g1s[t] = g1
 
     def crossings(t):
         k0, k1 = KB[t % 3], KB[(t + 1) % 3]
-        dma("cb%d" % t, "G", [(T[k0][:, 0:NB], T[k1][:, 0:NB])], [(k0, 0, NB), (k1, 0, NB)], [(k0, 0, NB)], 2.6, accum_op=ALU.add)
-        stage("stc%d" % t, "DH", t, T[k0], [(k0, 0, NB)])
-        dma("ca%d" % t, "G", [(T[k0][:, NB:V], T[k1][:, NB:V])], [(k0, NB, V), (k1, NB, V)], [(k0, NB, V)], 4.5,
-            accum_op=ALU.add, max_dma_last_dim=V - NB)
-        carr[t + 1] = send("xc%d" % t, "DH", t, k0, V, k0, g1s[t] + ([carr[t]] if t in carr else []))
+        carr[t] = send("xc%d" % t, "DH", [t, t + 1], k0, V, g1s[t] + held.get(t, []) + ([carr[t - 1]] if t > 1 else []))
+        dma("ca%d" % t, "G", [(T[k0][:, 0:V], T[k1][:, 0:V])], [(k0, 0, V), (k1, 0, V)], [(k0, 0, V)], 12, accum_op=ALU.add, max_dma_last_dim=V)
 
     def sums(t):
         cw, k0 = KB[(t - 1) % 3], KB[t % 3]
         for c, (a, b) in enumerate(C3):
             u = (a + 1024 * t) % 2048
             src, o, tr = T[cw][:, :].indirect(lst(L_B[t], a // 16, b // 16)), T.TT[:, u:u + 1024], ("TT", u, u + 1024)
-            more = ()
-            if (t, c) in ZOFF:
-                aop("gd%d_%d" % (t, c), 1024, act(o, src, AF.Identity), [(cw, 0, W), lr(L_B[t])], [tr], mul=GA)
-                w = ychunk[0] % 2
-                ychunk[0] += 1
-                for h in (0, 512):
-                    ps = T.PS[:, 1024 * w + h:1024 * w + h + 512]
-                    pop("ge%d" % t, [(ps, IH, T.TT[:, u + h:u + h + 512]), (ps, IDN, T[k0][:, a + h:a + h + 512])],
-                        [tr, (k0, a, b), ("IB", 0, 5)], [("PS", 1024 * w + h, 1024 * w + h + 512)], ["PS%d" % (2 * w + h // 512)])
-                aop("gf%d_%d" % (t, c), 1024, act(o, T.PS[:, 1024 * w:1024 * w + 1024], AF.Abs, 0.0, 2.0), [("PS", 1024 * w, 1024 * w + 1024)], [tr],
-                    ["PS%d" % (2 * w), "PS%d" % (2 * w + 1)])
-                k0c, o0 = a // 16, T.PZ[:, a // 16:b // 16]
-                pop("z%d_%d" % (t, c), [(o0, T.ZB[:, 15 - i:143 - i], T.TT[:, u + i:u + 1024:16]) for i in range(16)] + [(o0, T.ONE[0:1, 512:640], T.ONE[0:1, 640:704])],
-                    [("ZB", 0, 1), tr, ("ONE", 1, 3)], [("PZ", k0c, k0c + 64)], ["PZ"])
-                continue
             vop("gc%d_%d" % (t, c), b - a, tt(o, src, T[k0][:, a:b], ALU.mult), [(cw, 0, W), lr(L_B[t]), (k0, a, b)], [tr], mul=GT)
-            wrap("z%d_%d" % (t, c), "ZB", "ZB", "TT", "TT", u, u + 1024, "PZ", "PZ", (a - u) // 16, "PZ", False)
+            wrap("z%d_%d" % (t, c), "ZB", "TT", u, u + 1024, "PZ", a // 16)
+
+    def places(name, t, li, n, ps):
+        pop(name + "p", [(T[ps][:, 0:n], INEG, T.AGE[:, 0:n]), (T[ps][:, 0:n], IDN, T.VC[:, 0:n])],
+            [("IB", 0, 1), ("IB", 5, 6), ("AGE", 0, KW), ("VC", 0, KW)], [(ps, 0, n)], [ps])
+        vop(name, n, ts(lst(li, 0, n), T[ps][:, 0:n], T.COL[:, 4:5], float(OFF[t]), ALU.add, ALU.add), [(ps, 0, n), ("COL", 4, 5)], [lr(li, 0, n)], [ps])
 
     def turn(t):
         Z, z = T.PZ[:, 0:KW], ("PZ", 0, KW)
         j = t - 1
-        hs, ht = T.HS[:, j * KW:(j + 1) * KW], T.HT[:, j * KW:(j + 1) * KW]
+        ht = T.HT[:, j * KW:(j + 1) * KW]
         if t < RO:
-            vop("g4%d" % t, KW, ts(slot("A0", 5, LA), Z, 3.0, None, ALU.is_ge), [z], [("A0", 5, 6)], ["PZ"])
-            vop("adv%d" % t, KW, ts(slot("A0", 4, LA), Z, 7.0, None, ALU.is_ge), [z], [("A0", 4, 5)], ["PZ"])
+            step_at("g4%d" % t, mask(t, 5)[0], Z, 3.0, [z], [mask(t, 5)[1]], ["PZ"])
+            step_at("adv%d" % t, mask(t, 4)[0], Z, 7.0, [z], [mask(t, 4)[1]], ["PZ"])
+        else:
+            step_at("adv%d" % t, T.HS[:, :], Z, 7.0, [z], [("HS", 0, 1)], ["PZ"], "V!")
         aop("ht%d" % t, KW, act(ht, Z, AF.Sign, -5.0, -1.0), [z], [("HT", j, j + 1)], ["PZ"])
-        aop("hs%d" % t, KW, act(hs, Z, AF.Sign, -7.0, 1.0), [z], [("HS", j, j + 1)], ["PZ"])
         if t == 2:
-            aop("mt%d" % t, KW, act(slot("B0", 4, LB), ht, AF.Relu), [("HT", j, j + 1)], [("B0", 4, 5)])
-        aop("nh%d" % t, KW, act(T.NH[:, :], ht, AF.Relu, 0.0, -float(W * (t - 1))), [("HT", j, j + 1)], [("NH", 0, 1)])
-        vop("ver%d" % t, KW, tt(T.VER[:, 0:KW], T.VER[:, 0:KW], T.NH[:, :], ALU.max), [("VER", 0, KW), ("NH", 0, 1)], [("VER", 0, KW)], mul=1.5)
+            aop("mt%d" % t, KW, act(mask(t, 4, "B0")[0], ht, AF.Relu), [("HT", j, j + 1)], [mask(t, 4, "B0")[1]])
+        G = T.PZ[:, KW:2 * KW]
+        pop("ag%d" % t, [(G, IDN, T.AGE[:, 0:KW]), (G, IBIG, ht)], [("IB", 0, 1), ("IB", 6, 7), ("AGE", 0, KW), ("HT", j, j + 1)], [("PZ", KW, 2 * KW)], ["PZ"])
+        c = float(OFF[t] - OFF[t - 1]) - BIG
+        flex("age%d" % t, KW, ts(T.AGE[:, 0:KW], G, c, 0.0, ALU.add, ALU.max), act(T.AGE[:, 0:KW], G, AF.Relu, c), [("PZ", KW, 2 * KW)], [("AGE", 0, KW)], ["PZ"])
         if t < RO:
-            la = t + 1 if USE3D else LA
-            d0, d1 = (T.A0[:, :, LA - la:LA], T.A1[:, :, LA - la:LA]) if USE3D else (T.A0[:, :], T.A1[:, :])
-            vop("sa%d" % t, KW * la, lambda q: [q.tensor_tensor_scan(T.Y[:, YO:YO + KW * la], d0, d1, 0.0, ALU.mult, ALU.add)],
-                [("A0", LA - la, LA), ("A1", LA - la, LA)], [("Y", YO, YO + KW * la)])
-            na, nr = T.Y[:, YO + la - 1:YO + KW * la:la], ("Y", YO, YO + KW * la)
+            na, nr = scan("sa%d" % t, t, "A0", "A1", YO)
             vop("al%d" % t, KW, ts(lst(L_A[t + 1]), na, 7.5, None, ALU.add), [nr], [lr(L_A[t + 1])])
-            aop("as%d" % t, KW, act(slot("A1", 5, LA), na, AF.Identity), [nr], [("A1", 5, 6)])
+            if t < RO - 1:
+                gcopy("as%d" % t, slot("A1", 5, LA), na, [nr], [("A1", 5, 6)])
             alpha[0], alpha[1] = na, nr
             if t > 2:
                 pop("nt%d" % t, [(T.PN[:, KW:2 * KW], IDN, T.HT[:, u * KW:(u + 1) * KW]) for u in range(1, t)],
                     [("IB", 0, 1), ("HT", 1, t)], [("PN", KW, 2 * KW)], ["PN"])
                 for m in range(1, t):
-                    vop("mt%d_%d" % (t, m), KW, ts(slot("B0", LB - m, LB), T.PN[:, KW:2 * KW], float(2 * m - t), None, ALU.is_ge),
-                        [("PN", KW, 2 * KW)], [("B0", LB - m, LB - m + 1)], ["PN"])
-            lb = t if USE3D else LB
-            yb = YO + KW * LA
-            e0, e1 = (T.B0[:, :, LB - lb:LB], T.B1[:, :, LB - lb:LB]) if USE3D else (T.B0[:, :], T.B1[:, :])
-            vop("sb%d" % t, KW * lb, lambda q: [q.tensor_tensor_scan(T.Y[:, yb:yb + KW * lb], e0, e1, 0.0, ALU.mult, ALU.add)],
-                [("B0", LB - lb, LB), ("B1", LB - lb, LB)], [("Y", yb, yb + KW * lb)])
-            vop("bl%d" % t, KW, cp(lst(L_B[t + 1]), T.Y[:, yb + lb - 1:yb + KW * lb:lb]), [("Y", yb, yb + KW * lb)], [lr(L_B[t + 1])])
+                    step_at("mt%d_%d" % (t, m), mask(t, LB - m, "B0")[0], T.PN[:, KW:2 * KW], float(2 * m - t),
+                            [("PN", KW, 2 * KW)], [mask(t, LB - m, "B0")[1]], ["PN"], "A")
+            nb, br = scan("sb%d" % t, t, "B0", "B1", YO + KW * LA)
+            vop("bl%d" % t, KW, cp(lst(L_B[t + 1]), nb), [br], [lr(L_B[t + 1])])
 
     def counts(t):
         if t == 2:
-            aop("ms2", KW, act(slot("A0", 3, LA), T.HS[:, KW:2 * KW], AF.Relu), [("HS", 1, 2)], [("A0", 3, 4)])
+            gcopy("ms2", mask(3, 3)[0], mask(2, 4)[0], [mask(2, 4)[1]], [mask(3, 3)[1]])
             return
-        pop("ns%d" % t, [(T.PN[:, KW:2 * KW], IDN, T.HS[:, u * KW:(u + 1) * KW]) for u in range(1, t)],
-            [("IB", 0, 1), ("HS", 1, t)], [("PN", KW, 2 * KW)], ["PN"])
+        pop("ns%d" % t, [(T.PN[:, KW:2 * KW], IDN, mask(u, 4)[0]) for u in range(2, t + 1)],
+            [("IB", 0, 1)] + [mask(u, 4)[1] for u in range(2, t + 1)], [("PN", KW, 2 * KW)], ["PN"])
         for m in range(1, t):
-            vop("ms%d_%d" % (t, m), KW, ts(slot("A0", 4 - m, LA), T.PN[:, KW:2 * KW], float(2 * m - t), None, ALU.is_ge),
-                [("PN", KW, 2 * KW)], [("A0", 4 - m, 5 - m)], ["PN"])
+            step_at("ms%d_%d" % (t, m), mask(t + 1, 4 - m)[0], T.PN[:, KW:2 * KW], m - 0.5,
+                    [("PN", KW, 2 * KW)], [mask(t + 1, 4 - m)[1]], ["PN"], "A")
 
-    def ystep(t):
-        P = PB[t % 2]
-        wn, we = ("SD", W) if t == 1 else ("Y", W * (t - 1))
-        y0 = W * (t - 1)
-        for c, (a, b) in enumerate(C3):
-            u = ychunk[0] % 2
-            ychunk[0] += 1
-            Uc, ur = T.U[:, 1024 * u:1024 * u + 1024], ("U", u, u + 1)
-            Sc, sr, bk = T.PS[:, 1024 * u:1024 * u + 1024], ("PS", 1024 * u, 1024 * u + 1024), ["PS%d" % (2 * u), "PS%d" % (2 * u + 1)]
-            src = T[wn][:, 0:we].indirect(lst(L_Y[t], a // 16, b // 16))
-            flex("gy%d" % t, 1024, ts(Uc, src, 1.0, None, ALU.add), act(Uc, src, AF.Identity, 1.0), [(wn, 0, we), lr(L_Y[t])], [ur], mul=GA, who="A")
-            if t in PESP:
-                for h in (0, 512):
-                    o = T.PS[:, 1024 * u + h:1024 * u + h + 512]
-                    pop("sp%d" % t, [(o, T.ONE[0:1, 512:640], T.ONE[0:1, 0:512]), (o, T.IF[:, :], T[P][:, a + h:a + h + 512])],
-                        [(P, a + h, a + h + 512), ("ONE", 0, 2), ("IF", 0, 1)], [("PS", 1024 * u + h, 1024 * u + h + 512)], [bk[h // 512]], 2.5)
+    def ymul(t, c, a, b, src, fn, bias, scale, rd):
+        y0, n, u = OFF[t], b - a, ychunk[0] % 2
+        ychunk[0] += 1
+        Uc, ur = T.U[:, 1024 * u:1024 * u + n], ("U", 1024 * u, 1024 * u + n)
+        Sc, sr, bk = T.PS[:, 1024 * u:1024 * u + n], ("PS", 1024 * u, 1024 * u + n), ["PS%d" % (2 * u + h) for h in range(n // 512)]
+        P, pr = T.Y[:, y0 + a:y0 + b], ("Y", y0 + a, y0 + b)
+        aop("gy%d_%d" % (t, c), n, act(Uc, src, fn, bias, scale), rd, [ur], mul=GA)
+        if t > 1 or TUNE["sp1"][c] == "P":
+            for h in range(0, n, 512):
+                o = T.PS[:, 1024 * u + h:1024 * u + h + 512]
+                pop("sp%d" % t, [(o, T.ONE[0:1, 512:640], T.ONE[0:1, 0:512]), (o, T.IF[:, :], T.Y[:, y0 + a + h:y0 + a + h + 512])],
+                    [("Y", y0 + a + h, y0 + a + h + 512), ("ONE", 0, 2), ("IF", 0, 1)], [("PS", 1024 * u + h, 1024 * u + h + 512)], [bk[h // 512]], 2.5)
+        else:
+            aop("sp%d" % t, n, act(Sc, P, AF.Identity, -0.5), [pr], [sr], bk)
+        vop("x%d_%d" % (t, c), n, tt(P, Uc, Sc, ALU.mult), [ur, sr], [pr], bk)
+
+    def ystep(t, cs=(0, 1, 2)):
+        y0 = OFF[t]
+        for c in cs:
+            a, b = C3[c]
+            li = lst(L_Y[t], a // 16, b // 16)
+            if t == 1:
+                ymul(t, c, a, b, T.SD[:, :].indirect(li), AF.Identity, 0.5, 0.5, [("SD", 0, W), lr(L_Y[t], a // 16, b // 16)])
             else:
-                aop("sp%d" % t, 1024, act(Sc, T[P][:, a:b], AF.Identity, 1.0, -2.0), [(P, a, b)], [sr], bk)
-            vop("x%d_%d" % (t, c), 1024, tt(Uc, Uc, Sc, ALU.mult), [ur, sr], [ur], bk)
-            aop("th%d_%d" % (t, c), 1024, act(T.Y[:, y0 + a:y0 + b], Uc, AF.Tanh, 0.0, -2.0 if t in PESP else 1.0), [ur], [("Y", y0 + a, y0 + b)])
-            if c == 0 and t < RO:
+                ymul(t, c, a, b, T.Y[:, 0:y0].indirect(li), AF.Sigmoid, 0.0, -8.0, [("Y", 0, y0), lr(L_Y[t]), ("IB", 4, 5)])
+            if c == 0 and t < RO - 1:
                 if t == 1:
                     stage("sty1", "DF", 5, T.Y, [("Y", 0, NB)])
                 else:
-                    vop("yb%d" % t, 16, tt(T.FT[:, 0:16], T.VER[:, 0:16], T.VC[:, 0:16], ALU.add), [("VER", 0, KW), ("VC", 0, KW)], [("FT", 0, 16)])
-                    vop("ybl%d" % t, 16, cp(lst(L_YB, 0, 16), T.FT[:, 0:16]), [("FT", 0, 16)], [lr(L_YB, 0, 16)])
+                    places("yb%d" % t, t, L_YB, 16, "PX")
                     s2 = T.Y[:, 0:y0 + NB].indirect(lst(L_YB, 0, 16))
                     flex("yg%d" % t, NB, cp(T.YBUS[:, :], s2), act(T.YBUS[:, :], s2, AF.Identity), [("Y", 0, y0 + NB), lr(L_YB, 0, 16)],
                          [("YBUS", 0, 1)], mul=GA, who="A")
                     stage("sty%d" % t, "DF", 4 + t, T.YBUS, [("YBUS", 0, 1)])
-                send("xy%d" % t, "DF", 4 + t, "Y", y0 + V, "Y")
-            if t == RO:
-                s3 = T.Y[:, 0:y0 + b].indirect(lst(L_F, a // 16, b // 16))
-                O = PB[(t + 1) % 2]
-                flex("fg%d" % c, 1024, cp(T[O][:, a:b], s3), act(T[O][:, a:b], s3, AF.Identity), [("Y", 0, y0 + b), lr(L_F)], [(O, a, b)], mul=GA)
-                dma("yo%d" % c, "S", [(T.y[:, a:b], T[O][:, a:b])], [(O, a, b)], (), 2.9)
+                send("xy%d" % t, "DF", [4 + t], "Y", y0 + V, [carr[t]] if t > 1 else [])
+
+    def resolve():
+        places("rl", 5, L_R, KW, "PX")
+        for c, (a, b) in enumerate([(0, NB), (NB, 1024), (1024, 2048), (2048, V)]):
+            src = T.Y[:, 0:OFF[5] + b].indirect(lst(L_R, a // 16, b // 16))
+            aop("rs_%d" % c, b - a, act(T.SA[:, a:b], src, AF.Sigmoid, 0.0, -8.0), [("Y", 0, OFF[5] + b), lr(L_R)], [("SA", a, b)], mul=GA)
+            if c == 0:
+                stage("sty5", "DF", 9, T.SA, [("SA", 0, NB)])
+                send("xy5", "DF", [9], "SA", V, [carr[5]])
+
+    def last():
+        y0 = OFF[RO]
+        places("fl", RO, L_F, KW, "PW")
+        for c, (a, b) in enumerate(TUNE["cl"]):
+            P, pr = T.Y[:, y0 + a:y0 + b], ("Y", y0 + a, y0 + b)
+            src = T.SA[:, :].indirect(lst(L_A[RO], a // 16, b // 16))
+            if TUNE["last"][c] == "V":
+                flex("dh_%d" % c, b - a, ts(P, P, 0.5, None, ALU.subtract), act(P, P, AF.Identity, -0.5), [pr], [pr], who="A")
+                vop("x6_%d" % c, b - a, tt(P, src, P, ALU.mult), [("SA", 0, W), lr(L_A[RO]), pr], [pr], mul=GT)
+            else:
+                ymul(RO, c, a, b, src, AF.Identity, 0.0, 1.0, [("SA", 0, W), lr(L_A[RO])])
+            O, orr = T.SB[:, a:b], ("SB", a, b)
+            aop("fg_%d" % c, b - a, act(O, T.Y[:, 0:y0 + b].indirect(lst(L_F, a // 16, b // 16)), AF.Tanh, 0.0, -4.0),
+                [("Y", 0, y0 + b), lr(L_F)] + ([("tanh", 0, 1)] if c else []), [orr] + ([] if c else [("tanh", 0, 1)]), mul=GA + (0.0 if c else 1.7))
+            dma("yo%d" % c, "S", [(T.y[:, a:b], O)], [orr], (), (b - a) / 256)
 
     def finish():
-        vop("fl0", KW, tt(ft(3), T.VER[:, 0:KW], T.VC[:, 0:KW], ALU.add), [("VER", 0, KW), ("VC", 0, KW)], [fr(3)], mul=2)
-        vop("fl1", KW, cp(lst(L_F), ft(3)), [fr(3)], [lr(L_F)])
-        for h, nm in enumerate(("HS", "HT")):
-            pop("q%d" % h, [(T.PX[:, h * KW:(h + 1) * KW], IH, T[nm][:, u * KW:(u + 1) * KW]) for u in range(6)],
-                [("IB", 4, 5), (nm, 0, 6)], [("PX", h * KW, (h + 1) * KW)], ["PX"])
+        pop("q0", [(T.PX[:, 0:KW], IDN, x) for x in [mask(u, 4)[0] for u in range(2, RO)] + [T.HS[:, :]]],
+            [("IB", 0, 1), ("HS", 0, 1)] + [mask(u, 4)[1] for u in range(2, RO)], [("PX", 0, KW)], ["PX"])
+        pop("q1", [(T.PX[:, KW:2 * KW], IH, T.HT[:, u * KW:(u + 1) * KW]) for u in range(6)],
+            [("IB", 4, 5), ("HT", 0, 6)], [("PX", KW, 2 * KW)], ["PX"])
         vop("qi", 2 * KW, tt(T.IT[:, 0:2 * KW], T.PX[:, 0:2 * KW], T.CI[:, :], ALU.add), [("PX", 0, 2 * KW), ("CI", 0, 2)], [("IT", 0, 2 * KW)], ["PX"])
         vop("qm", 2 * KW, ts(T.IT[:, 2 * KW:4 * KW], T.IT[:, 0:2 * KW], 15, None, ALU.bitwise_and), [("IT", 0, 2 * KW)], [("IT", 2 * KW, 4 * KW)])
         vop("q16", KW, ts(ft(3), it(3), 16.0, None, ALU.mult), [ir(3)], [fr(3)])
@@ -580,88 +604,248 @@ def make_ops(g, core, T, topo):
         for b in range(2):
             vop("qc%d" % b, 128, cp(T.QT[0:96, :, 16 * b:16 * b + 16], T.PX[0:96, 128 * b:128 * b + 128]),
                 [("PX", 128 * b, 128 * b + 128)], [("QT", b, b + 1)], ["PX"])
-        dma("qo", "S", [(T.q[gg:gg + 1, :], T.QT[0:96, gg, :]) for gg in range(8)], [("QT", 0, 2)], (), 2.3)
+        dma("qo", "S", [(T.q[gg:gg + 1, :], T.QT[0:96, gg, :]) for gg in range(8)], [("QT", 0, 2)], (), 0.5)
 
     product(1)
-    crossings(1)
-    trigger0()
-    tables(0)
-    tables(1)
-    ystep(1)
-    for t in range(2, RO + 1):
+    parts = {"c1": lambda: crossings(1), "tr": trigger0, "S": lambda: tables("S"), "T": lambda: tables("T"), "y1": lambda: ystep(1),
+             "ya": lambda: ystep(1, [0]), "yb": lambda: ystep(1, [1, 2])}
+    for nm in TUNE["setup"].split():
+        parts[nm]()
+    for t in range(2, RO):
         lookup(t)
         product(t)
         sums(t)
-        if t < RO:
-            crossings(t)
+        crossings(t)
         turn(t)
-        if t == RO:
-            finish()
         ystep(t)
         if t < RO - 1:
             counts(t)
+    resolve()
+    product(RO)
+    sums(RO)
+    turn(RO)
+    last()
+    finish()
     return ops, sent[0]
 
 
-def schedule(ops):
+def place(ops, pri, back, eng):
     n = len(ops)
     succ = [[] for _ in range(n)]
     left = [0] * n
     for i, o in enumerate(ops):
-        for d in o["hard"] | o["soft"]:
-            succ[d].append(i)
-            left[i] += 1
-    pri = [0.0] * n
-    for i in range(n - 1, -1, -1):
-        o = ops[i]
-        c = min([a[0] for a in o["alts"].values()] or [0.0]) + o["lat"]
-        pri[i] = c + max([pri[s] + LAT for s in succ[i]] or [0.0])
-    for i, o in enumerate(ops):
-        pri[i] += TUNE["bias"].get(o["name"].split("_")[0], 0.0)
-    free = {e: 0.0 for e in "VAPGS"}
-    fin = [0.0] * n
-    eng = [None] * n
+        for d in o["hard"]:
+            a, b = (i, d) if back else (d, i)
+            succ[a].append(b)
+            left[b] += 1
+    line, lat = {}, EST["lat"]
+    fin, beg, t0, eng = [0.0] * n, [0.0] * n, [0.0] * n, list(eng)
     ready = [i for i in range(n) if left[i] == 0]
-    order = []
     while ready:
-        cand = []
-        for i in ready:
-            o = ops[i]
-            t0 = max([fin[d] + LAT for d in o["hard"]] or [0.0])
-            if not o["alts"]:
-                cand = [(-1.0, i, None, t0)]
-                break
-            best = None
-            for e, (c, f) in o["alts"].items():
-                t1 = max([t0, free[e]] + [fin[d] + LAT for d in o["soft"] if eng[d] != e])
-                if best is None or t1 + c < best[0] + best[3]:
-                    best = (t1, i, e, c)
-            cand.append(best)
-        first = min(cand)
-        if first[2] is None:
-            i = first[1]
-            fin[i] = first[3] + ops[i]["lat"]
-        else:
-            near = [c for c in cand if c[2] == first[2] and c[0] <= first[0] + TUNE["win"]]
-            t1, i, e, c = max(near, key=lambda x: (pri[x[1]], -x[1]))
-            eng[i] = e
-            free[e] = t1 + c
-            fin[i] = t1 + c + ops[i]["lat"]
-            ops[i]["t"] = t1
-        order.append(i)
+        i = max(ready, key=lambda x: (pri[x], -x))
         ready.remove(i)
+        o = ops[i]
+        wait = o["lat"] + o["move"]
+        beg[i], fin[i] = t0[i], t0[i] + wait
+        best = None
+        for e, (c, f) in o["alts"].items():
+            if eng[i] in (None, e):
+                t = t0[i] + (wait if back else 0.0)
+                busy = line.get(e, [])
+                if o["bank"]:
+                    busy = sorted(busy + [(a - lat, b + lat, x) for k in o["bank"] for (a, b, x) in line.get(k, []) if x != e and b + lat > t])
+                for (a, b, x) in busy:
+                    if a >= t + c:
+                        break
+                    t = max(t, b)
+                if best is None or t + c < best[0] + best[1]:
+                    best = (t, c, e)
+        if best:
+            t, c, e = best
+            for k in [e] + o["bank"]:
+                line[k] = sorted(line.get(k, []) + [(t, t + c, e)])
+            eng[i], beg[i], fin[i] = e, t, t + c + (0.0 if back else wait)
+            if o["move"] and not back:
+                t += c
+                for (a, b, x) in line.get("D", []):
+                    if a >= t + o["move"]:
+                        break
+                    t = max(t, b)
+                line["D"] = sorted(line.get("D", []) + [(t, t + o["move"], e)])
+                fin[i] = t + wait
         for s in succ[i]:
+            t0[s] = max(t0[s], fin[i] + EST["lat"])
             left[s] -= 1
             if left[s] == 0:
                 ready.append(s)
-    return order, eng, fin
+    return eng, fin, beg
+
+
+def kind(name):
+    head, cut, chunk = name.partition("_")
+    return (head[:-1] if head[-1].isdigit() and head[0] != "k" else head) + cut + chunk
+
+
+PLAN = {
+    "start": "k0h S0p af0 abs0 abs1 b0p a0l sg1_0 ab1_1 g11_0 af1 xs1a a2p a3p g11_1 S2p b1p bh1 bh0 Ts2 S1p ab1_2 xc1a bh2 Sd1 Ts1 Sd4 a1p Ts0 ca1 b2p T1p "
+             "sg1_2 g12_2 g11_2 xs2a sg2_2 Sd3 a0p gy1_2 T2p xc2a T0p x1_1 gw2_0 gc2_0 b0l Sd2 gw2_1 g12_1 g12_0 sg2_1 ca2 ab2_2 D2 gc2_2 x1_2 x1_0 sa2 "
+             "gy1_1 xy1a sg1_1 age2 gc2_1 ab2_1",
+    "step": "D+ sg+_2 g1+_0 xy-a g1+_2 sg+_1 xc+a x-_2 gw+_0 ca+ x-_1 ab+_2 bl- g1+_1 xs+a x-_0 sa+ gc+_2 age+ gw+_1 gc+_0 gc+_1 ab+_1 yl+",
+    "end": "gc6_0 yo1 bl5 x5_0 xy5a g16_1 x5_1 gc6_1 g16_0 g16_2 yo3 qo fl x5_2 yo2 gc6_2 rs_3 yo0",
+}
+
+
+def plan():
+    names = PLAN["start"].split()
+    for t in range(3, RO):
+        names += [x.replace("+", str(t)).replace("-", str(t - 1)) for x in PLAN["step"].split()]
+    return names + PLAN["end"].split()
+
+
+def schedule(ops):
+    n = len(ops)
+    pri = [0.0] * n
+    for i in range(n - 1, -1, -1):
+        o = ops[i]
+        pri[i] += min([a[0] for a in o["alts"].values()] or [0.0]) + o["lat"]
+        for d in o["hard"]:
+            pri[d] = max(pri[d], pri[i] + EST["lat"])
+    best = None
+    if TUNE["plan"]:
+        names = plan()
+        far, pri = pri, [-names.index(o["name"]) if o["name"] in names else -len(names) for o in ops]
+        for i in range(n - 1, -1, -1):
+            for d in ops[i]["hard"]:
+                pri[d] = max(pri[d], pri[i])
+        pri = [p + 1e-3 * f for p, f in zip(pri, far)]
+    for r in range(TUNE["rounds"]):
+        pri = [p + TUNE["bias"].get(o["name"], TUNE["bias"].get(kind(o["name"]), 0.0)) for p, o in zip(pri, ops)]
+        eng, fin, beg = place(ops, pri, False, [o.get("first") for o in ops])
+        if best is None or max(fin) < max(best[2]):
+            best = (sorted(range(n), key=lambda i: (beg[i], i)), eng, fin)
+        pri = place(ops, fin, True, eng)[1]
+    guard(ops, best[0], best[1])
+    return best
+
+
+def guard(ops, order, eng):
+    seen = {}
+    for i in order:
+        ops[i]["soft"] = set(seen[k][e] for k in ops[i]["bank"] for e in seen.get(k, {}) if e != eng[i])
+        for k in ops[i]["bank"]:
+            seen.setdefault(k, {})[eng[i]] = i
+
+
+def polish(cases, order, eng, tries):
+    ops = cases[0][0]
+    n = len(ops)
+    hard = [sorted(o["hard"]) for o in ops]
+    bank = [o["bank"] for o in ops]
+    succ = [set() for _ in ops]
+    for i in range(n):
+        for d in hard[i]:
+            succ[d].add(i)
+    cost = [([{e: a[0] for e, a in o["alts"].items()} for o in c], [o["lat"] for o in c], [o["move"] for o in c], w) for (c, w) in cases]
+    both = [i for i in range(n) if len(ops[i]["alts"]) > 1]
+
+    def run(order, eng, lo, old):
+        out = []
+        for (c, lat, move, wake), (end, fin) in zip(cost, old):
+            end, fin, free, seen, dma = list(end), list(fin), {}, {}, 0.0
+            for i in order[:lo]:
+                free[eng[i]] = end[i]
+                if move[i]:
+                    dma = fin[i] - lat[i]
+                for b in bank[i]:
+                    seen.setdefault(b, {})[eng[i]] = end[i]
+            for i in order[lo:]:
+                e, t = eng[i], -wake
+                for d in hard[i]:
+                    if fin[d] > t:
+                        t = fin[d]
+                for b in bank[i]:
+                    for x, u in seen.get(b, {}).items():
+                        if x != e and u > t:
+                            t = u
+                t += wake
+                if e:
+                    t = max(t, free.get(e, 0.0)) + c[i][e]
+                    free[e] = t
+                    for b in bank[i]:
+                        seen.setdefault(b, {})[e] = t
+                end[i] = t
+                if move[i]:
+                    t = dma = max(t, dma) + move[i]
+                fin[i] = t + lat[i]
+            out.append((end, fin))
+        return out
+
+    def tight(order, eng, now):
+        out = []
+        for (c, lat, move, wake), (end, fin) in zip(cost, now):
+            before, last = {}, {}
+            for i in order:
+                before[i] = last.get(eng[i])
+                last[eng[i]] = i
+            i = max(range(n), key=lambda x: fin[x])
+            while i is not None:
+                out.append(i)
+                j = before[i] if eng[i] else None
+                if j is None or end[j] < end[i] - c[i][eng[i]] - 1e-9:
+                    out += [j] if j is not None else []
+                    j = max(hard[i], key=lambda x: fin[x]) if hard[i] else None
+                i = j
+        return out
+
+    now = run(order, eng, 0, [([0.0] * n, [0.0] * n)] * len(cost))
+    base = [max(f) for (x, f) in now]
+    best, seed, hot = float(len(cost)), TUNE["seed"], tight(order, eng, now)
+    for k in range(tries):
+        seed = (seed * 1103515245 + 12345) % 2 ** 31
+        r, o2, e2 = seed >> 8, order, eng
+        if r % 12 == 0:
+            i = both[r // 12 % len(both)]
+            e2 = list(eng)
+            e2[i] = "A" if eng[i] == "V" else "V"
+            lo = order.index(i)
+        else:
+            p = q = r // 12 % n if r % 5 < TUNE["free"] else order.index(hot[r // 12 % len(hot)])
+            i, hops, up = order[p], 1 + r % 3, r % 4 < 2
+            while hops and eng[i] and (q > 0 and order[q - 1] not in ops[i]["hard"] if up else q < n - 1 and order[q + 1] not in succ[i]):
+                q += -1 if up else 1
+                hops -= eng[order[q]] == eng[i]
+            if hops == 1 + r % 3:
+                continue
+            o2 = list(order)
+            o2.insert(q, o2.pop(p))
+            lo = min(p, q)
+        new = run(o2, e2, lo, now)
+        score = sum(max(f) / b for (x, f), b in zip(new, base))
+        if score <= best + TUNE["slack"] * max(0.0, 1.0 - 1.25 * k / tries) * (seed >> 4 & 15) / 15:
+            if score < best or k % 8 == 0:
+                hot = tight(o2, e2, new)
+            best, order, eng, now = score, o2, e2, new
+    return order, eng
+
+
+DONE = []
+
+
+def arrange(g, core, T, topo, ops):
+    if not DONE:
+        order, eng, fin = schedule(ops)
+        DONE.append(polish([(make_ops(g, core, T, topo, c)[0], c["lat"]) for c in CASES], order, eng, TUNE["tries"]))
+    order, eng = DONE[0]
+    guard(ops, order, eng)
+    return order, eng
 
 
 def rank_program(g, core, T, topo):
     if T.rank_of(core) is None:
         return
     ops, sent = make_ops(g, core, T, topo)
-    order, eng, fin = schedule(ops)
+    order, eng = arrange(g, core, T, topo, ops)
+    fin = {i: k for k, i in enumerate(order)}
     Q = {"V": g.vector, "A": g.scalar, "P": g.tensor, "G": g, "S": g.sync}
     known = {e: {} for e in Q}
     count = {e: 0 for e in Q}

from concourse.bass import DstId, RemoteDMATransfer
from concourse.mybir import AluOpType, ActivationFunctionType

ALU = AluOpType
AF = ActivationFunctionType
N, V, NB, W, RO = 4, 3072, 256, 3840, 6
KW, KD = V // 16, W // 16
SHIFT = [d * (d + 1) // 2 for d in range(N)]
ROWS = 128 + 16 * SHIFT[N - 1]
MAGIC = 201326592.0
LA, LB = 6, 5
OFF = [None] + [W * j for j in range(5)] + [4 * W + V]
STEEP = 200.0

TH = V // 3
SCRATCH = {
    "Y": ("sbuf", [128, 4 * W + 2 * V], "float32"),
    "HB": ("sbuf", [128, V], "bfloat16"),
    "SA": ("sbuf", [128, W], "float32"), "SB": ("sbuf", [128, W], "float32"),
    "SD": ("sbuf", [128, W], "bfloat16"),
    "U": ("sbuf", [128, 2048], "float32"),
    "K0": ("sbuf", [128, W], "bfloat16"), "K1": ("sbuf", [128, W], "bfloat16"), "K2": ("sbuf", [128, W], "bfloat16"),
    "TT": ("sbuf", [128, 2048], "bfloat16"), "WG": ("sbuf", [128, V], "bfloat16"),
    "PT": ("sbuf", [128, V], "int32"), "SO": ("sbuf", [128, V], "float32"),
    "A1": ("sbuf", [128, KW * LA], "float32"), "A0": ("sbuf", [128, 4 * KW * LA], "bfloat16"),
    "B1": ("sbuf", [128, KW * LB], "float32"), "B0": ("sbuf", [128, KW * LB], "bfloat16"),
    "LST": ("sbuf", [128, 9 * KW + 16], "uint16"),
    "IT": ("sbuf", [128, 6 * KW], "int32"),
    "CI": ("sbuf", [128, 2 * KW], "int32"),
    "FT": ("sbuf", [128, KW], "float32"),
    "HI": ("sbuf", [128, KD], "bfloat16"), "LO": ("sbuf", [128, KD], "bfloat16"), "AGE": ("sbuf", [128, KD], "bfloat16"),
    "HS": ("sbuf", [128, KW], "bfloat16"), "HT": ("sbuf", [128, 6 * KW], "bfloat16"),
    "CT": ("sbuf", [128, 8, 32], "int32"), "CB": ("sbuf", [128, 256], "bfloat16"), "QT": ("sbuf", [128, 8, 32], "float32"),
    "YBUS": ("sbuf", [128, NB], "float32"),
    "RI": ("sbuf", [128, 64], "int32"), "MW": ("sbuf", [128, 16], "float32"), "COL": ("sbuf", [128, 8], "float32"),
    "GS": ("sbuf", [128, 24], "float32"),
    "ZB": ("sbuf", [128, 144], "bfloat16"), "ZV": ("sbuf", [128, 144], "bfloat16"), "ZY": ("sbuf", [128, 144], "bfloat16"),
    "IF": ("sbuf", [128, 128], "float32"), "IB": ("sbuf", [128, 896], "bfloat16"), "ONE": ("sbuf", [128, 640], "bfloat16"),
    "VC": ("sbuf", [128, KW], "bfloat16"),
    "PS": ("psum", [128, 2048], "float32"),
    "PZ": ("psum", [128, 512], "float32"), "PW": ("psum", [128, 512], "float32"),
    "PN": ("psum", [128, 512], "float32"), "PX": ("psum", [128, 512], "float32"),
    "DF": ("dram", [10 * ROWS, NB], "float32"), "DH": ("dram", [7 * ROWS, NB], "bfloat16"),
}
NDMA = 80
SEMAPHORES = ["cV", "cA", "cP", "cG", "sent"] + ["d%d" % i for i in range(NDMA)] + ["r%d" % i for i in range(16)]

EST = {"cy": 0.88e-3, "ga": 1.56, "gt": 1.7, "fix": 0.05, "pe": 0.46e-3, "lat": 0.12, "dma": 0.9, "kb": 0.22}
CASES = [{"cy": 0.83e-3, "ga": 1.56, "gt": 1.56, "fix": 0.05, "pe": 0.42e-3, "lat": 0.1, "dma": 0.85, "kb": 0.235},
         {"cy": 0.9e-3, "ga": 1.1, "gt": 1.1, "fix": 0.05, "pe": 0.5e-3, "lat": 0.25, "dma": 1.3, "kb": 0.25},
         {"cy": 1.2e-3, "ga": 1.9, "gt": 2.0, "fix": 0.06, "pe": 0.6e-3, "lat": 0.12, "dma": 0.9, "kb": 0.215}]
TUNE = {"tries": 25000, "slack": 0.002, "seed": 3, "free": 2, "pace": 2, "plan": True, "rounds": 2, "flex": {}, "bias": {}, "direct": "AAAA", "xq": "S", "xg": {"T": "V", "S": "A"}, "sp1": "AAP", "lo": "P", "last": "VAAV",
        "cl": [(0, 1024), (1024, 2048), (2048, 2560), (2560, 3072)],
        "setup": "c1 S tr ya T yb"}
BIG = 16384.0


def engine_split(src, peers, topo):
    use = {p: topo.engines(src, p) for p in peers}
    least = min(len(e) for e in use.values())
    tight = [p for p in peers if len(use[p]) == least]
    loose = [p for p in peers if len(use[p]) != least]
    out = {}
    taken = []
    for grp in (tight, loose):
        if not grp:
            continue
        free = [e for e in use[grp[0]] if e not in taken]
        n = 1
        while 2 * n * len(grp) <= len(free):
            n *= 2
        for j, p in enumerate(grp):
            out[p] = free[j * n:(j + 1) * n]
            taken = taken + out[p]
    return out


def make_ops(g, core, T, topo, est=EST):
    CY, GA, GT, FIX, PEC, DL = (est[k] for k in ("cy", "ga", "gt", "fix", "pe", "dma"))
    rank = T.rank_of(core)
    cores = list(T.cores)
    ops = []
    acc = {}
    banks = {}
    cnt = {"d": 0, "r": 0}

    def add(name, alts, r=(), w=(), bank=(), extra=(), kind="c", lat=0.0, sem=None, inc=1):
        i = len(ops)
        hard = set(extra)
        for (k, a, b) in r:
            for e in acc.get(k, []):
                if e[3] and e[0] < b and a < e[1]:
                    hard.add(e[2])
        for (k, a, b) in w:
            if kind != "arr":
                for e in acc.get(k, []):
                    if e[0] < b and a < e[1]:
                        hard.add(e[2])
            acc[k] = [e for e in acc.get(k, []) if not (a <= e[0] and e[1] <= b)] + [[a, b, i, True]]
        for (k, a, b) in r:
            acc.setdefault(k, []).append([a, b, i, False])
        hard.discard(i)
        ops.append({"name": name, "alts": alts, "hard": hard, "bank": list(bank), "kind": kind, "move": 0.0, "lat": lat * DL, "sem": sem, "inc": inc})
        return i

    def vop(name, n, f, r, w, bank=(), mul=1.0, extra=()):
        return add(name, {"V": (FIX + max(64, n * mul) * CY, f)}, r, w, bank, extra)

    def aop(name, n, f, r, w, bank=(), mul=1.0):
        return add(name, {"A": (FIX + 0.02 + max(64, n * mul) * CY, f)}, r, w, bank)

    def flex(name, n, fv, fa, r, w, bank=(), mul=1.0, who="VA"):
        alts = {}
        if who != "V!":
            alts["A"] = (FIX + 0.02 + max(64, n * mul) * CY, fa)
        if who != "A!":
            alts["V"] = (FIX + max(64, n * mul) * CY, fv)
        i = add(name, alts, r, w, bank)
        ops[i]["first"] = who[0] if who != "VA" else None
        return i

    def pop(name, mms, r, w, bank, f32=False):
        def f(q):
            last = None
            for j, (o, l, x) in enumerate(mms):
                last = q.matmul(o, l, x, j == 0, j == len(mms) - 1)
            return [last]
        cost = sum(max(64, x.shape[-1]) for (o, l, x) in mms) * PEC * (4 if f32 is True else f32 or 1) + 0.1
        return add(name, {"P": (cost, f)}, r, w, bank)

    def gop(name, n, f, r, w):
        return add(name, {"G": (0.15 + 2 * n * CY, f)}, r, w)

    def gcopy(name, o, x, r, w):
        return gop(name, KW, lambda q: [q.affine_select(o, x, [[0, KW]], ALU.is_ge, 0.0, 0, 0)], r, w)

    def dma(name, eng, pairs, r, w, kb, extra=(), **kw):
        s = "d%d" % cnt["d"]
        cnt["d"] += 1
        f = lambda q: [q.dma_start(o, x, **kw) for (o, x) in pairs]
        iss = (1.0 if eng == "G" else 0.12) * len(pairs)
        i = add(name, {eng: (iss, f)}, r, w, (), extra, "dma", 2.2, s, 16 * len(pairs))
        ops[i]["move"] = kb * est["kb"]
        return i

    peers = [cores[(rank + d) % N] for d in range(1, N)]
    mine = engine_split(core, peers, topo)
    arrive = sum(len(engine_split(c, [x for x in cores if x != c], topo)[core]) for c in cores if c != core)
    sent = [0]

    def send(name, dr, blks, dst, c0, extra=()):
        s = "r%d" % cnt["r"]
        cnt["r"] += 1

        def f(q):
            trs = []
            for d in range(1, N):
                p = cores[(rank + d) % N]
                rid, pid, se = topo.addr(p)
                srcs = [T[dr][k * ROWS + 16 * SHIFT[d]:k * ROWS + 16 * SHIFT[d] + 128, :] for k in blks]
                trs.append(RemoteDMATransfer(dst_ids=[DstId(rid=rid, pnc=pid)], dma_engine_mask=sum(1 << e for e in mine[p]), remote_sem=T.sem[s],
                                             srcs=srcs, dsts=[T[dst][:, c0 + (d - 1) * NB:c0 + d * NB]], alu_op=len(blks) - 1))
            q.remote_dma_fused(trs, local_sem=T.sem.sent)
            return []
        sent[0] += sum(len(e) for e in mine.values())
        i = add(name, {"G": (1.0 if cnt["r"] > 1 else 3.0, f)}, [(dr, k, k + 1) for k in blks], (), (), extra, "rem")
        ops[i]["move"] = 3.0 * est["kb"]
        return add(name + "a", {}, (), [(dst, c0, c0 + (N - 1) * NB)], (), [i], "arr", 3.0, s, arrive)

    def stage(name, dr, blk, src, r, eng="S"):
        r0 = blk * ROWS
        return dma(name, eng, [(T[dr][r0:r0 + 128, :], src[:, 0:NB]), (T[dr][r0 + 128:r0 + ROWS, :], src[0:ROWS - 128, 0:NB])],
                   r, [(dr, blk, blk + 1)], 1.75 if dr == "DF" else 0.9)

    def ts(o, x, s1, s2, o0, o1=None):
        if o1 is None:
            return lambda q: [q.tensor_scalar(o, x, s1, None, o0)]
        return lambda q: [q.tensor_scalar(o, x, s1, s2, o0, o1)]

    def tt(o, x, y, o0):
        return lambda q: [q.tensor_tensor(o, x, y, o0)]

    def cp(o, x):
        return lambda q: [q.tensor_copy(o, x)]

    def act(o, x, fn, bias=0.0, scale=1.0):
        return lambda q: [q.activation(o, x, fn, bias=bias, scale=scale)]

    def ms(o, c):
        return lambda q: [q.memset(o, c)]

    def step_at(name, o, x, thr, r, w, bank, who="VA"):
        return flex(name, KW, ts(o, x, thr, None, ALU.is_ge), act(o, x, AF.Sigmoid, -STEEP * thr, STEEP), r + [("IB", 4, 5)], w, bank, who=who)

    def slot(nm, j, L):
        return T[nm][:, j::L]

    def mask(t, j, nm="A0"):
        n, s0 = (LA, (t - 2) * LA) if nm == "A0" else (LB, 0)
        return T[nm][:, s0 * KW + j:(s0 + n) * KW:n], (nm, s0 + j, s0 + j + 1)

    def scan(name, t, nm, d1, out):
        n, s0 = (LA, (t - 2) * LA) if nm == "A0" else (LB, 0)
        vop(name, KW * n, lambda q: [q.tensor_tensor_scan(T.Y[:, out:out + KW * n], T[nm][:, s0 * KW:(s0 + n) * KW], T[d1][:, :], 0.0, ALU.mult, ALU.add)],
            [(nm, s0, s0 + n), (d1, 0, n)], [("Y", out, out + KW * n)])
        return T.Y[:, out + n - 1:out + KW * n:n], ("Y", out, out + KW * n)

    def lst(j, a=0, b=KW):
        return T.LST[:, j * KW + a:j * KW + b]

    def lr(j, a=0, b=KW):
        return ("LST", j * KW + a, j * KW + b)

    def it(j, a=0, b=KW):
        return T.IT[:, j * KW + a:j * KW + b]

    def ir(j, a=0, b=KW):
        return ("IT", j * KW + a, j * KW + b)

    YO = OFF[RO]

    def ft(j):
        return T.FT[:, :] if j == 3 else T.Y[:, YO + (11 + j) * KW:YO + (12 + j) * KW]

    def fr(j):
        return ("FT", 0, KW) if j == 3 else ("Y", YO + (11 + j) * KW, YO + (12 + j) * KW)

    def wrap(name, z, src, c0, c1, out, k0, more=(), morer=()):
        n = (c1 - c0) // 16
        o = T[out][:, k0:k0 + n]
        mms = [(o, T[z][:, 15 - i:143 - i], T[src][:, c0 + i:c1:16]) for i in range(16)]
        mms += [(o, l, T[x][:, c0 // 16:c1 // 16]) for (l, x) in more]
        return pop(name, mms, [(z, 0, 1), (src, c0, c1)] + list(morer), [(out, k0, k0 + n)], [out])

    L_CS, L_A0, L_B0, L_D, L_F, L_R, L_YB, L_CT = 0, 2, 3, 1, 0, 8, 9, 7
    L_A = {1: 2, 2: 2, 3: 5, 4: 6, 5: 5, 6: 6}
    L_B = {2: 3, 3: 4, 4: 3, 5: 4, 6: 3}
    L_Y = {1: 2, 2: 2, 3: 7, 4: 8, 5: 7}
    SW = ["SA", "SB"]
    KB = ["K0", "K1", "K2"]
    C3 = [(0, 1024), (1024, 2048), (2048, 3072)]
    C2 = [(0, 1536), (1536, 3072)]
    CG = [(0, 256), (256, 1536), (1536, 3072)]
    IDN, I240, I16, WT, IH, INEG, IBIG = (T.IB[:, 128 * j:128 * j + 128] for j in range(7))

    for h, eng in ((0, "S"), (1, "A")):
        dma("cur%d" % h, eng, [(T.CT[0:96, gg, :], T.cur[gg:gg + 1, :]) for gg in range(4 * h, 4 * h + 4)], (), [("CT", h, h + 1)], 0.5)
    for c, (a, b) in enumerate(C3):
        dma("pt%d" % c, "S", [(T.PT[:, a:b], T.pt[:, a:b])], (), [("PT", a, b)], 4)
    stage("st0", "DH", 0, T.s0, (), "A")
    for a, b in C2:
        dma("s0", "S", [(T.SD[:, a:b], T.s0[:, a:b])], (), [("SD", a, b)], 3)
    send("x0", "DH", [0], "SD", V)

    gop("i0", 16, lambda q: [q.iota(T.RI[:, 0:16], [[-1, 16]], 128, 1)], (), [("RI", 0, 16)])
    gop("i1", 8, lambda q: [q.iota(T.RI[:, 32:40], [[-16, 8]], 0, 1)], (), [("RI", 32, 40)])
    II = T.IT[:, 5 * KW:5 * KW + 128]
    gop("i2", 128, lambda q: [q.iota(II, [[1, 128]], 128, -1)], (), [ir(5)])
    gop("i3", KW, lambda q: [q.iota(T.VC[:, :], [[16, KW]], 0, 0, allow_small_or_imprecise_dtypes=True)], (), [("VC", 0, KW)])
    gop("i6", 48, lambda q: [q.iota(T.HI[:, KW:KD], [[16, KD - KW]], V, 0, allow_small_or_imprecise_dtypes=True)], (), [("HI", KW, KD)])

    def fill(name, o, c, w):
        n = o.shape[1]
        gop(name, n, lambda q: [q.iota(o, [[0, n]], c, 0, allow_small_or_imprecise_dtypes=True)], (), w)

    vop("k0", 128, ts(IDN, II, 128.0, None, ALU.is_equal), [ir(5)], [("IB", 0, 1)])
    aop("k0h", 128, act(IH, IDN, AF.Sigmoid, -STEEP, STEEP), [("IB", 0, 1)], [("IB", 4, 5)], mul=12)
    for nm, o, c, w in (("k0f", T.IF[:, :], 1.0, ("IF", 0, 1)), ("k19", I240, float(KD), ("IB", 1, 2)), ("k20", I16, 0.0625, ("IB", 2, 3)),
                        ("k0n", INEG, -1.0, ("IB", 5, 6)), ("k0b", IBIG, BIG, ("IB", 6, 7))):
        gop(nm, 128, lambda q, o=o, c=c: [q.affine_select(o, IDN, [[-1, 128]], ALU.not_equal, c, 0, 1)], [("IB", 0, 1)], [w])
    fill("k0o", T.ONE[0:1, 0:512], 1, [("ONE", 0, 1)])
    vop("k0p", 128, ms(T.ONE[0:1, 512:640], -0.5), (), [("ONE", 1, 2)], mul=0.5)
    vop("k1", 16, ts(T.RI[:, 16:32], T.RI[:, 0:16], 15, None, ALU.bitwise_and), [("RI", 0, 16)], [("RI", 16, 32)])
    RR, rr = T.RI[:, 16:32], ("RI", 16, 32)
    vop("k2", 16, ts(T.MW[:, 0:16], RR, 0.0, None, ALU.is_equal), [rr], [("MW", 0, 16)])
    vop("k3", 72, ms(T.ZB[:, :], 0.0), (), [("ZB", 0, 1)])
    vop("k4", 8, ts(T.RI[:, 40:48], T.RI[:, 32:40], 4, None, ALU.arith_shift_right), [("RI", 32, 40)], [("RI", 40, 48)])
    vop("k5", 8, ts(T.GS[:, 0:8], T.RI[:, 40:48], 0.0, None, ALU.is_equal), [("RI", 40, 48)], [("GS", 0, 8)])
    R2, r2 = T.IT[:, 4 * KW:4 * KW + 128], ir(4)
    w0, w1, w2 = (T.U[:, 128 * j:128 * j + 128] for j in range(3))
    vop("k6a", 128, ts(R2, II, 15, None, ALU.bitwise_and), [ir(5)], [r2])
    vop("k6", 128, ts(w0, R2, 1.0, None, ALU.is_ge), [r2], [("U", 0, 128)])
    vop("k7", 128, ts(w1, R2, 3.0, 4095.0, ALU.is_ge, ALU.mult), [r2], [("U", 128, 256)])
    vop("k8", 128, ts(w2, R2, 5.0, -4096.0, ALU.is_ge, ALU.mult), [r2], [("U", 256, 384)])
    vop("k9", 128, tt(w1, w1, w2, ALU.add), [("U", 128, 384)], [("U", 128, 256)], mul=2)
    vop("k10", 128, tt(w0, w0, w1, ALU.add), [("U", 0, 256)], [("U", 0, 128)], mul=2)
    gop("i4", 128, lambda q: [q.affine_select(w1, w0, [[-16, 8], [0, 16]], ALU.is_ge, 0.0, 0, 1)], [("U", 0, 128)], [("U", 128, 256)])
    gop("i5", 128, lambda q: [q.affine_select(WT, w1, [[16, 8], [0, 16]], ALU.is_ge, 0.0, 15, -1)], [("U", 128, 256)], [("IB", 3, 4)])
    E = T.RI[:, 16:17]
    vop("k11", 1, ts(T.RI[:, 48:49], E, 1, None, ALU.bitwise_and), [rr], [("RI", 48, 49)])
    vop("k12", 1, ts(T.RI[:, 49:50], E, 11, None, ALU.bitwise_and), [rr], [("RI", 49, 50)])
    vop("k13", 1, cp(T.COL[:, 0:1], T.RI[:, 48:49]), [("RI", 48, 49)], [("COL", 0, 1)])
    vop("k14", 1, ts(T.COL[:, 1:2], T.RI[:, 48:49], -2.0, 1.0, ALU.mult, ALU.add), [("RI", 48, 49)], [("COL", 1, 2)])
    for j in range(2):
        aop("kG%d" % j, 8, act(T.GS[:, 8 + 8 * j:16 + 8 * j], T.GS[:, 0:8], AF.Identity, 0.0, T.COL[:, j:j + 1]), [("GS", 0, 8), ("COL", j, j + 1)], [("GS", 8 + 8 * j, 16 + 8 * j)])
    vop("k15", 1, ts(T.COL[:, 2:3], T.RI[:, 49:50], 0.0, None, ALU.is_equal), [("RI", 49, 50)], [("COL", 2, 3)])
    vop("k16", 1, ts(T.COL[:, 3:4], E, 8.0, -1.0, ALU.is_equal, ALU.mult), [rr], [("COL", 3, 4)])
    vop("k17", 1, cp(T.COL[:, 4:5], E), [rr], [("COL", 4, 5)])
    vop("k18", 1, ts(T.COL[:, 5:6], E, 7.5, None, ALU.subtract), [rr], [("COL", 5, 6)])
    vop("kZB", 8, cp(T.ZB[:, 15:143:16], T.GS[:, 0:8]), [("GS", 0, 8)], [("ZB", 0, 1)])
    for nm, j in (("ZV", 2), ("ZY", 3)):
        aop("k" + nm, 144, act(T[nm][:, :], T.ZB[:, :], AF.Identity, 0.0, T.COL[:, j:j + 1]), [("ZB", 0, 1), ("COL", j, j + 1)], [(nm, 0, 1)])
    aop("k22", 48, act(T.LO[:, KW:KD], T.HI[:, KW:KD], AF.Identity, T.COL[:, 5:6], 0.0), [("HI", KW, KD), ("COL", 5, 6)], [("LO", KW, KD)])
    fill("k28", T.HT[:, 0:KW], 5, [("HT", 0, 1)])
    for t in range(2, RO):
        fill("k24", T.A0[:, (t - 2) * KW * LA:(t - 1) * KW * LA], 0, [("A0", (t - 2) * LA, (t - 1) * LA)])
    fill("k25", T.B0[:, :], 0, [("B0", 0, LB)])
    fill("k26", T.AGE[:, :], 0, [("AGE", 0, KD)])

    for b in range(2):
        vop("cb%d" % b, 128, cp(T.CB[0:96, 128 * b:128 * b + 128], T.CT[0:96, :, 16 * b:16 * b + 16]), [("CT", 0, 2)], [("CB", b, b + 1)])
        pop("cm%d" % b, [(T.PN[:, 96 * b:96 * b + 96], T.CB[0:96, 128 * b:128 * b + 128], T.IB[0:96, 0:96])],
            [("CB", b, b + 1), ("IB", 0, 1)], [("PN", 96 * b, 96 * b + 96)], ["PN"])
    for b in range(2):
        vop("cw%d" % b, 96, cp(T.IT[:, b:KW:2], T.PN[:, 96 * b:96 * b + 96]), [("PN", 96 * b, 96 * b + 96)], [("ITc", b, b + 1)], ["PN"])
    CS, CT2 = T.CI[:, 0:KW], T.CI[:, KW:2 * KW]
    vop("cs", KW, ts(CS, it(0), 15, None, ALU.bitwise_and), [("ITc", 0, 2), ir(0)], [("CI", 0, 1)])
    vop("csl", KW, cp(lst(L_CS), CS), [("CI", 0, 1)], [lr(L_CS)])
    vop("ct", KW, ts(CT2, it(0), 4, None, ALU.logical_shift_right), [("ITc", 0, 2), ir(0)], [("CI", 1, 2)])
    vop("ctl", KW, cp(lst(L_CT), CT2), [("CI", 1, 2)], [lr(L_CT)])

    ychunk = [0]
    gchunk = [0]
    held = {}

    def weigh(nm, l, lk, hot, a, b, src, y0):
        u = ychunk[0] % 2
        ychunk[0] += 1
        n = b - a
        for h in range(0, n, 512):
            pop(nm + "m", [(T.PS[:, 1024 * u + h:1024 * u + h + 512], l, T[hot][:, a + h:a + h + 512])], [lk, (hot, a + h, a + h + 512)],
                [("PS", 1024 * u + h, 1024 * u + h + 512)], ["PS%d" % (2 * u + h // 512)])
        vop(nm + "p", n, tt(T.Y[:, y0 + a:y0 + b], T.PS[:, 1024 * u:1024 * u + n], T[src][:, a:b], ALU.mult), [("PS", 1024 * u, 1024 * u + n), (src, a, b)],
            [("Y", y0 + a, y0 + b)], ["PS%d" % (2 * u + h // 512) for h in range(0, n, 512)])

    def onehot(nm, li, hot, a, b):
        src = T.MW[:, 0:16].indirect(lst(li, a // 16, b // 16))
        flex(nm, b - a, cp(T[hot][:, a:b], src), act(T[hot][:, a:b], src, AF.Identity), [("MW", 0, 16), lr(li), ("IB", 4, 5)], [(hot, a, b)], mul=GA, who="A")

    def fold(nm, y0, g0, nc, ps, p0, tmp, halves=(0, 1)):
        w = 128 * nc
        for b in halves:
            c0 = y0 + 1536 * b
            for h in range(0, 16, 4):
                mm = [(T[ps][0:96, p0 + w * b + i:p0 + w * b + w:16], T.Y[:, c0 + i:c0 + 1536:16], T.GS[:, g0:g0 + 8 * nc]) for i in range(h, h + 4)]
                add("%sf%d" % (nm, b), {"P": (4 * 256 * PEC + 0.1, lambda q, mm=mm: [q.matmul(o, l, x, True, True) for (o, l, x) in mm])},
                    [("GS", 0, 24), ("Y", c0, c0 + 1536)], [(ps + "f", 16 * b + h, 16 * b + h + 4), (ps, p0 + w * b, p0 + w * b + w)] if h == 0 else [(ps + "f", 16 * b + h, 16 * b + h + 4)], [ps])
            o, x = T.Y[0:96, tmp + w * b:tmp + w * b + w], T[ps][0:96, p0 + w * b:p0 + w * b + w]
            flex("%sc%d" % (nm, b), w, cp(o, x), act(o, x, AF.Identity), [(ps + "f", 16 * b, 16 * b + 16), (ps, p0 + w * b, p0 + w * b + w)],
                 [("Y", tmp + w * b, tmp + w * b + w)], [ps], who="A")
        for b in halves:
            for cl in range(nc):
                t0, o0 = tmp + w * b + 128 * cl, KW * cl + 96 * b
                pop("%st%d" % (nm, b), [(T[ps][:, o0:o0 + 96], T.Y[0:96, t0:t0 + 128], T.IF[0:96, 0:96])], [("Y", t0, t0 + 128), ("IF", 0, 1)],
                    [(ps, o0, o0 + 96)], [ps], True)

    for c, (a, b) in enumerate(C3):
        vop("Ss%d" % c, 1024, ts(T.PT[:, a:b], T.PT[:, a:b], 4095, None, ALU.bitwise_and), [("PT", a, b)], [("PT", a, b)])
    for c, (a, b) in enumerate([(0, 1024), (1024, 1536), (1536, 2048), (2048, 3072)]):
        onehot("oh%d" % c, L_CS, "HB", a, b)
        if TUNE["direct"][c] == "V":
            vop("a%dp" % c, b - a, tt(T.Y[:, OFF[2] + a:OFF[2] + b], T.MW[:, 0:16].indirect(lst(L_CS, a // 16, b // 16)), T.PT[:, a:b], ALU.mult),
                [("MW", 0, 16), lr(L_CS), ("PT", a, b)], [("Y", OFF[2] + a, OFF[2] + b)], mul=GT)
        else:
            weigh("a%d" % c, IDN, ("IB", 0, 1), "HB", a, b, "PT", OFF[2])
        if b % 1536 == 0:
            h = b // 1536 - 1
            k0, k1, ps = 96 * h, 96 * h + 96, ("PZ", "PW")[h]
            fold("a", OFF[2], 0, 1, ps, 256, YO, [h])
            vop("a0l", 96, cp(lst(L_A0, k0, k1), T[ps][:, k0:k1]), [(ps, k0, k1)], [lr(L_A0, k0, k1)], [ps])
            o = T.A1[:, k0 * LA + 5:k1 * LA:LA]
            flex("a0s", 96, ts(o, T[ps][:, k0:k1], 7.5, None, ALU.subtract), act(o, T[ps][:, k0:k1], AF.Identity, -7.5), [(ps, k0, k1)], [("A1", 5, 6)], [ps], who="A")

    for a, b in C2:
        aop("abs0", b - a, act(T.K0[:, a:b], T.SD[:, a:b], AF.Abs), [("SD", a, b)], [("K0", a, b)])
        dma("so0", "S", [(T.WG[:, a:b], T.K0[:, a:b])], [("K0", a, b)], [("WG", a, b)], 3)
    aop("abs1", W - V, act(T.K0[:, V:W], T.SD[:, V:W], AF.Abs), [("SD", V, W)], [("K0", V, W)])
    for c, (a, b) in enumerate(CG):
        aop("sg0_%d" % c, b - a, act(T.K1[:, a:b], T.SD[:, a:b], AF.Sign, -2.0 ** -30, -1.0), [("SD", a, b)], [("K1", a, b)])
    stage("stc0", "DH", 1, T.K1, [("K1", 0, NB)])

    def trigger0():
        for c, (a, b) in enumerate(C3):
            dma("pr%d" % c, "S", [(T.PT[:, a:b], T.pt[:, a:b])], (), [("PT", a, b)], 4)
            vop("Ts%d" % c, 1024, ts(T.PT[:, a:b], T.PT[:, a:b], 12, None, ALU.logical_shift_right), [("PT", a, b)], [("PT", a, b)])
            onehot("bh%d" % c, L_CT, "HB", a, b)
            weigh("b%d" % c, IDN, ("IB", 0, 1), "HB", a, b, "PT", OFF[5])
        fold("b", OFF[5], 0, 1, "PW", 256, YO + 512)
        vop("b0l", KW, cp(lst(L_B0), T.PW[:, 0:KW]), [("PW", 0, KW)], [lr(L_B0)], ["PW"])
        flex("b0s", KW, cp(slot("B1", 4, LB), T.PW[:, 0:KW]), act(slot("B1", 4, LB), T.PW[:, 0:KW], AF.Identity), [("PW", 0, KW)], [("B1", 4, 5)], ["PW"], who="A")

    def tables(nm):
        y0, cur, ck = (OFF[3], CS, 0) if nm == "S" else (OFF[4], CT2, 1)
        for c, (a, b) in enumerate(C3):
            weigh("%s%d" % (nm, c), WT, ("IB", 3, 4), "HB", a, b, "PT", y0)
        fold(nm, y0, 8, 2, "PX", 0, YO + 768 + 512 * ck)
        P1, P2 = T.PX[:, 0:KW], T.PX[:, KW:2 * KW]
        p1, p2 = ("PX", 0, KW), ("PX", KW, 2 * KW)
        vop(nm + "par", KW, ts(it(0), cur, 1, None, ALU.bitwise_and), [("CI", ck, ck + 1)], [ir(0)])
        vop(nm + "md", KW, tt(ft(0), P2, it(0), ALU.mult), [p2, ir(0)], [fr(0)], ["PX"])
        vop(nm + "x13", KW, tt(it(1), P1, ft(0), ALU.add), [p1, fr(0)], [ir(1)], ["PX"])
        vop(nm + "xd", KW, tt(ft(1), P2, ft(0), ALU.subtract), [p2, fr(0)], [fr(1)], ["PX"])
        vop(nm + "x24", KW, tt(it(2), P1, ft(1), ALU.add), [p1, fr(1)], [ir(2)], ["PX"])
        vop(nm + "lo", 2 * KW, ts(T.IT[:, 3 * KW:5 * KW], T.IT[:, KW:3 * KW], 4095, None, ALU.bitwise_and), [ir(1), ir(2)], [ir(3), ir(4)])
        vop(nm + "hi", 2 * KW, ts(T.IT[:, KW:3 * KW], T.IT[:, KW:3 * KW], 12, None, ALU.logical_shift_right), [ir(1), ir(2)], [ir(1), ir(2)])
        e1, e2, e3, e4 = 3, 4, 1, 2
        D1, L = ("A1", LA) if nm == "S" else ("B1", LB)
        if nm == "S":
            vop("Sd1", KW, ts(ft(2), it(e1), 7.5, None, ALU.subtract), [ir(e1)], [fr(2)])
        else:
            vop("Td1", KW, tt(slot(D1, 3, L), it(e1), slot(D1, 4, L), ALU.subtract), [ir(e1), (D1, 4, 5)], [(D1, 3, 4)], mul=2)
        for j, (u, v) in enumerate(((e4, e3), (e3, e2), (e2, e1))):
            vop(nm + "d%d" % (4 - j), KW, tt(slot(D1, j, L), it(u), it(v), ALU.subtract), [ir(u), ir(v)], [(D1, j, j + 1)], mul=2)

    carr = {}
    g1s = {}
    alpha = [slot("A1", 5, LA), ("A1", 5, 6)]

    def lookup(t):
        al, ar = alpha
        vop("hi%d" % t, KW, ts(T.HI[:, 0:KW], al, MAGIC, MAGIC, ALU.add, ALU.subtract), [ar], [("HI", 0, KW)])
        if TUNE["lo"] == "V":
            vop("lo%d" % t, KW, tt(T.LO[:, 0:KW], al, T.HI[:, 0:KW], ALU.subtract), [ar, ("HI", 0, KW)], [("LO", 0, KW)], mul=2)
        else:
            pop("lp%d" % t, [(T.PN[:, 0:KW], T.IF[:, :], al), (T.PN[:, 0:KW], INEG, T.HI[:, 0:KW])], [ar, ("HI", 0, KW), ("IF", 0, 1), ("IB", 5, 6)], [("PN", 0, KW)], ["PN"], 2.5)
            flex("lo%d" % t, KW, cp(T.LO[:, 0:KW], T.PN[:, 0:KW]), act(T.LO[:, 0:KW], T.PN[:, 0:KW], AF.Identity), [("PN", 0, KW)], [("LO", 0, KW)], ["PN"])
        al, ar = slot("A1", 5, LA), ("A1", 5, 6)
        pop("dl%d" % t, [(T.PN[:, 0:KW], I240, T.LO[:, 0:KW]), (T.PN[:, 0:KW], I16, T.HI[:, 0:KW])],
            [("IB", 1, 3), ("LO", 0, KW), ("HI", 0, KW)], [("PN", 0, KW)], ["PN"])
        vop("dll%d" % t, KW, ts(lst(L_D), T.PN[:, 0:KW], 7.5 * KD, None, ALU.add), [("PN", 0, KW)], [lr(L_D)], ["PN"])
        pairs = [(T.SD[0::16, :], T.HI[:, :]), (T.SD[4::16, :], T.LO[:, :])]
        rd = [("HI", 0, KD), ("LO", 0, KD)]
        if t > 2:
            pairs += [(T.SD[8::16, :], T.AGE[:, :])]
            rd += [("AGE", 0, KD)]
        dma("D%d" % t, "S", pairs, rd, [("SD", 0, W)], 3)
        for c, (a, b) in enumerate(C2):
            src = T.SD[:, :].indirect(lst(L_D, a // 16, b // 16))
            flex("gw%d_%d" % (t, c), b - a, cp(T.WG[:, a:b], src), act(T.WG[:, a:b], src, AF.Identity),
                 [("SD", 0, W), lr(L_D)], [("WG", a, b)], mul=GA, who="A")
            wrap("via%d_%d" % (t, c), "ZV", "WG", a, b, "PW", a // 16)
            if t > 2:
                wrap("yo%d_%d" % (t, c), "ZY", "WG", a, b, "PW", KW + a // 16, [(IDN, "HI"), (IDN, "LO")], [("IB", 0, 1), ("HI", 0, KW), ("LO", 0, KW)])
        vop("sv%d" % t, KW, tt(slot("A1", 3, LA), ft(2), T.PW[:, 0:KW], ALU.subtract), [fr(2), ("PW", 0, KW)], [("A1", 3, 4)], ["PW"])
        vop("dv%d" % t, KW, tt(slot("A1", 4, LA), T.PW[:, 0:KW], al, ALU.subtract), [ar, ("PW", 0, KW)], [("A1", 4, 5)], ["PW"])
        if t > 2:
            vop("yl%d" % t, KW, ts(lst(L_Y[t]), T.PW[:, KW:2 * KW], 7.5 + OFF[t - 1], None, ALU.add), [("PW", KW, 2 * KW)], [lr(L_Y[t])], ["PW"])

    def product(t):
        sw, nw, y0 = SW[(t - 1) % 2], SW[t % 2], OFF[t]
        sw, so = (sw, "SO") if t > 1 else ("K0", "WG")
        k1 = KB[(t + 1) % 3]
        sgn = 1.0 if t % 2 else -1.0
        g1 = []
        for c, (a, b) in enumerate(CG if t < RO else C3):
            P, pr = T.Y[:, y0 + a:y0 + b], ("Y", y0 + a, y0 + b)
            g1.append(vop("g1%d_%d" % (t, c), b - a, tt(P, T[sw][:, :].indirect(lst(L_A[t], a // 16, b // 16)), T[so][:, a:b], ALU.mult),
                          [(sw, 0, W), (so, a, b), lr(L_A[t], a // 16, b // 16)], [pr], mul=GT))
            if t == RO:
                continue
            aop("ab%d_%d" % (t, c), b - a, act(T[nw][:, a:b], P, AF.Abs, 1.0, -2.0), [pr], [(nw, a, b)])
            if c:
                a0 = a if c > 1 else 0
                dma("so%d_%d" % (t, c), "S", [(T.SO[:, a0:b], T[nw][:, a0:b])], [(nw, a0, b)], [("SO", a0, b)], 6)
            aop("sg%d_%d" % (t, c), b - a, act(T[k1][:, a:b], P, AF.Sign, sgn * (0.875 + 2.0 ** -24), -1.75 * sgn), [pr], [(k1, a, b)])
            if c == 0:
                stage("sts%d" % t, "DF", t - 1, T[nw], [(nw, 0, NB)])
                send("xs%d" % t, "DF", [t - 1], nw, V, [carr[t - 1]] if t > 1 else [])
                stage("stc%d" % t, "DH", t + 1, T[k1], [(k1, 0, NB)])
        g1s[t] = g1

    def crossings(t):
        k0, k1 = KB[t % 3], KB[(t + 1) % 3]
        carr[t] = send("xc%d" % t, "DH", [t, t + 1], k0, V, g1s[t] + held.get(t, []) + ([carr[t - 1]] if t > 1 else []))
        dma("ca%d" % t, "G", [(T[k0][:, 0:V], T[k1][:, 0:V])], [(k0, 0, V), (k1, 0, V)], [(k0, 0, V)], 12, accum_op=ALU.add, max_dma_last_dim=V)

    def sums(t):
        cw, k0 = KB[(t - 1) % 3], KB[t % 3]
        for c, (a, b) in enumerate(C3):
            u = (a + 1024 * t) % 2048
            src, o, tr = T[cw][:, :].indirect(lst(L_B[t], a // 16, b // 16)), T.TT[:, u:u + 1024], ("TT", u, u + 1024)
            vop("gc%d_%d" % (t, c), b - a, tt(o, src, T[k0][:, a:b], ALU.mult), [(cw, 0, W), lr(L_B[t]), (k0, a, b)], [tr], mul=GT)
            wrap("z%d_%d" % (t, c), "ZB", "TT", u, u + 1024, "PZ", a // 16)

    def places(name, t, li, n, ps):
        pop(name + "p", [(T[ps][:, 0:n], INEG, T.AGE[:, 0:n]), (T[ps][:, 0:n], IDN, T.VC[:, 0:n])],
            [("IB", 0, 1), ("IB", 5, 6), ("AGE", 0, KW), ("VC", 0, KW)], [(ps, 0, n)], [ps])
        vop(name, n, ts(lst(li, 0, n), T[ps][:, 0:n], T.COL[:, 4:5], float(OFF[t]), ALU.add, ALU.add), [(ps, 0, n), ("COL", 4, 5)], [lr(li, 0, n)], [ps])

    def turn(t):
        Z, z = T.PZ[:, 0:KW], ("PZ", 0, KW)
        j = t - 1
        ht = T.HT[:, j * KW:(j + 1) * KW]
        if t < RO:
            step_at("g4%d" % t, mask(t, 5)[0], Z, 3.0, [z], [mask(t, 5)[1]], ["PZ"])
            step_at("adv%d" % t, mask(t, 4)[0], Z, 7.0, [z], [mask(t, 4)[1]], ["PZ"])
        else:
            step_at("adv%d" % t, T.HS[:, :], Z, 7.0, [z], [("HS", 0, 1)], ["PZ"], "V!")
        aop("ht%d" % t, KW, act(ht, Z, AF.Sign, -5.0, -1.0), [z], [("HT", j, j + 1)], ["PZ"])
        if t == 2:
            aop("mt%d" % t, KW, act(mask(t, 4, "B0")[0], ht, AF.Relu), [("HT", j, j + 1)], [mask(t, 4, "B0")[1]])
        G = T.PZ[:, KW:2 * KW]
        pop("ag%d" % t, [(G, IDN, T.AGE[:, 0:KW]), (G, IBIG, ht)], [("IB", 0, 1), ("IB", 6, 7), ("AGE", 0, KW), ("HT", j, j + 1)], [("PZ", KW, 2 * KW)], ["PZ"])
        c = float(OFF[t] - OFF[t - 1]) - BIG
        flex("age%d" % t, KW, ts(T.AGE[:, 0:KW], G, c, 0.0, ALU.add, ALU.max), act(T.AGE[:, 0:KW], G, AF.Relu, c), [("PZ", KW, 2 * KW)], [("AGE", 0, KW)], ["PZ"])
        if t < RO:
            na, nr = scan("sa%d" % t, t, "A0", "A1", YO)
            vop("al%d" % t, KW, ts(lst(L_A[t + 1]), na, 7.5, None, ALU.add), [nr], [lr(L_A[t + 1])])
            if t < RO - 1:
                gcopy("as%d" % t, slot("A1", 5, LA), na, [nr], [("A1", 5, 6)])
            alpha[0], alpha[1] = na, nr
            if t > 2:
                pop("nt%d" % t, [(T.PN[:, KW:2 * KW], IDN, T.HT[:, u * KW:(u + 1) * KW]) for u in range(1, t)],
                    [("IB", 0, 1), ("HT", 1, t)], [("PN", KW, 2 * KW)], ["PN"])
                for m in range(1, t):
                    step_at("mt%d_%d" % (t, m), mask(t, LB - m, "B0")[0], T.PN[:, KW:2 * KW], float(2 * m - t),
                            [("PN", KW, 2 * KW)], [mask(t, LB - m, "B0")[1]], ["PN"], "A")
            nb, br = scan("sb%d" % t, t, "B0", "B1", YO + KW * LA)
            vop("bl%d" % t, KW, cp(lst(L_B[t + 1]), nb), [br], [lr(L_B[t + 1])])

    def counts(t):
        if t == 2:
            gcopy("ms2", mask(3, 3)[0], mask(2, 4)[0], [mask(2, 4)[1]], [mask(3, 3)[1]])
            return
        pop("ns%d" % t, [(T.PN[:, KW:2 * KW], IDN, mask(u, 4)[0]) for u in range(2, t + 1)],
            [("IB", 0, 1)] + [mask(u, 4)[1] for u in range(2, t + 1)], [("PN", KW, 2 * KW)], ["PN"])
        for m in range(1, t):
            step_at("ms%d_%d" % (t, m), mask(t + 1, 4 - m)[0], T.PN[:, KW:2 * KW], m - 0.5,
                    [("PN", KW, 2 * KW)], [mask(t + 1, 4 - m)[1]], ["PN"], "A")

    def ymul(t, c, a, b, src, fn, bias, scale, rd):
        y0, n, u = OFF[t], b - a, ychunk[0] % 2
        ychunk[0] += 1
        Uc, ur = T.U[:, 1024 * u:1024 * u + n], ("U", 1024 * u, 1024 * u + n)
        Sc, sr, bk = T.PS[:, 1024 * u:1024 * u + n], ("PS", 1024 * u, 1024 * u + n), ["PS%d" % (2 * u + h) for h in range(n // 512)]
        P, pr = T.Y[:, y0 + a:y0 + b], ("Y", y0 + a, y0 + b)
        aop("gy%d_%d" % (t, c), n, act(Uc, src, fn, bias, scale), rd, [ur], mul=GA)
        if t > 1 or TUNE["sp1"][c] == "P":
            for h in range(0, n, 512):
                o = T.PS[:, 1024 * u + h:1024 * u + h + 512]
                pop("sp%d" % t, [(o, T.ONE[0:1, 512:640], T.ONE[0:1, 0:512]), (o, T.IF[:, :], T.Y[:, y0 + a + h:y0 + a + h + 512])],
                    [("Y", y0 + a + h, y0 + a + h + 512), ("ONE", 0, 2), ("IF", 0, 1)], [("PS", 1024 * u + h, 1024 * u + h + 512)], [bk[h // 512]], 2.5)
        else:
            aop("sp%d" % t, n, act(Sc, P, AF.Identity, -0.5), [pr], [sr], bk)
        vop("x%d_%d" % (t, c), n, tt(P, Uc, Sc, ALU.mult), [ur, sr], [pr], bk)

    def ystep(t, cs=(0, 1, 2)):
        y0 = OFF[t]
        for c in cs:
            a, b = C3[c]
            li = lst(L_Y[t], a // 16, b // 16)
            if t == 1:
                ymul(t, c, a, b, T.SD[:, :].indirect(li), AF.Identity, 0.5, 0.5, [("SD", 0, W), lr(L_Y[t], a // 16, b // 16)])
            else:
                ymul(t, c, a, b, T.Y[:, 0:y0].indirect(li), AF.Sigmoid, 0.0, -8.0, [("Y", 0, y0), lr(L_Y[t]), ("IB", 4, 5)])
            if c == 0 and t < RO - 1:
                if t == 1:
                    stage("sty1", "DF", 5, T.Y, [("Y", 0, NB)])
                else:
                    places("yb%d" % t, t, L_YB, 16, "PX")
                    s2 = T.Y[:, 0:y0 + NB].indirect(lst(L_YB, 0, 16))
                    flex("yg%d" % t, NB, cp(T.YBUS[:, :], s2), act(T.YBUS[:, :], s2, AF.Identity), [("Y", 0, y0 + NB), lr(L_YB, 0, 16)],
                         [("YBUS", 0, 1)], mul=GA, who="A")
                    stage("sty%d" % t, "DF", 4 + t, T.YBUS, [("YBUS", 0, 1)])
                send("xy%d" % t, "DF", [4 + t], "Y", y0 + V, [carr[t]] if t > 1 else [])

    def resolve():
        places("rl", 5, L_R, KW, "PX")
        for c, (a, b) in enumerate([(0, NB), (NB, 1024), (1024, 2048), (2048, V)]):
            src = T.Y[:, 0:OFF[5] + b].indirect(lst(L_R, a // 16, b // 16))
            aop("rs_%d" % c, b - a, act(T.SA[:, a:b], src, AF.Sigmoid, 0.0, -8.0), [("Y", 0, OFF[5] + b), lr(L_R)], [("SA", a, b)], mul=GA)
            if c == 0:
                stage("sty5", "DF", 9, T.SA, [("SA", 0, NB)])
                send("xy5", "DF", [9], "SA", V, [carr[5]])

    def last():
        y0 = OFF[RO]
        places("fl", RO, L_F, KW, "PW")
        for c, (a, b) in enumerate(TUNE["cl"]):
            P, pr = T.Y[:, y0 + a:y0 + b], ("Y", y0 + a, y0 + b)
            src = T.SA[:, :].indirect(lst(L_A[RO], a // 16, b // 16))
            if TUNE["last"][c] == "V":
                flex("dh_%d" % c, b - a, ts(P, P, 0.5, None, ALU.subtract), act(P, P, AF.Identity, -0.5), [pr], [pr], who="A")
                vop("x6_%d" % c, b - a, tt(P, src, P, ALU.mult), [("SA", 0, W), lr(L_A[RO]), pr], [pr], mul=GT)
            else:
                ymul(RO, c, a, b, src, AF.Identity, 0.0, 1.0, [("SA", 0, W), lr(L_A[RO])])
            O, orr = T.SB[:, a:b], ("SB", a, b)
            aop("fg_%d" % c, b - a, act(O, T.Y[:, 0:y0 + b].indirect(lst(L_F, a // 16, b // 16)), AF.Tanh, 0.0, -4.0),
                [("Y", 0, y0 + b), lr(L_F)] + ([("tanh", 0, 1)] if c else []), [orr] + ([] if c else [("tanh", 0, 1)]), mul=GA + (0.0 if c else 1.7))
            dma("yo%d" % c, "S", [(T.y[:, a:b], O)], [orr], (), (b - a) / 256)

    def finish():
        pop("q0", [(T.PX[:, 0:KW], IDN, x) for x in [mask(u, 4)[0] for u in range(2, RO)] + [T.HS[:, :]]],
            [("IB", 0, 1), ("HS", 0, 1)] + [mask(u, 4)[1] for u in range(2, RO)], [("PX", 0, KW)], ["PX"])
        pop("q1", [(T.PX[:, KW:2 * KW], IH, T.HT[:, u * KW:(u + 1) * KW]) for u in range(6)],
            [("IB", 4, 5), ("HT", 0, 6)], [("PX", KW, 2 * KW)], ["PX"])
        vop("qi", 2 * KW, tt(T.IT[:, 0:2 * KW], T.PX[:, 0:2 * KW], T.CI[:, :], ALU.add), [("PX", 0, 2 * KW), ("CI", 0, 2)], [("IT", 0, 2 * KW)], ["PX"])
        vop("qm", 2 * KW, ts(T.IT[:, 2 * KW:4 * KW], T.IT[:, 0:2 * KW], 15, None, ALU.bitwise_and), [("IT", 0, 2 * KW)], [("IT", 2 * KW, 4 * KW)])
        vop("q16", KW, ts(ft(3), it(3), 16.0, None, ALU.mult), [ir(3)], [fr(3)])
        for b in range(2):
            vop("qa%d" % b, 96, tt(T.CB[:, 128 * b:128 * b + 96], T.IT[:, 2 * KW + b:3 * KW:2], T.FT[:, b:KW:2], ALU.add), [ir(2), fr(3)], [("CB", b, b + 1)], mul=2)
            pop("qt%d" % b, [(T.PX[0:96, 128 * b:128 * b + 128], T.CB[:, 128 * b:128 * b + 96], IDN)],
                [("CB", b, b + 1), ("IB", 0, 1)], [("PX", 128 * b, 128 * b + 128)], ["PX"])
        for b in range(2):
            vop("qc%d" % b, 128, cp(T.QT[0:96, :, 16 * b:16 * b + 16], T.PX[0:96, 128 * b:128 * b + 128]),
                [("PX", 128 * b, 128 * b + 128)], [("QT", b, b + 1)], ["PX"])
        dma("qo", "S", [(T.q[gg:gg + 1, :], T.QT[0:96, gg, :]) for gg in range(8)], [("QT", 0, 2)], (), 0.5)

    product(1)
    parts = {"c1": lambda: crossings(1), "tr": trigger0, "S": lambda: tables("S"), "T": lambda: tables("T"), "y1": lambda: ystep(1),
             "ya": lambda: ystep(1, [0]), "yb": lambda: ystep(1, [1, 2])}
    for nm in TUNE["setup"].split():
        parts[nm]()
    for t in range(2, RO):
        lookup(t)
        product(t)
        sums(t)
        crossings(t)
        turn(t)
        ystep(t)
        if t < RO - 1:
            counts(t)
    resolve()
    product(RO)
    sums(RO)
    turn(RO)
    last()
    finish()
    return ops, sent[0]


def place(ops, pri, back, eng):
    n = len(ops)
    succ = [[] for _ in range(n)]
    left = [0] * n
    for i, o in enumerate(ops):
        for d in o["hard"]:
            a, b = (i, d) if back else (d, i)
            succ[a].append(b)
            left[b] += 1
    line, lat = {}, EST["lat"]
    fin, beg, t0, eng = [0.0] * n, [0.0] * n, [0.0] * n, list(eng)
    ready = [i for i in range(n) if left[i] == 0]
    while ready:
        i = max(ready, key=lambda x: (pri[x], -x))
        ready.remove(i)
        o = ops[i]
        wait = o["lat"] + o["move"]
        beg[i], fin[i] = t0[i], t0[i] + wait
        best = None
        for e, (c, f) in o["alts"].items():
            if eng[i] in (None, e):
                t = t0[i] + (wait if back else 0.0)
                busy = line.get(e, [])
                if o["bank"]:
                    busy = sorted(busy + [(a - lat, b + lat, x) for k in o["bank"] for (a, b, x) in line.get(k, []) if x != e and b + lat > t])
                for (a, b, x) in busy:
                    if a >= t + c:
                        break
                    t = max(t, b)
                if best is None or t + c < best[0] + best[1]:
                    best = (t, c, e)
        if best:
            t, c, e = best
            for k in [e] + o["bank"]:
                line[k] = sorted(line.get(k, []) + [(t, t + c, e)])
            eng[i], beg[i], fin[i] = e, t, t + c + (0.0 if back else wait)
            if o["move"] and not back:
                t += c
                for (a, b, x) in line.get("D", []):
                    if a >= t + o["move"]:
                        break
                    t = max(t, b)
                line["D"] = sorted(line.get("D", []) + [(t, t + o["move"], e)])
                fin[i] = t + wait
        for s in succ[i]:
            t0[s] = max(t0[s], fin[i] + EST["lat"])
            left[s] -= 1
            if left[s] == 0:
                ready.append(s)
    return eng, fin, beg


def kind(name):
    head, cut, chunk = name.partition("_")
    return (head[:-1] if head[-1].isdigit() and head[0] != "k" else head) + cut + chunk


PLAN = {
    "start": "k0h S0p af0 abs0 abs1 b0p a0l sg1_0 ab1_1 g11_0 af1 xs1a a2p a3p g11_1 S2p b1p bh1 bh0 Ts2 S1p ab1_2 xc1a bh2 Sd1 Ts1 Sd4 a1p Ts0 ca1 b2p T1p "
             "sg1_2 g12_2 g11_2 xs2a sg2_2 Sd3 a0p gy1_2 T2p xc2a T0p x1_1 gw2_0 gc2_0 b0l Sd2 gw2_1 g12_1 g12_0 sg2_1 ca2 ab2_2 D2 gc2_2 x1_2 x1_0 sa2 "
             "gy1_1 xy1a sg1_1 age2 gc2_1 ab2_1",
    "step": "D+ sg+_2 g1+_0 xy-a g1+_2 sg+_1 xc+a x-_2 gw+_0 ca+ x-_1 ab+_2 bl- g1+_1 xs+a x-_0 sa+ gc+_2 age+ gw+_1 gc+_0 gc+_1 ab+_1 yl+",
    "end": "gc6_0 yo1 bl5 x5_0 xy5a g16_1 x5_1 gc6_1 g16_0 g16_2 yo3 qo fl x5_2 yo2 gc6_2 rs_3 yo0",
}


def plan():
    names = PLAN["start"].split()
    for t in range(3, RO):
        names += [x.replace("+", str(t)).replace("-", str(t - 1)) for x in PLAN["step"].split()]
    return names + PLAN["end"].split()


def schedule(ops):
    n = len(ops)
    pri = [0.0] * n
    for i in range(n - 1, -1, -1):
        o = ops[i]
        pri[i] += min([a[0] for a in o["alts"].values()] or [0.0]) + o["lat"]
        for d in o["hard"]:
            pri[d] = max(pri[d], pri[i] + EST["lat"])
    best = None
    if TUNE["plan"]:
        names = plan()
        far, pri = pri, [-names.index(o["name"]) if o["name"] in names else -len(names) for o in ops]
        for i in range(n - 1, -1, -1):
            for d in ops[i]["hard"]:
                pri[d] = max(pri[d], pri[i])
        pri = [p + 1e-3 * f for p, f in zip(pri, far)]
    for r in range(TUNE["rounds"]):
        pri = [p + TUNE["bias"].get(o["name"], TUNE["bias"].get(kind(o["name"]), 0.0)) for p, o in zip(pri, ops)]
        eng, fin, beg = place(ops, pri, False, [o.get("first") for o in ops])
        if best is None or max(fin) < max(best[2]):
            best = (sorted(range(n), key=lambda i: (beg[i], i)), eng, fin)
        pri = place(ops, fin, True, eng)[1]
    guard(ops, best[0], best[1])
    return best


def guard(ops, order, eng):
    seen = {}
    for i in order:
        ops[i]["soft"] = set(seen[k][e] for k in ops[i]["bank"] for e in seen.get(k, {}) if e != eng[i])
        for k in ops[i]["bank"]:
            seen.setdefault(k, {})[eng[i]] = i


def polish(cases, order, eng, tries):
    ops = cases[0][0]
    n = len(ops)
    hard = [sorted(o["hard"]) for o in ops]
    bank = [o["bank"] for o in ops]
    succ = [set() for _ in ops]
    for i in range(n):
        for d in hard[i]:
            succ[d].add(i)
    cost = [([{e: a[0] for e, a in o["alts"].items()} for o in c], [o["lat"] for o in c], [o["move"] for o in c], w) for (c, w) in cases]
    both = [i for i in range(n) if len(ops[i]["alts"]) > 1]

    def run(order, eng, lo, old):
        out = []
        for (c, lat, move, wake), (end, fin) in zip(cost, old):
            end, fin, free, seen, dma = list(end), list(fin), {}, {}, 0.0
            for i in order[:lo]:
                free[eng[i]] = end[i]
                if move[i]:
                    dma = fin[i] - lat[i]
                for b in bank[i]:
                    seen.setdefault(b, {})[eng[i]] = end[i]
            for i in order[lo:]:
                e, t = eng[i], -wake
                for d in hard[i]:
                    if fin[d] > t:
                        t = fin[d]
                for b in bank[i]:
                    for x, u in seen.get(b, {}).items():
                        if x != e and u > t:
                            t = u
                t += wake
                if e:
                    t = max(t, free.get(e, 0.0)) + c[i][e]
                    free[e] = t
                    for b in bank[i]:
                        seen.setdefault(b, {})[e] = t
                end[i] = t
                if move[i]:
                    t = dma = max(t, dma) + move[i]
                fin[i] = t + lat[i]
            out.append((end, fin))
        return out

    def tight(order, eng, now):
        out = []
        for (c, lat, move, wake), (end, fin) in zip(cost, now):
            before, last = {}, {}
            for i in order:
                before[i] = last.get(eng[i])
                last[eng[i]] = i
            i = max(range(n), key=lambda x: fin[x])
            while i is not None:
                out.append(i)
                j = before[i] if eng[i] else None
                if j is None or end[j] < end[i] - c[i][eng[i]] - 1e-9:
                    out += [j] if j is not None else []
                    j = max(hard[i], key=lambda x: fin[x]) if hard[i] else None
                i = j
        return out

    now = run(order, eng, 0, [([0.0] * n, [0.0] * n)] * len(cost))
    base = [max(f) for (x, f) in now]
    best, seed, hot = float(len(cost)), TUNE["seed"], tight(order, eng, now)
    for k in range(tries):
        seed = (seed * 1103515245 + 12345) % 2 ** 31
        r, o2, e2 = seed >> 8, order, eng
        if r % 12 == 0:
            i = both[r // 12 % len(both)]
            e2 = list(eng)
            e2[i] = "A" if eng[i] == "V" else "V"
            lo = order.index(i)
        else:
            p = q = r // 12 % n if r % 5 < TUNE["free"] else order.index(hot[r // 12 % len(hot)])
            i, hops, up = order[p], 1 + r % 3, r % 4 < 2
            while hops and eng[i] and (q > 0 and order[q - 1] not in ops[i]["hard"] if up else q < n - 1 and order[q + 1] not in succ[i]):
                q += -1 if up else 1
                hops -= eng[order[q]] == eng[i]
            if hops == 1 + r % 3:
                continue
            o2 = list(order)
            o2.insert(q, o2.pop(p))
            lo = min(p, q)
        new = run(o2, e2, lo, now)
        score = sum(max(f) / b for (x, f), b in zip(new, base))
        if score <= best + TUNE["slack"] * max(0.0, 1.0 - 1.25 * k / tries) * (seed >> 4 & 15) / 15:
            if score < best or k % 8 == 0:
                hot = tight(o2, e2, new)
            best, order, eng, now = score, o2, e2, new
    return order, eng


DONE = []


def arrange(g, core, T, topo, ops):
    if not DONE:
        order, eng, fin = schedule(ops)
        DONE.append(polish([(make_ops(g, core, T, topo, c)[0], c["lat"]) for c in CASES], order, eng, TUNE["tries"]))
    order, eng = DONE[0]
    guard(ops, order, eng)
    return order, eng


def rank_program(g, core, T, topo):
    if T.rank_of(core) is None:
        return
    ops, sent = make_ops(g, core, T, topo)
    order, eng = arrange(g, core, T, topo, ops)
    fin = {i: k for k, i in enumerate(order)}
    Q = {"V": g.vector, "A": g.scalar, "P": g.tensor, "G": g, "S": g.sync}
    known = {e: {} for e in Q}
    count = {e: 0 for e in Q}
    tok = {}
    clock = {}
    total = {}
    for i in order:
        o = ops[i]
        if o["kind"] == "arr":
            tok[i] = (o["sem"], o["inc"])
            clock[i] = {o["sem"]: o["inc"]}
            total[o["sem"]] = o["inc"]
            continue
        e = eng[i]
        kn = known[e]
        deps = [d for d in o["hard"] if ops[d]["kind"] != "rem"] + [d for d in o["soft"] if eng[d] != e]
        deps.sort(key=lambda d: -fin[d])
        for d in deps:
            s, v = tok[d]
            if kn.get(s, 0) >= v:
                continue
            Q[e].wait_ge(T.sem[s], v)
            for s2, v2 in clock[d].items():
                if kn.get(s2, 0) < v2:
                    kn[s2] = v2
        ins = o["alts"][e][1](Q[e])
        if o["kind"] == "rem":
            continue
        if o["kind"] == "dma":
            for x in ins:
                x.then_inc(T.sem[o["sem"]], 16)
            tok[i] = (o["sem"], o["inc"])
        else:
            count[e] += 1
            ins[-1].then_inc(T.sem["c" + e], 1)
            tok[i] = ("c" + e, count[e])
        total[tok[i][0]] = tok[i][1]
        clock[i] = dict(kn)
        clock[i][tok[i][0]] = tok[i][1]
    total["sent"] = sent
    for s, v in total.items():
        if known["G"].get(s, 0) < v:
            g.wait_ge(T.sem[s], v)
